import numpy as np, ml_dtypes
CORES = [24,25,26,27,28,29,30,31]
N = 8
import mx_ref
BF = ml_dtypes.bfloat16
def gcols(t, e):
    v = np.concatenate([t.reshape(8, 16, -1, 4), np.zeros((8, 16, 1, 4), BF)], axis=2)
    return np.ascontiguousarray(np.stack([v[g][:, e[g]] for g in range(8)])).reshape(128, -1)
def tile(rs):
    return np.stack(rs, axis=2).reshape(128, -1).astype(BF)
def cut(t, i, w=512):
    return t[:, w * i:w * i + w]
def pick(q, e):
    c = np.concatenate([q[0].reshape(128, -1, 4), np.zeros((128, 1, 4), np.uint8)], axis=1); s = np.concatenate([q[1], np.ones((16, 1), np.uint8)], axis=1)
    return (np.ascontiguousarray(c[:, e].reshape(128, -1)), np.ascontiguousarray(s[:, e]))
def join(*qs):
    return (np.concatenate([q[0] for q in qs], axis=1), np.concatenate([q[1] for q in qs], axis=1))
def put(q, e, v):
    c, s = q[0].reshape(128, -1, 4).copy(), q[1].copy(); c[:, e] = v[0].reshape(128, -1, 4); s[:, e] = v[1]
    return (c.reshape(128, -1), s)
def pk(c, s):
    return (np.ascontiguousarray(c), mx_ref.live(s))
def emit(q):
    return q[0], q[1]
def packed(v, rng):
    q = [mx_ref.quantize(np.ascontiguousarray(v[r])) for r in range(N)]
    return np.stack([a for a, b in q]), np.stack([mx_ref.plane(b, rng) for a, b in q])
def values_of_codes():
    e, c = np.zeros((128, 128, 4), np.float32), np.zeros((128, 2, 4), np.uint8)
    e[np.arange(128), np.arange(128), 0] = 1
    c[:127, :, 0] = np.arange(256).reshape(2, 128).T[:127]
    return mx_ref.matmul(mx_ref.quantize(e.reshape(128, 512).astype(BF)), (c.reshape(128, 8), np.full((16, 2), 127, np.uint8))).T.reshape(-1).astype(np.float64)
CODE_VALUE, SCALE_VALUE = values_of_codes(), 2.0 ** (np.arange(256) - 127.0)
def decode(q):
    return (CODE_VALUE[q[0]].reshape(16, 8, -1, 4) * SCALE_VALUE[q[1]][:, None, :, None] + 0.0).reshape(128, -1).astype(np.float32)
def f(rng, *shape):
    return mx_ref.flush((rng.standard_normal(shape, dtype=np.float32) * np.exp2(rng.integers(-2, 3, shape[:-1] + (1,)))).astype(BF))
def wide(rng, *shape, cols=0):
    v = rng.standard_normal(shape, dtype=np.float32) * np.exp2(rng.integers(-12, 13, shape)).astype(np.float32)
    if cols: v *= np.repeat(np.exp2(rng.integers(-cols, cols + 1, shape[:-2] + (1, shape[-1] // 4))) * (rng.random(shape[:-2] + (1, shape[-1] // 4)) > 0.0625), 4, axis=-1).astype(np.float32)
    return mx_ref.flush(v.astype(BF))
T, C, M = 320, 48, 2
def big(v):
    v = v.astype(np.float32)
    v[np.abs(v) < np.float32(2.0 ** -20)] = 0
    return v.astype(BF)
def numbers_of(rng):
    return {"x": big(f(rng, N, 128, 4 * T)), "u": np.array(f(rng, N, 128, 512)), "v": np.array(f(rng, N, 128, 512))}
def weights(rng, k):
    d = {}
    for n, s in (("a", k), ("c", 1.0)):
        a = mx_ref.flush((f(rng, N, 128, 256 * M).astype(np.float32) * np.float32(s)).astype(BF)).reshape(N, 8, 16, 4 * M, 16, 4)
        w = np.zeros((N, 8, 16, 4 * M, 8, 16, 4), BF)
        for g in range(8): w[:, g, :, :, g] = a[:, g]
        d[n + "c"], d[n + "p"] = packed(w.reshape(N, 128, 2048 * M), rng)
    return d
def signs(rng):
    return np.stack([rng.permutation(8) % 2 * 2.0 - 1.0 for r in range(N)])
def setup_inputs(rng):
    return {**numbers_of(rng), **weights(rng, 1.0)}
def setup_inputs_ties(rng):
    d = numbers_of(rng)
    u = d["u"].reshape(N, 128, 8, 16, 4)
    x = d["x"].reshape(N, 128, T, 4)
    for r in range(N):
        h = rng.integers(0, 8)
        for g in range(8):
            k = np.zeros(N, int) if g == h else rng.permutation(N) % 2
            a = u[r, :, g].copy()
            u[r, :, g, :N] = a[:, k]
        x[r][:, rng.permutation(T)[:T // 16]] = 0
    return {"x": x.reshape(N, 128, 4 * T), "u": u.reshape(N, 128, 512), "v": d["v"], **weights(rng, 1.0)}
def setup_inputs_near(rng):
    d = numbers_of(rng)
    x = d["x"].astype(np.float32).reshape(N, 128, T, 4)
    kind = rng.integers(0, 15, (N, T))
    x[:, 0, :, 0] = 1
    x[:, 8::8, :, 0] = kind[:, None, :] == np.arange(15)[None, :, None]
    u = d["u"].astype(np.float32).reshape(N, 128, 8, 16, 4)
    u[:, :, :, :N] = 0
    top = rng.integers(1, N, (N, 15, 8, 1))
    k = np.arange(N)
    s = np.where(k < top, 6, np.where(k == top, 7, 6 + rng.integers(0, 2, (N, 15, 8, N))))
    u[:, 0, :, :N, 0] = signs(rng)[:, :, None]
    u[:, 8::8, :, :N, 0] = s * 2.0 ** -23
    return {"x": x.reshape(N, 128, 4 * T).astype(BF), "u": u.reshape(N, 128, 512).astype(BF), "v": d["v"], **weights(rng, 1.0)}
def setup_inputs_huge(rng):
    d = numbers_of(rng)
    m = np.arange(128) // 16 % N
    kind = rng.integers(0, N, (N, T))
    below = rng.permutation(N) < N // 2
    c = np.stack([rng.permutation(T) % 2 * 2.0 - 1.0 for r in range(N)])
    c[below] = 1
    x = np.where(m[None, :, None] == kind[:, None, :], 0.875, 0.625) * c[:, None, :]
    x = 2.0 ** 30 * x[..., None] * (0.95 + 0.1 * rng.random((N, 128, T, 4)))
    p = np.stack([np.stack([rng.permutation(N) for g in range(8)]) for r in range(N)])
    a = p[:, None] == m[None, :, None, None]
    a = np.where(below[:, None, None, None], -(1 - 0.25 * a), signs(rng)[:, None, :, None] * (0.75 + 0.25 * a))
    u = d["u"].reshape(N, 128, 8, 16, 4)
    u[:, :, :, :N] = (2.0 ** 30 * a[..., None]).astype(np.float32).astype(BF)
    return {"x": x.astype(np.float32).reshape(N, 128, 4 * T).astype(BF), "u": u.reshape(N, 128, 512), "v": d["v"], **weights(rng, 2.0 ** -8)}
def setup_inputs_caps(rng):
    d = numbers_of(rng)
    o = rng.permutation(N)
    e = np.zeros((N, 8, T), int)
    for r in range(N):
        for g in range(8):
            w = rng.permutation(N)
            w = w[w != r]
            n = np.full(N, 8)
            n[w[:3]] = [C, C + 1, 0]
            n[r] = 0
            n[r] = T - np.sum(n)
            e[r, g] = rng.permutation(np.repeat(np.arange(N), n))
    e[o[0]] = o[1]
    e[o[1]] = o[1]
    x = d["x"].astype(np.float32).reshape(N, 8, 16, T, 4)
    top = e[:, :, None, :] == np.arange(N)[None, None, :, None]
    s = np.where(top, -1.0, -1.0 - 0.5 * rng.integers(1, 3, (N, 8, N, T)))
    x[:, :, :N, :, 0] = s + 3.0 * (signs(rng) > 0)[:, :, None, None]
    u = d["u"].reshape(N, 128, 8, 16, 4)
    u[:, :, :, :N] = 0
    for g in range(8):
        for k in range(N): u[:, 16 * g + k, g, k, 0] = 2.0 ** -30
    return {"x": x.reshape(N, 128, 4 * T).astype(BF), "u": u.reshape(N, 128, 512), "v": d["v"], **weights(rng, 1.0)}
def setup_inputs_spread(rng):
    d = setup_inputs(rng)
    d["x"] = big(wide(rng, N, 128, 4 * T, cols=6))
    return d
def check_inputs(d):
    b = []
    for k in ("x", "u", "v"):
        a = np.abs(d[k].astype(np.float32))
        if not (np.isfinite(a).all() and ((a == 0) | (a >= 2.0 ** -30) & (a <= 2.0 ** 30)).all()): b.append("a value of " + k)
    g = np.arange(128) // 16
    for k in ("ac", "cc"):
        a = ((d[k] & 127) != 0).reshape(-1, 128, 4 * M, 128, 4).any(axis=(0, 2, 4))
        if (a & (g[:, None] != g[None, :])).any(): b.append("a code of " + k + " outside the blocks")
        if ((d[k] & 127) == 127).any(): b.append("a code of " + k + " is no number")
    return b
def reference(x, u, v, ac, ap, cc, cp):
    took = np.full((N, N, 8, C), -1)
    slot = np.full((N, 8, T), -1)
    for r in range(N):
        s = mx_ref.matmul(mx_ref.quantize(u[r]), mx_ref.quantize(x[r])) + np.float32(0.0)
        e = np.argmax(s.reshape(8, 16, T)[:, :N], axis=1)
        for g in range(8):
            for d in range(N):
                j = np.flatnonzero(e[g] == d)[:C]
                took[r, d, g, :len(j)] = j
                slot[r, g, j] = C * d + np.arange(len(j))
    z = []
    for d in range(N):
        a, c = pk(ac[d], ap[d]), pk(cc[d], cp[d])
        q = join(*[mx_ref.quantize(gcols(x[r], took[r, d])) for r in range(N)])
        total = None
        for i in range(M):
            h = mx_ref.quantize(tile([np.maximum(mx_ref.matmul(pick(a, 512 * i + 128 * b + np.arange(128)), q), np.float32(0.0)) * np.float32(0.0625) for b in range(4)]))
            m = [mx_ref.matmul(pick(c, 512 * i + 128 * b + np.arange(128)), h) for b in range(4)]
            total = m if i == 0 else [total[b] + m[b] for b in range(4)]
        z.append(decode(mx_ref.quantize(tile([p * np.float32(0.0625) for p in total]))).astype(BF))
    y, ol = np.zeros((N, 128, T), np.float32), np.zeros((N, 8, T), np.float32)
    oc, osc = np.zeros((N, 128, 4 * T), np.uint8), np.zeros((N, 16, T), np.uint8)
    for r in range(N):
        came = np.concatenate([cut(z[d], r, 4 * C) for d in range(N)], axis=1)
        q = mx_ref.quantize((x[r].astype(np.float32) + gcols(came, slot[r]).astype(np.float32)).astype(BF))
        y[r] = mx_ref.matmul(mx_ref.quantize(v[r]), q)
        ol[r] = slot[r]
        oc[r], osc[r] = emit(q)
    return {"y": y, "ol": ol, "oc": oc, "osc": osc}

@@ -1,0 +1,362 @@
+from concourse.bass import DstId, RemoteDMATransfer
+from concourse.mybir import dt, AluOpType as A, ActivationFunctionType as F
+
+NT, C, N = 320, 48, 8
+NA, NB, NO = 4 * C, 3 * C, 128
+XOWN, XOUTB, XINB, XINA, XEND = 4 * C, 5 * C, 8 * C, 11 * C, 15 * C
+ZOWN = 7 * C
+ZERO, ZB, ZA, ZEND = ZOWN + C, ZOWN + NO, ZOWN + NO + NB, ZOWN + NO + NB + NA
+NE = NO + NA + NB
+X4, U8, BF, F32, I32, U16 = "float8_e4m3fn_x4", "uint8", "bfloat16", "float32", "int32", "uint16"
+
+
+def _sb(n, d):
+    return ("sbuf", [128, n], d)
+
+
+SCRATCH = {
+    "ps": ("psum", [128, 4096], F32),
+    "xb": _sb(4 * NT, BF), "ub": _sb(512, BF), "vb": _sb(512, BF),
+    "aq": _sb(1024, X4), "asc": _sb(1024, U8), "cq": _sb(1024, X4), "csc": _sb(1024, U8),
+    "uq": _sb(128, X4), "us": _sb(128, U8), "uq2": _sb(128, X4), "us2": _sb(128, U8),
+    "vq": _sb(128, X4), "vs": _sb(128, U8), "sq": _sb(NT, X4), "ss": _sb(NT, U8),
+    "pi": _sb(1, I32), "bits": _sb(8, I32), "bf": _sb(8, F32), "col": _sb(8, F32),
+    "c16": _sb(8, F32), "uoff": _sb(8, U16), "uniq": _sb(20, F32), "jv": _sb(NT, BF),
+    "cx0": _sb(384, BF), "cx": _sb(384, BF), "thr": _sb(160, BF), "cr": _sb(160, F32), "clip": _sb(NT, BF),
+    "offw": _sb(2, U16), "offe": _sb(2, U16), "offo": _sb(2, U16),
+    "ff": _sb(516, BF), "fe": _sb(516, BF), "fo": _sb(516, BF),
+    "eq": _sb(1024, X4), "es": _sb(1024, U8),
+    "pt": _sb(NT, F32), "rm": _sb(160, F32), "sm": _sb(160, F32), "gg": _sb(162, BF), "oht": _sb(NT, BF),
+    "oh": _sb(NT, BF), "val": _sb(NT, BF), "valt": _sb(NT, BF), "csel": _sb(160, BF), "sel": _sb(160, BF),
+    "th": _sb(160, BF), "ta": _sb(20, F32), "tb": _sb(20, F32), "tv": _sb(20, F32), "rr": _sb(64, F32),
+    "xx": _sb(64, F32), "wo": _sb(32, U16), "win": _sb(800, BF), "ex": _sb(384, BF), "offs": _sb(96, U16),
+    "ha": _sb(64, F32), "hb": _sb(64, F32), "hc": _sb(64, F32), "hd": _sb(64, F32), "hv": _sb(64, F32),
+    "le": _sb(32, U16), "lo": _sb(32, U16), "ob": _sb(32, F32), "ob2": _sb(32, F32), "ob3": _sb(32, F32),
+    "xt": _sb(4 * 8 * C, BF), "xq": _sb(XEND, X4), "xs": _sb(XEND, U8),
+    "ht": _sb(8 * NE, BF), "hq": _sb(2 * NE, X4), "hs": _sb(2 * NE, U8), "zb": _sb(4 * NE, BF),
+    "zq": _sb(ZEND, X4), "zs": _sb(ZEND, U8),
+    "zeq": _sb(NT, X4), "zes": _sb(NT, U8), "zoq": _sb(NT, X4), "zos": _sb(NT, U8),
+    "yb": _sb(4 * NT, BF), "yq": _sb(NT, X4), "ys": _sb(NT, U8), "yo": _sb(NT, F32),
+}
+SEMAPHORES = ["cv", "cs", "ct", "cg", "ldu", "ldxa", "ldxb", "lda", "ldc", "ldv", "fa", "fb", "ra", "rb",
+              "sent", "sty", "sts"]
+
+
+def _pieces(T, topo, r, sign):
+    cores = T.cores
+    mine = [k for k in range(N) if topo.die(cores[k]) == topo.die(cores[r])]
+    other = [k for k in range(N) if k not in mine]
+    i = mine.index(r)
+    near = lambda k: mine[(i + sign * k) % len(mine)]
+    far = lambda k: other[(i + sign * k) % len(other)]
+    return [far(0), far(1), near(2), near(3)], [near(1), far(2), far(3)]
+
+
+def rank_program(g, core, T, topo):
+    r = T.rank_of(core)
+    if r is None:
+        return
+    Q = {"v": g.vector, "s": g.scalar, "t": g.tensor, "g": g, "y": g.sync}
+    count = {}
+    seen = {q: {} for q in Q}
+
+    def wait(q, deps):
+        need = {}
+        for s, n in deps:
+            need[s] = max(need.get(s, 0), n)
+        for s, n in need.items():
+            if seen[q].get(s, 0) < n:
+                Q[q].wait_ge(T.sem[s], n)
+                seen[q][s] = n
+
+    def run(q, deps, fn):
+        wait(q, deps)
+        s = "c" + q
+        count[s] = count.get(s, 0) + 1
+        fn().then_inc(T.sem[s], 1)
+        return (s, count[s])
+
+    def dma(q, s, out, in_, deps=()):
+        wait(q, deps)
+        count[s] = count.get(s, 0) + 16
+        Q[q].dma_start(out, in_).then_inc(T.sem[s], 16)
+        return (s, count[s])
+
+    V, S, P = g.vector, g.scalar, g.tensor
+    u8 = lambda ap: ap.bitcast(dt.uint8)
+    u32 = lambda ap: ap.bitcast(dt.uint32)
+    bank = lambda b, n: T.ps[:, 512 * b:512 * b + n]
+
+    def ts(deps, out, in0, s1, op0, s2=None, op1=None):
+        if op1 is None:
+            return run("v", deps, lambda: V.tensor_scalar(out, in0, s1, None, op0))
+        return run("v", deps, lambda: V.tensor_scalar(out, in0, s1, s2, op0, op1))
+
+    def tt(deps, out, a, b, op):
+        return run("v", deps, lambda: V.tensor_tensor(out, a, b, op))
+
+    def cp(deps, out, a):
+        return run("v", deps, lambda: V.tensor_copy(out, a))
+
+    def tr(deps, out, a):
+        return run("v", deps, lambda: V.transpose(out, a))
+
+    def scan(deps, out, d0, d1, init, op0, op1):
+        return run("v", deps, lambda: V.tensor_tensor_scan(out, d0, d1, init, op0, op1))
+
+    def quant(deps, q, s, a):
+        return run("v", deps, lambda: V.quantize_mx(q, s, a))
+
+    def ms(ap, c):
+        return run("v", [], lambda: V.memset(ap, c))
+
+    def act(deps, out, a, func, **kw):
+        return run("s", deps, lambda: S.activation(out, a, func, **kw))
+
+    def mm(deps, out, wq, ws, xq, xs, start, stop):
+        return run("t", deps, lambda: P.matmul_mx(out, wq, ws, xq, xs, start, stop))
+
+    def iota(out, pattern, base, cm, flag=True):
+        if flag:
+            return run("g", [], lambda: g.iota(out, pattern, base, cm, allow_small_or_imprecise_dtypes=True))
+        return run("g", [], lambda: g.iota(out, pattern, base, cm))
+
+    H = NT // 2
+    ldu = dma("y", "ldu", T.ub[:], T.u[:])
+    ldxa = dma("s", "ldxa", T.xb[:, :4 * H], T.x[:, :4 * H])
+    ldxb = dma("y", "ldxb", T.xb[:, 4 * H:], T.x[:, 4 * H:])
+    dma("y", "lda", u8(T.aq[:]), T.ac[:], [ldu])
+    lda = dma("y", "lda", T.asc[:], T.ap[:])
+    dma("y", "ldc", u8(T.cq[:]), T.cc[:])
+    ldc = dma("y", "ldc", T.csc[:], T.cp[:])
+    ldv = dma("y", "ldv", T.vb[:], T.v[:])
+
+    i_p = iota(T.pi[:], [[0, 1]], 0, 1, False)
+    i_c16 = iota(T.c16[:], [[16, 8]], 0, 0)
+    i_thr = iota(T.thr[:], [[0, 20], [C, 8]], C - 193, 0)
+    i_jv = iota(T.jv[:], [[1, NT]], -64, 0)
+    i_uniq = iota(T.uniq[:], [[32, 10], [0, 2]], N * C, 1)
+    i_cx0 = iota(T.cx0[:], [[0, 96], [-512, 4]], 0, 0)
+    i_ff = iota(T.ff[:], [[-1, 516]], 3, 4)
+
+    AND, SHR = A.bitwise_and, A.logical_shift_right
+    m_g = ms(T.gg[:], 0.5)
+    m_oht = ms(T.oht[:], 0.0)
+    m_win = ms(T.win[:, 0:N * C], 255.0)
+    m_rr = ms(T.rr[:], 0.0)
+    m_zb = ms(T.zb[:, 4 * C:4 * NO], 0.0)
+    bits = [ts([i_p], T.bits[:, 0:1], T.pi[:], 15, AND, 1, SHR),
+            ts([i_p], T.bits[:, 1:2], T.pi[:], 12, AND, 2, SHR),
+            ts([i_p], T.bits[:, 2:3], T.pi[:], 3, AND),
+            ts([i_p], T.bits[:, 3:4], T.pi[:], 16, AND, 4, SHR),
+            ts([i_p], T.bits[:, 4:5], T.pi[:], 1, AND),
+            ts([i_p], T.bits[:, 5:6], T.pi[:], 14, AND)]
+    c_bf = cp(bits, T.bf[:, 0:6], T.bits[:, 0:6])
+    c_uoff = ts([c_bf, i_c16], T.uoff[:], T.c16[:], T.bf[:, 0:1], A.add)
+    c_x1 = ts([c_bf], T.col[:, 5:6], T.bf[:, 4:5], T.bf[:, 3:4], A.not_equal, 32.0, A.mult)
+    c_x2 = tt([c_x1], T.col[:, 6:7], T.col[:, 5:6], T.bf[:, 5:6], A.add)
+    c_offw = ts([c_x2], T.offw[:], T.c16[:, 0:2], T.col[:, 6:7], A.add, T.bf[:, 3:4], A.add)
+
+    c_cr = act([i_thr], T.cr[:], T.thr[:], F.Identity, scale=1e26, bias=1.21e28)
+    c_base = act([c_bf], T.col[:, 0:1], T.bf[:, 0:1], F.Identity, scale=float(C), bias=-193.0)
+    c_top = act([c_bf], T.col[:, 1:2], T.bf[:, 0:1], F.Identity, scale=float(C), bias=C + 1 - 193.0)
+    c_cxc = act([c_bf], T.col[:, 2:3], T.bf[:, 1:2], F.Identity, scale=512.0, bias=256.0)
+    c_tc = act([c_bf], T.col[:, 3:4], T.bf[:, 2:3], F.Identity, scale=1.0, bias=256.0)
+    c_m0 = act([c_bf], T.col[:, 4:5], T.bf[:, 3:4], F.Identity, scale=-1.0, bias=1.0)
+
+    q_u = quant([ldu], T.uq[:], T.us[:], T.ub[:])
+    p_uc = cp([q_u, c_uoff], u32(T.uq2[:]), u32(T.uq[:]).indirect(T.uoff[:]))
+    p_us = act([q_u, c_uoff], T.us2[:], T.us[:].indirect(T.uoff[:]), F.Copy)
+    c_clip = act([i_jv, c_top], T.clip[:], T.jv[:], F.Identity, scale=0.0, bias=T.col[:, 1:2])
+    c_cx = act([i_cx0, c_cxc], T.cx[:], T.cx0[:], F.Identity, scale=1.0, bias=T.col[:, 2:3])
+    q_xa = quant([ldxa], T.sq[:, :H], T.ss[:, :H], T.xb[:, :4 * H])
+    q_xb = quant([ldxb], T.sq[:, H:], T.ss[:, H:], T.xb[:, 4 * H:])
+    s_a = mm([p_uc, p_us, q_xa], bank(0, H), T.uq2[:], T.us2[:], T.sq[:, :H], T.ss[:, :H], True, True)
+    s_b = mm([q_xb], bank(1, H), T.uq2[:], T.us2[:], T.sq[:, H:], T.ss[:, H:], True, True)
+    t1a = tr([s_a], T.pt[:, :H], bank(0, H))
+    t1b = tr([s_b], T.pt[:, H:], bank(1, H))
+
+    e_r = scan([t1a, t1b, c_cr], T.rm[:], T.cr[:], T.pt[:, 0:NT:2], 0.0, A.min, A.max)
+    e_s = scan([], T.sm[:, 159::-1], T.cr[:], T.pt[:, NT - 2::-2], 0.0, A.min, A.max)
+    e_g = [tt([e_r, e_s, m_g], T.gg[:, 1 + o:161:st], T.rm[:, o::st], T.sm[:, o::st], A.is_ge)
+           for o, st in ((0, 2), (1, 4), (3, 8))]
+    e_oh = tt(e_g + [m_oht], T.oht[:, 0:NT:2], T.gg[:, 1:161], T.gg[:, 0:160], A.is_gt)
+    e_c = act(e_g, T.csel[:], T.gg[:, 160:0:-1], F.Identity, scale=-1024.0, bias=256.0)
+    e_t2 = tr([e_oh], T.oh[:], T.oht[:])
+    e_cnt = scan([e_t2, c_clip, c_base], T.val[:], T.oh[:], T.clip[:], T.col[:, 0:1], A.add, A.min)
+    e_th = scan([e_c, i_thr], T.th[:, 159::-1], T.csel[:], T.thr[:, 159::-1], 0.0, A.min, A.max)
+    e_t3 = tr([e_cnt], T.valt[:], T.val[:])
+    e_sel = scan([e_t3], T.sel[:, 159::-1], T.csel[:], T.valt[:, NT - 2::-2], 0.0, A.min, A.max)
+    e_a = tt([e_sel, e_th], T.ta[:], T.sel[:, 0::8], T.th[:, 0::8], A.is_gt)
+    e_v = act([e_sel], T.tv[:], T.sel[:, 0::8], F.Identity, scale=1.0, bias=192.0)
+    e_b = tt([e_a, i_uniq], T.tb[:], T.ta[:], T.uniq[:], A.mult)
+    e_w = tt([e_b, e_v, m_rr], T.rr[:, 0:20], T.tv[:], T.tb[:], A.max)
+    e_t4 = [tr([e_w], T.xx[:, 0:32], T.rr[:, 0:32]), tr([e_w], T.xx[:, 32:64], T.rr[:, 0:32])]
+    e_t5 = tr(e_t4, T.rr[:, 32:64], T.xx[:, 16:48])
+    e_wo = cp([e_t5, c_offw], T.wo[:], T.rr[:].indirect(T.offw[:]))
+    e_sc = cp([e_wo, i_jv, m_win], T.win[:].indirect(T.wo[:, 0:20]), T.jv[:])
+    e_ex = scan([e_sc, c_cx], T.ex[:], T.cx[:], T.win[:, 0:N * C], 0.0, A.max, A.min)
+    e_of = ts([e_ex, c_tc], T.offs[:], T.ex[:, 3::4], 4.0, A.mult, T.col[:, 3:4], A.add)
+
+    out_a, out_b = _pieces(T, topo, r, 1)
+    in_a, in_b = _pieces(T, topo, r, -1)
+    order = out_a + [r] + out_b
+
+    def gather(q, lo, hi):
+        runs = []
+        for k in range(lo, hi):
+            o = 12 * order[k // 2] + 6 * (k % 2)
+            if runs and runs[-1][1] + runs[-1][2] == o:
+                runs[-1][2] += 6
+            else:
+                runs.append([k, o, 6])
+        evs = []
+        for k, o, n in runs:
+            out = T.xt[:, 96 * k:96 * k + 16 * n]
+            src = T.xb[:].indirect(T.offs[:, o:o + n])
+            evs.append(cp([e_of, ldxa, ldxb], out, src) if q == "v" else act([e_of, ldxa, ldxb], out, src, F.Copy))
+        return evs
+
+    ga = gather("v", 0, 4) + gather("s", 4, 8)
+    q_a = quant(ga, T.xq[:, 0:NA], T.xs[:, 0:NA], T.xt[:, 0:4 * NA])
+    gb = gather("v", 8, 11) + gather("s", 11, 16)
+    q_b = quant(gb, T.xq[:, NA:2 * NA], T.xs[:, NA:2 * NA], T.xt[:, 4 * NA:8 * NA])
+
+    def send(deps, sem, q, s, moves, apart=False):
+        wait("g", deps)
+        eng = topo.engines(core, T.cores[moves[0][0]])
+        far = [m for m in moves if topo.die(T.cores[m[0]]) != topo.die(core)]
+        near = [m for m in moves if m not in far]
+        total = 0
+        for buf, flip in ((q, 0), (s, 1)):
+            if apart:
+                es = eng[flip::2]
+                lanes = ((far, es[flip::2]), (near, es[1 - flip::2]))
+            else:
+                lanes = ((far, eng[1 - flip::2]), (near, eng[flip::2]))
+            trs = []
+            for part, es in lanes:
+                w = len(es) // len(part)
+                for k, (d, here, there) in enumerate(part):
+                    mask = sum(1 << e for e in es[w * k:w * k + w])
+                    rid, pid, _ = topo.addr(T.cores[d])
+                    src, dst = buf[:, here:here + C], buf[:, there:there + C]
+                    if not flip:
+                        src, dst = u8(src), u8(dst)
+                    trs.append(RemoteDMATransfer(dst_ids=[DstId(rid=rid, pnc=pid)], dma_engine_mask=mask,
+                                                 remote_sem=T.sem[sem], src=src, dst=dst))
+                    total += w
+            g.remote_dma_fused(trs, local_sem=T.sem["sent"])
+        count["sent"] = count.get("sent", 0) + total
+        return (sem, total)
+
+    got_a = send([q_a], "fa", T.xq, T.xs, [(d, C * k, XINA + C * k) for k, d in enumerate(out_a)], True)
+    got_b = send([q_b], "fb", T.xq, T.xs, [(d, XOUTB + C * k, XINB + C * k) for k, d in enumerate(out_b)])
+
+    free = {b: [] for b in range(8)}
+    free[0], free[1] = [t1a], [t1b]
+
+    def expert(at, col0, n, m, zcol, arrived, lo, hi):
+        xq, xs = T.xq[:, col0:col0 + n], T.xs[:, col0:col0 + n]
+        prod = {}
+        for i, base in ((0, lo), (1, hi)):
+            for b in range(4):
+                w = slice(512 * i + 128 * b, 512 * i + 128 * b + 128)
+                prod[i, b] = mm(arrived + [lda] + free[base + b], bank(base + b, n), T.aq[:, w], T.asc[:, w], xq, xs, True, True)
+        qh = []
+        for i, base, on in ((0, lo, "vsvs"), (1, hi, "svsv")):
+            c0 = 2 * at + n * i
+            evs = []
+            for b in range(4):
+                out = T.ht[:, 4 * c0 + b:4 * (c0 + n):4]
+                if on[b] == "v":
+                    e = ts([prod[i, b]], out, bank(base + b, n), 0.0, A.max, 0.0625, A.mult)
+                else:
+                    e = act([prod[i, b]], out, bank(base + b, n), F.Relu, scale=0.0625)
+                free[base + b] = [e]
+                evs.append(e)
+            qh.append(quant(evs, T.hq[:, c0:c0 + n], T.hs[:, c0:c0 + n], T.ht[:, 4 * c0:4 * (c0 + n)]))
+        for i in range(2):
+            c0 = 2 * at + n * i
+            for b in range(4):
+                w = slice(512 * i + 128 * b, 512 * i + 128 * b + 128)
+                prod[2, b] = mm([qh[i], ldc] + free[lo + b], bank(lo + b, n), T.cq[:, w], T.csc[:, w],
+                                T.hq[:, c0:c0 + n], T.hs[:, c0:c0 + n], i == 0, i == 1)
+        evs = [m_zb]
+        for b in range(4):
+            out = T.zb[:, 4 * at + b:4 * (at + m):4]
+            if b % 2 == 1:
+                e = ts([prod[2, b]], out, bank(lo + b, m), 0.0625, A.mult)
+            else:
+                e = act([prod[2, b]], out, bank(lo + b, m), F.Copy, scale=0.0625)
+            free[lo + b] = [e]
+            evs.append(e)
+        return quant(evs, T.zq[:, zcol:zcol + n], T.zs[:, zcol:zcol + n], T.zb[:, 4 * at:4 * (at + n)])
+
+    z_o = expert(0, XOWN, NO, C, ZOWN, [q_b], 0, 4)
+
+    first = float(C * (r + 1))
+    m_ob = ms(T.ob[:], 0.0)
+    h_b = ts([e_t5], T.hb[:], T.rr[:], float(N * C), A.is_ge, 1000.0, A.mult)
+    h_a = ts([e_t5], T.ha[:], T.rr[:], first, A.is_lt, float(N * C), A.mult)
+    o_a = [tt([h_b, m_ob], T.ob[:, 16 * p:16 * p + 10], T.rr[:, p:20:2], T.hb[:, p:20:2], A.subtract) for p in range(2)]
+    h_c = tt([h_a, h_b], T.hc[:], T.ha[:], T.hb[:], A.add)
+    o_b = tr(o_a, T.ob2[:], T.ob[:])
+    h_d = tt([h_c], T.hd[:], T.hc[:], T.rr[:], A.add)
+    o_c = ts([o_b], T.ob3[:], T.ob2[:], -1.0, A.max)
+    h_v = ts([h_d], T.hv[:], T.hd[:], -first, A.add, float(ZERO), A.min)
+    for k in range(8):
+        dma("y", "sts", T.ol[k], T.ob3[16 * k:16 * k + 10, :], [o_c])
+
+    home = lambda s: C * ((r - s - 1) % N)
+    z_a = expert(NO, XINA, NA, NA, ZA, [got_a], 4, 0)
+    back_a = send([z_a], "ra", T.zq, T.zs, [(s, ZA + C * k, home(s)) for k, s in enumerate(in_a)])
+    z_b = expert(NO + NA, XINB, NB, NB, ZB, [got_b], 0, 4)
+    back_b = send([z_b], "rb", T.zq, T.zs, [(s, ZB + C * k, home(s)) for k, s in enumerate(in_b)])
+
+    c_offe = ts([c_x2], T.offe[:], T.c16[:, 0:2], T.col[:, 6:7], A.add)
+    c_offo = ts([c_x2], T.offo[:], T.c16[:, 0:2], T.col[:, 6:7], A.add, 1.0, A.add)
+    c_fe = ts([i_ff, c_m0], T.fe[:], T.ff[:], 0.0, A.is_equal, T.col[:, 4:5], A.mult)
+    c_fo = ts([i_ff, c_bf], T.fo[:], T.ff[:], 0.0, A.is_equal, T.bf[:, 3:4], A.mult)
+    l_e = cp([h_v, c_offe], T.le[:], T.hv[:].indirect(T.offe[:]))
+    l_o = cp([h_v, c_offo], T.lo[:], T.hv[:].indirect(T.offo[:]))
+    q_e = []
+    for b in range(4):
+        for p, (src, dep) in enumerate(((T.fe, c_fe), (T.fo, c_fo))):
+            w = slice(256 * b + 128 * p, 256 * b + 128 * p + 128)
+            q_e.append(quant([dep], T.eq[:, w], T.es[:, w], src[:, 3 - b:515 - b]))
+    q_v = quant([ldv], T.vq[:], T.vs[:], T.vb[:])
+
+    here = [back_a, back_b, z_o, l_e, l_o]
+    W = ZB
+    runs = ((0, 192), (192, NT))
+    picks = []
+    for lo, hi in runs:
+        cs, os_ = slice(lo, hi), slice(lo // 16, hi // 16)
+        picks.append([(cp(here, u32(q[:, cs]), u32(T.zq[:, 0:W]).indirect(lst[:, os_])),
+                       act(here, s[:, cs], T.zs[:, 0:W].indirect(lst[:, os_]), F.Copy))
+                      for q, s, lst in ((T.zeq, T.zes, T.le), (T.zoq, T.zos, T.lo))])
+    dec = {}
+    for h, (lo, hi) in enumerate(runs):
+        for b in range(4):
+            for p, (q, s) in enumerate(((T.zeq, T.zes), (T.zoq, T.zos))):
+                w = slice(256 * b + 128 * p, 256 * b + 128 * p + 128)
+                dec[h, b] = mm(list(picks[h][p]) + q_e + free[4 * h + b], bank(4 * h + b, hi - lo), T.eq[:, w], T.es[:, w],
+                               q[:, lo:hi], s[:, lo:hi], p == 0, p == 1)
+    q_y = []
+    for h, (lo, hi) in enumerate(runs):
+        evs = [tt([dec[h, b]], T.yb[:, 4 * lo + b:4 * hi:4], bank(4 * h + b, hi - lo),
+                  T.xb[:, 4 * lo + b:4 * hi:4], A.add) for b in range(4)]
+        q_y.append(quant(evs, T.yq[:, lo:hi], T.ys[:, lo:hi], T.yb[:, 4 * lo:4 * hi]))
+    for h, (lo, hi) in enumerate(runs):
+        m = mm([q_y[h], q_v], bank(h, hi - lo), T.vq[:], T.vs[:], T.yq[:, lo:hi], T.ys[:, lo:hi], True, True)
+        if h == 0:
+            c = act([m], T.yo[:, lo:hi], bank(h, hi - lo), F.Copy)
+        else:
+            c = cp([m], T.yo[:, lo:hi], bank(h, hi - lo))
+        dma("y", "sts", T.oc[:, 4 * lo:4 * hi], u8(T.yq[:, lo:hi]), [q_y[h]])
+        dma("s", "sty", T.y[:, lo:hi], T.yo[:, lo:hi], [c])
+    for k in range(4):
+        dma("y", "sts", T.osc[4 * k:4 * k + 4, :], T.ys[32 * k:32 * k + 4, :], q_y)
+
+    wait("g", list(count.items()))

@@ -4,9 +4,10 @@ from concourse.mybir import dt, AluOpType as A, ActivationFunctionType as F
 NT, C, N = 320, 48, 8
 NA, NB, NO = 4 * C, 3 * C, 128
 XOWN, XOUTB, XINB, XINA, XEND = 4 * C, 5 * C, 8 * C, 11 * C, 15 * C
-ZOWN = 7 * C
-ZERO, ZB, ZA, ZEND = ZOWN + C, ZOWN + NO, ZOWN + NO + NB, ZOWN + NO + NB + NA
+ZINA, ZOWN = 3 * C, 7 * C
+ZB, ZA, ZEND = ZOWN + NO, ZOWN + NO + NB, ZOWN + NO + NB + NA
 NE = NO + NA + NB
+DW = 400
 X4, U8, BF, F32, I32, U16 = "float8_e4m3fn_x4", "uint8", "bfloat16", "float32", "int32", "uint16"
 
 
@@ -23,19 +24,16 @@ SCRATCH = {
     "pi": _sb(1, I32), "bits": _sb(8, I32), "bf": _sb(8, F32), "col": _sb(8, F32),
     "c16": _sb(8, F32), "uoff": _sb(8, U16), "uniq": _sb(20, F32), "jv": _sb(NT, BF),
     "cx0": _sb(384, BF), "cx": _sb(384, BF), "thr": _sb(160, BF), "cr": _sb(160, F32), "clip": _sb(NT, BF),
-    "offw": _sb(2, U16), "offe": _sb(2, U16), "offo": _sb(2, U16),
-    "ff": _sb(516, BF), "fe": _sb(516, BF), "fo": _sb(516, BF),
-    "eq": _sb(1024, X4), "es": _sb(1024, U8),
+    "offw": _sb(2, U16), "ff": _sb(516, BF), "fa": _sb(516, BF), "fe": _sb(516, BF),
+    "eq": _sb(512, X4), "es": _sb(512, U8),
     "pt": _sb(NT, F32), "rm": _sb(160, F32), "sm": _sb(160, F32), "gg": _sb(162, BF), "oht": _sb(NT, BF),
     "oh": _sb(NT, BF), "val": _sb(NT, BF), "valt": _sb(NT, BF), "csel": _sb(160, BF), "sel": _sb(160, BF),
     "th": _sb(160, BF), "ta": _sb(20, F32), "tb": _sb(20, F32), "tv": _sb(20, F32), "rr": _sb(64, F32),
     "xx": _sb(64, F32), "wo": _sb(32, U16), "win": _sb(800, BF), "ex": _sb(384, BF), "offs": _sb(96, U16),
-    "ha": _sb(64, F32), "hb": _sb(64, F32), "hc": _sb(64, F32), "hd": _sb(64, F32), "hv": _sb(64, F32),
-    "le": _sb(32, U16), "lo": _sb(32, U16), "ob": _sb(32, F32), "ob2": _sb(32, F32), "ob3": _sb(32, F32),
+    "hb": _sb(20, F32), "lh": _sb(32, U16), "ob": _sb(32, F32), "ob2": _sb(32, F32), "ob3": _sb(32, F32),
     "xt": _sb(4 * 8 * C, BF), "xq": _sb(XEND, X4), "xs": _sb(XEND, U8),
     "ht": _sb(8 * NE, BF), "hq": _sb(2 * NE, X4), "hs": _sb(2 * NE, U8), "zb": _sb(4 * NE, BF),
-    "zq": _sb(ZEND, X4), "zs": _sb(ZEND, U8),
-    "zeq": _sb(NT, X4), "zes": _sb(NT, U8), "zoq": _sb(NT, X4), "zos": _sb(NT, U8),
+    "zq": _sb(ZEND, X4), "zs": _sb(ZEND, U8), "dd": _sb(4 * DW, BF),
     "yb": _sb(4 * NT, BF), "yq": _sb(NT, X4), "ys": _sb(NT, U8), "yo": _sb(NT, F32),
 }
 SEMAPHORES = ["cv", "cs", "ct", "cg", "ldu", "ldxa", "ldxb", "lda", "ldc", "ldv", "fa", "fb", "ra", "rb",
@@ -85,7 +83,7 @@ def rank_program(g, core, T, topo):
     V, S, P = g.vector, g.scalar, g.tensor
     u8 = lambda ap: ap.bitcast(dt.uint8)
     u32 = lambda ap: ap.bitcast(dt.uint32)
-    bank = lambda b, n: T.ps[:, 512 * b:512 * b + n]
+    bank = lambda b, n, o=0: T.ps[:, 512 * b + o:512 * b + o + n]
 
     def ts(deps, out, in0, s1, op0, s2=None, op1=None):
         if op1 is None:
@@ -138,13 +136,17 @@ def rank_program(g, core, T, topo):
     i_uniq = iota(T.uniq[:], [[32, 10], [0, 2]], N * C, 1)
     i_cx0 = iota(T.cx0[:], [[0, 96], [-512, 4]], 0, 0)
     i_ff = iota(T.ff[:], [[-1, 516]], 3, 4)
+    PAD = 4 * (NO - C)
+    pads = [iota(T.ht[:, 4 * C:4 * NO], [[0, PAD]], 0, 0), iota(T.ht[:, 4 * (NO + C):8 * NO], [[0, PAD]], 0, 0),
+            iota(T.zb[:, 4 * C:4 * NO], [[0, PAD]], 0, 0)]
+    m_dd = iota(T.dd[:, N * C::DW], [[0, 4]], 0, 0)
+    m_ob = iota(T.ob[:], [[0, 32]], 0, 0)
 
     AND, SHR = A.bitwise_and, A.logical_shift_right
     m_g = ms(T.gg[:], 0.5)
     m_oht = ms(T.oht[:], 0.0)
     m_win = ms(T.win[:, 0:N * C], 255.0)
     m_rr = ms(T.rr[:], 0.0)
-    m_zb = ms(T.zb[:, 4 * C:4 * NO], 0.0)
     bits = [ts([i_p], T.bits[:, 0:1], T.pi[:], 15, AND, 1, SHR),
             ts([i_p], T.bits[:, 1:2], T.pi[:], 12, AND, 2, SHR),
             ts([i_p], T.bits[:, 2:3], T.pi[:], 3, AND),
@@ -162,7 +164,6 @@ def rank_program(g, core, T, topo):
     c_top = act([c_bf], T.col[:, 1:2], T.bf[:, 0:1], F.Identity, scale=float(C), bias=C + 1 - 193.0)
     c_cxc = act([c_bf], T.col[:, 2:3], T.bf[:, 1:2], F.Identity, scale=512.0, bias=256.0)
     c_tc = act([c_bf], T.col[:, 3:4], T.bf[:, 2:3], F.Identity, scale=1.0, bias=256.0)
-    c_m0 = act([c_bf], T.col[:, 4:5], T.bf[:, 3:4], F.Identity, scale=-1.0, bias=1.0)
 
     q_u = quant([ldu], T.uq[:], T.us[:], T.ub[:])
     p_uc = cp([q_u, c_uoff], u32(T.uq2[:]), u32(T.uq[:]).indirect(T.uoff[:]))
@@ -182,6 +183,7 @@ def rank_program(g, core, T, topo):
            for o, st in ((0, 2), (1, 4), (3, 8))]
     e_oh = tt(e_g + [m_oht], T.oht[:, 0:NT:2], T.gg[:, 1:161], T.gg[:, 0:160], A.is_gt)
     e_c = act(e_g, T.csel[:], T.gg[:, 160:0:-1], F.Identity, scale=-1024.0, bias=256.0)
+    c_fa = act([i_ff], T.fa[:], T.ff[:], F.Abs)
     e_t2 = tr([e_oh], T.oh[:], T.oht[:])
     e_cnt = scan([e_t2, c_clip, c_base], T.val[:], T.oh[:], T.clip[:], T.col[:, 0:1], A.add, A.min)
     e_th = scan([e_c, i_thr], T.th[:, 159::-1], T.csel[:], T.thr[:, 159::-1], 0.0, A.min, A.max)
@@ -189,8 +191,10 @@ def rank_program(g, core, T, topo):
     e_sel = scan([e_t3], T.sel[:, 159::-1], T.csel[:], T.valt[:, NT - 2::-2], 0.0, A.min, A.max)
     e_a = tt([e_sel, e_th], T.ta[:], T.sel[:, 0::8], T.th[:, 0::8], A.is_gt)
     e_v = act([e_sel], T.tv[:], T.sel[:, 0::8], F.Identity, scale=1.0, bias=192.0)
+    c_fe = act([c_fa], T.fe[:], T.fa[:], F.Relu, scale=-1.0, bias=1.0)
     e_b = tt([e_a, i_uniq], T.tb[:], T.ta[:], T.uniq[:], A.mult)
     e_w = tt([e_b, e_v, m_rr], T.rr[:, 0:20], T.tv[:], T.tb[:], A.max)
+    h_b = act([e_w], T.hb[:], T.rr[:, 0:20], F.Relu, scale=1000.0, bias=500.0 - 1000.0 * N * C)
     e_t4 = [tr([e_w], T.xx[:, 0:32], T.rr[:, 0:32]), tr([e_w], T.xx[:, 32:64], T.rr[:, 0:32])]
     e_t5 = tr(e_t4, T.rr[:, 32:64], T.xx[:, 16:48])
     e_wo = cp([e_t5, c_offw], T.wo[:], T.rr[:].indirect(T.offw[:]))
@@ -255,8 +259,14 @@ def rank_program(g, core, T, topo):
 
     free = {b: [] for b in range(8)}
     free[0], free[1] = [t1a], [t1b]
+    q_e = []
 
-    def expert(at, col0, n, m, zcol, arrived, lo, hi):
+    def unpackers(bs):
+        for b in bs:
+            w = slice(128 * b, 128 * b + 128)
+            q_e.append(quant([c_fe], T.eq[:, w], T.es[:, w], T.fe[:, 3 - b:515 - b]))
+
+    def expert(at, col0, n, m, zcol, arrived, lo, hi, bs):
         xq, xs = T.xq[:, col0:col0 + n], T.xs[:, col0:col0 + n]
         prod = {}
         for i, base in ((0, lo), (1, hi)):
@@ -266,23 +276,24 @@ def rank_program(g, core, T, topo):
         qh = []
         for i, base, on in ((0, lo, "vsvs"), (1, hi, "svsv")):
             c0 = 2 * at + n * i
-            evs = []
+            evs = list(pads)
             for b in range(4):
-                out = T.ht[:, 4 * c0 + b:4 * (c0 + n):4]
+                out = T.ht[:, 4 * c0 + b:4 * (c0 + m):4]
                 if on[b] == "v":
-                    e = ts([prod[i, b]], out, bank(base + b, n), 0.0, A.max, 0.0625, A.mult)
+                    e = ts([prod[i, b]], out, bank(base + b, m), 0.0, A.max, 0.0625, A.mult)
                 else:
-                    e = act([prod[i, b]], out, bank(base + b, n), F.Relu, scale=0.0625)
+                    e = act([prod[i, b]], out, bank(base + b, m), F.Relu, scale=0.0625)
                 free[base + b] = [e]
                 evs.append(e)
             qh.append(quant(evs, T.hq[:, c0:c0 + n], T.hs[:, c0:c0 + n], T.ht[:, 4 * c0:4 * (c0 + n)]))
+        unpackers(bs)
         for i in range(2):
             c0 = 2 * at + n * i
             for b in range(4):
                 w = slice(512 * i + 128 * b, 512 * i + 128 * b + 128)
                 prod[2, b] = mm([qh[i], ldc] + free[lo + b], bank(lo + b, n), T.cq[:, w], T.csc[:, w],
                                 T.hq[:, c0:c0 + n], T.hs[:, c0:c0 + n], i == 0, i == 1)
-        evs = [m_zb]
+        evs = []
         for b in range(4):
             out = T.zb[:, 4 * at + b:4 * (at + m):4]
             if b % 2 == 1:
@@ -293,67 +304,58 @@ def rank_program(g, core, T, topo):
             evs.append(e)
         return quant(evs, T.zq[:, zcol:zcol + n], T.zs[:, zcol:zcol + n], T.zb[:, 4 * at:4 * (at + n)])
 
-    z_o = expert(0, XOWN, NO, C, ZOWN, [q_b], 0, 4)
+    def home(s, piece, base):
+        return base + C * sorted(_pieces(T, topo, s, 1)[piece]).index(r)
 
-    first = float(C * (r + 1))
-    m_ob = ms(T.ob[:], 0.0)
-    h_b = ts([e_t5], T.hb[:], T.rr[:], float(N * C), A.is_ge, 1000.0, A.mult)
-    h_a = ts([e_t5], T.ha[:], T.rr[:], first, A.is_lt, float(N * C), A.mult)
+    z_o = expert(0, XOWN, NO, C, ZOWN, [q_b], 0, 4, (0, 1))
+    z_a = expert(NO, XINA, NA, NA, ZA, [got_a], 4, 0, (2,))
+    back_a = send([z_a], "ra", T.zq, T.zs, [(s, ZA + C * k, home(s, 0, ZINA)) for k, s in enumerate(in_a)])
+    z_b = expert(NO + NA, XINB, NB, NB, ZB, [got_b], 0, 4, (3,))
+    back_b = send([z_b], "rb", T.zq, T.zs, [(s, ZB + C * k, home(s, 1, 0)) for k, s in enumerate(in_b)])
+
+    l_h = ts([e_t5], T.lh[:], T.rr[:].indirect(T.offw[:]), float(N * C), A.min)
     o_a = [tt([h_b, m_ob], T.ob[:, 16 * p:16 * p + 10], T.rr[:, p:20:2], T.hb[:, p:20:2], A.subtract) for p in range(2)]
-    h_c = tt([h_a, h_b], T.hc[:], T.ha[:], T.hb[:], A.add)
+    q_v = quant([ldv], T.vq[:], T.vs[:], T.vb[:])
     o_b = tr(o_a, T.ob2[:], T.ob[:])
-    h_d = tt([h_c], T.hd[:], T.hc[:], T.rr[:], A.add)
     o_c = ts([o_b], T.ob3[:], T.ob2[:], -1.0, A.max)
-    h_v = ts([h_d], T.hv[:], T.hd[:], -first, A.add, float(ZERO), A.min)
     for k in range(8):
         dma("y", "sts", T.ol[k], T.ob3[16 * k:16 * k + 10, :], [o_c])
 
-    home = lambda s: C * ((r - s - 1) % N)
-    z_a = expert(NO, XINA, NA, NA, ZA, [got_a], 4, 0)
-    back_a = send([z_a], "ra", T.zq, T.zs, [(s, ZA + C * k, home(s)) for k, s in enumerate(in_a)])
-    z_b = expert(NO + NA, XINB, NB, NB, ZB, [got_b], 0, 4)
-    back_b = send([z_b], "rb", T.zq, T.zs, [(s, ZB + C * k, home(s)) for k, s in enumerate(in_b)])
-
-    c_offe = ts([c_x2], T.offe[:], T.c16[:, 0:2], T.col[:, 6:7], A.add)
-    c_offo = ts([c_x2], T.offo[:], T.c16[:, 0:2], T.col[:, 6:7], A.add, 1.0, A.add)
-    c_fe = ts([i_ff, c_m0], T.fe[:], T.ff[:], 0.0, A.is_equal, T.col[:, 4:5], A.mult)
-    c_fo = ts([i_ff, c_bf], T.fo[:], T.ff[:], 0.0, A.is_equal, T.bf[:, 3:4], A.mult)
-    l_e = cp([h_v, c_offe], T.le[:], T.hv[:].indirect(T.offe[:]))
-    l_o = cp([h_v, c_offo], T.lo[:], T.hv[:].indirect(T.offo[:]))
-    q_e = []
-    for b in range(4):
-        for p, (src, dep) in enumerate(((T.fe, c_fe), (T.fo, c_fo))):
-            w = slice(256 * b + 128 * p, 256 * b + 128 * p + 128)
-            q_e.append(quant([dep], T.eq[:, w], T.es[:, w], src[:, 3 - b:515 - b]))
-    q_v = quant([ldv], T.vq[:], T.vs[:], T.vb[:])
-
-    here = [back_a, back_b, z_o, l_e, l_o]
-    W = ZB
-    runs = ((0, 192), (192, NT))
-    picks = []
-    for lo, hi in runs:
-        cs, os_ = slice(lo, hi), slice(lo // 16, hi // 16)
-        picks.append([(cp(here, u32(q[:, cs]), u32(T.zq[:, 0:W]).indirect(lst[:, os_])),
-                       act(here, s[:, cs], T.zs[:, 0:W].indirect(lst[:, os_]), F.Copy))
-                      for q, s, lst in ((T.zeq, T.zes, T.le), (T.zoq, T.zos, T.lo))])
-    dec = {}
-    for h, (lo, hi) in enumerate(runs):
+    def unpack(ranks, col0, deps, base, on):
+        n = C * len(ranks)
+        runs = []
+        for k, d in enumerate(ranks):
+            if runs and runs[-1][1] + runs[-1][2] == d:
+                runs[-1][2] += 1
+            else:
+                runs.append([k, d, 1])
+        ms_ = [mm(deps + q_e + free[base + b], bank(base + b, n), T.eq[:, 128 * b:128 * b + 128], T.es[:, 128 * b:128 * b + 128],
+                  T.zq[:, col0:col0 + n], T.zs[:, col0:col0 + n], True, True) for b in range(4)]
+        done = []
         for b in range(4):
-            for p, (q, s) in enumerate(((T.zeq, T.zes), (T.zoq, T.zos))):
-                w = slice(256 * b + 128 * p, 256 * b + 128 * p + 128)
-                dec[h, b] = mm(list(picks[h][p]) + q_e + free[4 * h + b], bank(4 * h + b, hi - lo), T.eq[:, w], T.es[:, w],
-                               q[:, lo:hi], s[:, lo:hi], p == 0, p == 1)
+            evs = []
+            for k, d, m in runs:
+                out, src = T.dd[:, DW * b + C * d:DW * b + C * (d + m)], bank(base + b, C * m, C * k)
+                evs.append(cp([ms_[b]], out, src) if on[b] == "v" else act([ms_[b]], out, src, F.Copy))
+            done.append(evs)
+        return done
+
+    d_a = unpack(sorted(out_a) + [r], ZINA, [back_a, z_o], 4, "vsvs")
+    d_b = unpack(sorted(out_b), 0, [back_b], 0, "vsss")
+
+    runs = ((0, 192), (192, NT))
     q_y = []
-    for h, (lo, hi) in enumerate(runs):
-        evs = [tt([dec[h, b]], T.yb[:, 4 * lo + b:4 * hi:4], bank(4 * h + b, hi - lo),
+    for lo, hi in runs:
+        evs = [tt(d_a[b] + d_b[b] + [l_h, m_dd], T.yb[:, 4 * lo + b:4 * hi:4],
+                  T.dd[:, DW * b:DW * b + N * C + 1].indirect(T.lh[:, lo // 16:hi // 16]),
                   T.xb[:, 4 * lo + b:4 * hi:4], A.add) for b in range(4)]
         q_y.append(quant(evs, T.yq[:, lo:hi], T.ys[:, lo:hi], T.yb[:, 4 * lo:4 * hi]))
     for h, (lo, hi) in enumerate(runs):
-        m = mm([q_y[h], q_v], bank(h, hi - lo), T.vq[:], T.vs[:], T.yq[:, lo:hi], T.ys[:, lo:hi], True, True)
+        m = mm([q_y[h], q_v], bank(4 + h, hi - lo), T.vq[:], T.vs[:], T.yq[:, lo:hi], T.ys[:, lo:hi], True, True)
         if h == 0:
-            c = act([m], T.yo[:, lo:hi], bank(h, hi - lo), F.Copy)
+            c = act([m], T.yo[:, lo:hi], bank(4 + h, hi - lo), F.Copy)
         else:
-            c = cp([m], T.yo[:, lo:hi], bank(h, hi - lo))
+            c = cp([m], T.yo[:, lo:hi], bank(4 + h, hi - lo))
         dma("y", "sts", T.oc[:, 4 * lo:4 * hi], u8(T.yq[:, lo:hi]), [q_y[h]])
         dma("s", "sty", T.y[:, lo:hi], T.yo[:, lo:hi], [c])
     for k in range(4):

@@ -3,11 +3,12 @@ from concourse.mybir import dt, AluOpType as A, ActivationFunctionType as F
 
 NT, C, N = 320, 48, 8
 NA, NB, NO = 4 * C, 3 * C, 128
-XOWN, XOUTB, XINB, XINA, XEND = 4 * C, 5 * C, 8 * C, 11 * C, 15 * C
+XOWN, XINB, XINA, XEND = 4 * C, 8 * C, 11 * C, 15 * C
 ZINA, ZOWN = 3 * C, 7 * C
 ZB, ZA, ZEND = ZOWN + NO, ZOWN + NO + NB, ZOWN + NO + NB + NA
 NE = NO + NA + NB
 DW = 400
+DX = N * C + NT
 X4, U8, BF, F32, I32, U16 = "float8_e4m3fn_x4", "uint8", "bfloat16", "float32", "int32", "uint16"
 
 
@@ -22,7 +23,7 @@ SCRATCH = {
     "uq": _sb(128, X4), "us": _sb(128, U8), "uq2": _sb(128, X4), "us2": _sb(128, U8),
     "vq": _sb(128, X4), "vs": _sb(128, U8), "sq": _sb(NT, X4), "ss": _sb(NT, U8),
     "pi": _sb(1, I32), "bits": _sb(8, I32), "bf": _sb(8, F32), "col": _sb(8, F32),
-    "c16": _sb(8, F32), "uoff": _sb(8, U16), "uniq": _sb(20, F32), "jv": _sb(NT, BF),
+    "c16": _sb(8, F32), "uoff": _sb(8, U16), "uniq0": _sb(20, F32), "uniq": _sb(20, F32), "jv": _sb(NT, BF),
     "cx0": _sb(384, BF), "cx": _sb(384, BF), "thr": _sb(160, BF), "cr": _sb(160, F32), "clip": _sb(NT, BF),
     "offw": _sb(2, U16), "ff": _sb(516, BF), "fa": _sb(516, BF), "fe": _sb(516, BF),
     "eq": _sb(512, X4), "es": _sb(512, U8),
@@ -33,7 +34,7 @@ SCRATCH = {
     "hb": _sb(20, F32), "lh": _sb(32, U16), "ob": _sb(32, F32), "ob2": _sb(32, F32), "ob3": _sb(32, F32),
     "xt": _sb(4 * 8 * C, BF), "xq": _sb(XEND, X4), "xs": _sb(XEND, U8),
     "ht": _sb(8 * NE, BF), "hq": _sb(2 * NE, X4), "hs": _sb(2 * NE, U8), "zb": _sb(4 * NE, BF),
-    "zq": _sb(ZEND, X4), "zs": _sb(ZEND, U8), "dd": _sb(4 * DW, BF),
+    "zq": _sb(ZEND, X4), "zs": _sb(ZEND, U8), "dd": _sb(2 * DW, BF), "dx": _sb(2 * DX, BF),
     "yb": _sb(4 * NT, BF), "yq": _sb(NT, X4), "ys": _sb(NT, U8), "yo": _sb(NT, F32),
 }
 SEMAPHORES = ["cv", "cs", "ct", "cg", "ldu", "ldxa", "ldxb", "lda", "ldc", "ldv", "fa", "fb", "ra", "rb",
@@ -133,13 +134,13 @@ def rank_program(g, core, T, topo):
     i_c16 = iota(T.c16[:], [[16, 8]], 0, 0)
     i_thr = iota(T.thr[:], [[0, 20], [C, 8]], C - 193, 0)
     i_jv = iota(T.jv[:], [[1, NT]], -64, 0)
-    i_uniq = iota(T.uniq[:], [[32, 10], [0, 2]], N * C, 1)
+    i_uniq = iota(T.uniq0[:], [[32, 10], [0, 2]], N * C, 0)
     i_cx0 = iota(T.cx0[:], [[0, 96], [-512, 4]], 0, 0)
     i_ff = iota(T.ff[:], [[-1, 516]], 3, 4)
     PAD = 4 * (NO - C)
     pads = [iota(T.ht[:, 4 * C:4 * NO], [[0, PAD]], 0, 0), iota(T.ht[:, 4 * (NO + C):8 * NO], [[0, PAD]], 0, 0),
             iota(T.zb[:, 4 * C:4 * NO], [[0, PAD]], 0, 0)]
-    m_dd = iota(T.dd[:, N * C::DW], [[0, 4]], 0, 0)
+    m_dd = iota(T.dd[:, N * C::DW], [[0, 2]], 0, 0)
     m_ob = iota(T.ob[:], [[0, 32]], 0, 0)
 
     AND, SHR = A.bitwise_and, A.logical_shift_right
@@ -152,8 +153,9 @@ def rank_program(g, core, T, topo):
             ts([i_p], T.bits[:, 2:3], T.pi[:], 3, AND),
             ts([i_p], T.bits[:, 3:4], T.pi[:], 16, AND, 4, SHR),
             ts([i_p], T.bits[:, 4:5], T.pi[:], 1, AND),
-            ts([i_p], T.bits[:, 5:6], T.pi[:], 14, AND)]
-    c_bf = cp(bits, T.bf[:, 0:6], T.bits[:, 0:6])
+            ts([i_p], T.bits[:, 5:6], T.pi[:], 14, AND),
+            ts([i_p], T.bits[:, 6:7], T.pi[:], 31, AND)]
+    c_bf = cp(bits, T.bf[:, 0:7], T.bits[:, 0:7])
     c_uoff = ts([c_bf, i_c16], T.uoff[:], T.c16[:], T.bf[:, 0:1], A.add)
     c_x1 = ts([c_bf], T.col[:, 5:6], T.bf[:, 4:5], T.bf[:, 3:4], A.not_equal, 32.0, A.mult)
     c_x2 = tt([c_x1], T.col[:, 6:7], T.col[:, 5:6], T.bf[:, 5:6], A.add)
@@ -169,6 +171,7 @@ def rank_program(g, core, T, topo):
     p_uc = cp([q_u, c_uoff], u32(T.uq2[:]), u32(T.uq[:]).indirect(T.uoff[:]))
     p_us = act([q_u, c_uoff], T.us2[:], T.us[:].indirect(T.uoff[:]), F.Copy)
     c_clip = act([i_jv, c_top], T.clip[:], T.jv[:], F.Identity, scale=0.0, bias=T.col[:, 1:2])
+    c_uniq = act([i_uniq, c_bf], T.uniq[:], T.uniq0[:], F.Identity, scale=1.0, bias=T.bf[:, 6:7])
     c_cx = act([i_cx0, c_cxc], T.cx[:], T.cx0[:], F.Identity, scale=1.0, bias=T.col[:, 2:3])
     q_xa = quant([ldxa], T.sq[:, :H], T.ss[:, :H], T.xb[:, :4 * H])
     q_xb = quant([ldxb], T.sq[:, H:], T.ss[:, H:], T.xb[:, 4 * H:])
@@ -192,7 +195,7 @@ def rank_program(g, core, T, topo):
     e_a = tt([e_sel, e_th], T.ta[:], T.sel[:, 0::8], T.th[:, 0::8], A.is_gt)
     e_v = act([e_sel], T.tv[:], T.sel[:, 0::8], F.Identity, scale=1.0, bias=192.0)
     c_fe = act([c_fa], T.fe[:], T.fa[:], F.Relu, scale=-1.0, bias=1.0)
-    e_b = tt([e_a, i_uniq], T.tb[:], T.ta[:], T.uniq[:], A.mult)
+    e_b = tt([e_a, c_uniq], T.tb[:], T.ta[:], T.uniq[:], A.mult)
     e_w = tt([e_b, e_v, m_rr], T.rr[:, 0:20], T.tv[:], T.tb[:], A.max)
     h_b = act([e_w], T.hb[:], T.rr[:, 0:20], F.Relu, scale=1000.0, bias=500.0 - 1000.0 * N * C)
     e_t4 = [tr([e_w], T.xx[:, 0:32], T.rr[:, 0:32]), tr([e_w], T.xx[:, 32:64], T.rr[:, 0:32])]
@@ -204,7 +207,7 @@ def rank_program(g, core, T, topo):
 
     out_a, out_b = _pieces(T, topo, r, 1)
     in_a, in_b = _pieces(T, topo, r, -1)
-    order = out_a + [r] + out_b
+    order = sorted(out_a) + [r] + sorted(out_b)
 
     def gather(q, lo, hi):
         runs = []
@@ -254,8 +257,8 @@ def rank_program(g, core, T, topo):
         count["sent"] = count.get("sent", 0) + total
         return (sem, total)
 
-    got_a = send([q_a], "fa", T.xq, T.xs, [(d, C * k, XINA + C * k) for k, d in enumerate(out_a)], True)
-    got_b = send([q_b], "fb", T.xq, T.xs, [(d, XOUTB + C * k, XINB + C * k) for k, d in enumerate(out_b)])
+    got_a = send([q_a], "fa", T.xq, T.xs, [(d, C * order.index(d), XINA + C * k) for k, d in enumerate(out_a)], True)
+    got_b = send([q_b], "fb", T.xq, T.xs, [(d, C * order.index(d), XINB + C * k) for k, d in enumerate(out_b)])
 
     free = {b: [] for b in range(8)}
     free[0], free[1] = [t1a], [t1b]
@@ -266,53 +269,80 @@ def rank_program(g, core, T, topo):
             w = slice(128 * b, 128 * b + 128)
             q_e.append(quant([c_fe], T.eq[:, w], T.es[:, w], T.fe[:, 3 - b:515 - b]))
 
-    def expert(at, col0, n, m, zcol, arrived, lo, hi, bs):
-        xq, xs = T.xq[:, col0:col0 + n], T.xs[:, col0:col0 + n]
-        prod = {}
-        for i, base in ((0, lo), (1, hi)):
-            for b in range(4):
-                w = slice(512 * i + 128 * b, 512 * i + 128 * b + 128)
-                prod[i, b] = mm(arrived + [lda] + free[base + b], bank(base + b, n), T.aq[:, w], T.asc[:, w], xq, xs, True, True)
-        qh = []
-        for i, base, on in ((0, lo, "vsvs"), (1, hi, "svsv")):
-            c0 = 2 * at + n * i
-            evs = list(pads)
-            for b in range(4):
-                out = T.ht[:, 4 * c0 + b:4 * (c0 + m):4]
-                if on[b] == "v":
-                    e = ts([prod[i, b]], out, bank(base + b, m), 0.0, A.max, 0.0625, A.mult)
-                else:
-                    e = act([prod[i, b]], out, bank(base + b, m), F.Relu, scale=0.0625)
-                free[base + b] = [e]
-                evs.append(e)
-            qh.append(quant(evs, T.hq[:, c0:c0 + n], T.hs[:, c0:c0 + n], T.ht[:, 4 * c0:4 * (c0 + n)]))
-        unpackers(bs)
-        for i in range(2):
-            c0 = 2 * at + n * i
-            for b in range(4):
-                w = slice(512 * i + 128 * b, 512 * i + 128 * b + 128)
-                prod[2, b] = mm([qh[i], ldc] + free[lo + b], bank(lo + b, n), T.cq[:, w], T.csc[:, w],
-                                T.hq[:, c0:c0 + n], T.hs[:, c0:c0 + n], i == 0, i == 1)
+    def layer_a(job, i, base, deps):
+        at, col0, n, m, zcol = job
+        prod = []
+        for b in range(4):
+            w = slice(512 * i + 128 * b, 512 * i + 128 * b + 128)
+            prod.append(mm(deps + [lda] + free[base + b], bank(base + b, n), T.aq[:, w], T.asc[:, w],
+                           T.xq[:, col0:col0 + n], T.xs[:, col0:col0 + n], True, True))
+        return prod
+
+    def tile_h(job, i, base, prod, on):
+        at, col0, n, m, zcol = job
+        c0 = 2 * at + n * i
+        evs = list(pads)
+        for b in range(4):
+            out = T.ht[:, 4 * c0 + b:4 * (c0 + m):4]
+            if on[b] == "v":
+                e = ts([prod[b]], out, bank(base + b, m), 0.0, A.max, 0.0625, A.mult)
+            else:
+                e = act([prod[b]], out, bank(base + b, m), F.Relu, scale=0.0625)
+            free[base + b] = [e]
+            evs.append(e)
+        return quant(evs, T.hq[:, c0:c0 + n], T.hs[:, c0:c0 + n], T.ht[:, 4 * c0:4 * (c0 + n)])
+
+    def layer_c(job, i, base, qh):
+        at, col0, n, m, zcol = job
+        c0 = 2 * at + n * i
+        prod = []
+        for b in range(4):
+            w = slice(512 * i + 128 * b, 512 * i + 128 * b + 128)
+            prod.append(mm([qh, ldc] + free[base + b], bank(base + b, n), T.cq[:, w], T.csc[:, w],
+                           T.hq[:, c0:c0 + n], T.hs[:, c0:c0 + n], i == 0, i == 1))
+        return prod
+
+    def tile_z(job, base, prod, on):
+        at, col0, n, m, zcol = job
         evs = []
         for b in range(4):
             out = T.zb[:, 4 * at + b:4 * (at + m):4]
-            if b % 2 == 1:
-                e = ts([prod[2, b]], out, bank(lo + b, m), 0.0625, A.mult)
+            if on[b] == "v":
+                e = ts([prod[b]], out, bank(base + b, m), 0.0625, A.mult)
             else:
-                e = act([prod[2, b]], out, bank(lo + b, m), F.Copy, scale=0.0625)
-            free[lo + b] = [e]
+                e = act([prod[b]], out, bank(base + b, m), F.Copy, scale=0.0625)
+            free[base + b] = [e]
             evs.append(e)
         return quant(evs, T.zq[:, zcol:zcol + n], T.zs[:, zcol:zcol + n], T.zb[:, 4 * at:4 * (at + n)])
 
     def home(s, piece, base):
         return base + C * sorted(_pieces(T, topo, s, 1)[piece]).index(r)
 
-    z_o = expert(0, XOWN, NO, C, ZOWN, [q_b], 0, 4, (0, 1))
-    z_a = expert(NO, XINA, NA, NA, ZA, [got_a], 4, 0, (2,))
+    own, ja, jb = (0, XOWN, NO, C, ZOWN), (NO, XINA, NA, NA, ZA), (NO + NA, XINB, NB, NB, ZB)
+    p0, p1 = layer_a(own, 0, 0, [q_b]), layer_a(own, 1, 4, [q_b])
+    h0 = tile_h(own, 0, 0, p0, "vsvs")
+    h1 = tile_h(own, 1, 4, p1, "svsv")
+    unpackers((0, 1))
+    layer_c(own, 0, 0, h0)
+    z_o = tile_z(own, 0, layer_c(own, 1, 0, h1), "svsv")
+    unpackers((2,))
+    p0, p1 = layer_a(ja, 0, 4, [got_a]), layer_a(ja, 1, 0, [got_a])
+    h0 = tile_h(ja, 0, 4, p0, "vsvs")
+    h1 = tile_h(ja, 1, 0, p1, "svss")
+    layer_c(ja, 0, 4, h0)
+    p0 = layer_a(jb, 0, 0, [got_b])
+    pc = layer_c(ja, 1, 4, h1)
+    h0 = tile_h(jb, 0, 0, p0, "sssv")
+    p1 = layer_a(jb, 1, 0, [got_b])
+    z_a = tile_z(ja, 4, pc, "vsvs")
     back_a = send([z_a], "ra", T.zq, T.zs, [(s, ZA + C * k, home(s, 0, ZINA)) for k, s in enumerate(in_a)])
-    z_b = expert(NO + NA, XINB, NB, NB, ZB, [got_b], 0, 4, (3,))
+    layer_c(jb, 0, 4, h0)
+    h1 = tile_h(jb, 1, 0, p1, "sssv")
+    z_b = tile_z(jb, 4, layer_c(jb, 1, 4, h1), "vsvs")
     back_b = send([z_b], "rb", T.zq, T.zs, [(s, ZB + C * k, home(s, 1, 0)) for k, s in enumerate(in_b)])
 
+    unpackers((3,))
+    x_pl = [act([ldxa, ldxb], T.dx[:, DX * b + N * C:DX * (b + 1)], T.xb[:, b::4], F.Copy) for b in range(2)]
     l_h = ts([e_t5], T.lh[:], T.rr[:].indirect(T.offw[:]), float(N * C), A.min)
     o_a = [tt([h_b, m_ob], T.ob[:, 16 * p:16 * p + 10], T.rr[:, p:20:2], T.hb[:, p:20:2], A.subtract) for p in range(2)]
     q_v = quant([ldv], T.vq[:], T.vs[:], T.vb[:])
@@ -321,7 +351,7 @@ def rank_program(g, core, T, topo):
     for k in range(8):
         dma("y", "sts", T.ol[k], T.ob3[16 * k:16 * k + 10, :], [o_c])
 
-    def unpack(ranks, col0, deps, base, on):
+    def unpack(ranks, col0, deps, base):
         n = C * len(ranks)
         runs = []
         for k, d in enumerate(ranks):
@@ -329,26 +359,34 @@ def rank_program(g, core, T, topo):
                 runs[-1][2] += 1
             else:
                 runs.append([k, d, 1])
-        ms_ = [mm(deps + q_e + free[base + b], bank(base + b, n), T.eq[:, 128 * b:128 * b + 128], T.es[:, 128 * b:128 * b + 128],
-                  T.zq[:, col0:col0 + n], T.zs[:, col0:col0 + n], True, True) for b in range(4)]
+        ms_ = {b: mm(deps + q_e + free[base + b], bank(base + b, n), T.eq[:, 128 * b:128 * b + 128],
+                     T.es[:, 128 * b:128 * b + 128], T.zq[:, col0:col0 + n], T.zs[:, col0:col0 + n], True, True)
+               for b in (0, 2, 1, 3)}
         done = []
         for b in range(4):
             evs = []
             for k, d, m in runs:
-                out, src = T.dd[:, DW * b + C * d:DW * b + C * (d + m)], bank(base + b, C * m, C * k)
-                evs.append(cp([ms_[b]], out, src) if on[b] == "v" else act([ms_[b]], out, src, F.Copy))
+                src = bank(base + b, C * m, C * k)
+                if b < 2:
+                    at = C * order.index(d)
+                    evs.append(tt([ms_[b]], T.dx[:, DX * b + C * d:DX * b + C * (d + m)], src,
+                                  T.xt[:, 4 * at + b:4 * (at + C * m):4], A.add))
+                else:
+                    evs.append(act([ms_[b]], T.dd[:, DW * (b - 2) + C * d:DW * (b - 2) + C * (d + m)], src, F.Copy))
             done.append(evs)
         return done
 
-    d_a = unpack(sorted(out_a) + [r], ZINA, [back_a, z_o], 4, "vsvs")
-    d_b = unpack(sorted(out_b), 0, [back_b], 0, "vsss")
+    d_a = unpack(order[:5], ZINA, [back_a, z_o], 4)
+    d_b = unpack(order[5:], 0, [back_b], 0)
 
     runs = ((0, 192), (192, NT))
     q_y = []
     for lo, hi in runs:
-        evs = [tt(d_a[b] + d_b[b] + [l_h, m_dd], T.yb[:, 4 * lo + b:4 * hi:4],
-                  T.dd[:, DW * b:DW * b + N * C + 1].indirect(T.lh[:, lo // 16:hi // 16]),
-                  T.xb[:, 4 * lo + b:4 * hi:4], A.add) for b in range(4)]
+        evs = [act(d_a[b] + d_b[b] + x_pl + [e_wo], T.yb[:, 4 * lo + b:4 * hi:4],
+                   T.dx[:, DX * b:DX * (b + 1)].indirect(T.wo[:, lo // 16:hi // 16]), F.Copy) for b in range(2)]
+        evs += [tt(d_a[b] + d_b[b] + [l_h, m_dd], T.yb[:, 4 * lo + b:4 * hi:4],
+                   T.dd[:, DW * (b - 2):DW * (b - 2) + N * C + 1].indirect(T.lh[:, lo // 16:hi // 16]),
+                   T.xb[:, 4 * lo + b:4 * hi:4], A.add) for b in range(2, 4)]
         q_y.append(quant(evs, T.yq[:, lo:hi], T.ys[:, lo:hi], T.yb[:, 4 * lo:4 * hi]))
     for h, (lo, hi) in enumerate(runs):
         m = mm([q_y[h], q_v], bank(4 + h, hi - lo), T.vq[:], T.vs[:], T.yq[:, lo:hi], T.ys[:, lo:hi], True, True)

@@ -2,14 +2,21 @@ from concourse.bass import DstId, RemoteDMATransfer
 from concourse.mybir import dt, AluOpType as A, ActivationFunctionType as F
 
 NT, C, N = 320, 48, 8
-NA, NB, NO = 4 * C, 3 * C, 128
-XOWN, XINB, XINA, XEND = 4 * C, 8 * C, 11 * C, 15 * C
-ZINA, ZOWN = 3 * C, 7 * C
+H = NT // 2
+NO = 128
+NA, NB = 3 * C, 4 * C
+XINB, XINA, XEND = N * C, N * C + NB, N * C + NB + NA
+ZINA, ZOWN = NB, NB + NA
 ZB, ZA, ZEND = ZOWN + NO, ZOWN + NO + NB, ZOWN + NO + NB + NA
-NE = NO + NA + NB
 DW = 400
 DX = N * C + NT
-X4, U8, BF, F32, I32, U16 = "float8_e4m3fn_x4", "uint8", "bfloat16", "float32", "int32", "uint16"
+CUT = 160
+GA, GB = 18, 22
+ON = ["svss", "sssv", "vsvs", "svss", "svss", "vsvs", "ssss", "svsv", "svsv"]
+E1 = 3
+APART = 0
+LOADQ = "yyy"
+X4, U8, BF, F32, U16 = "float8_e4m3fn_x4", "uint8", "bfloat16", "float32", "uint16"
 
 
 def _sb(n, d):
@@ -22,18 +29,19 @@ SCRATCH = {
     "aq": _sb(1024, X4), "asc": _sb(1024, U8), "cq": _sb(1024, X4), "csc": _sb(1024, U8),
     "uq": _sb(128, X4), "us": _sb(128, U8), "uq2": _sb(128, X4), "us2": _sb(128, U8),
     "vq": _sb(128, X4), "vs": _sb(128, U8), "sq": _sb(NT, X4), "ss": _sb(NT, U8),
-    "pi": _sb(1, I32), "bits": _sb(8, I32), "bf": _sb(8, F32), "col": _sb(8, F32),
+    "k0": _sb(32, F32), "k1": _sb(32, F32), "k2": _sb(128, F32), "k3": _sb(128, F32), "col": _sb(8, F32),
     "c16": _sb(8, F32), "uoff": _sb(8, U16), "uniq0": _sb(20, F32), "uniq": _sb(20, F32), "jv": _sb(NT, BF),
-    "cx0": _sb(384, BF), "cx": _sb(384, BF), "thr": _sb(160, BF), "cr": _sb(160, F32), "clip": _sb(NT, BF),
+    "cx0": _sb(192, BF), "cx": _sb(384, BF), "thr": _sb(160, BF), "cr": _sb(80, F32), "clip": _sb(H, BF),
     "offw": _sb(2, U16), "ff": _sb(516, BF), "fa": _sb(516, BF), "fe": _sb(516, BF),
     "eq": _sb(512, X4), "es": _sb(512, U8),
     "pt": _sb(NT, F32), "rm": _sb(160, F32), "sm": _sb(160, F32), "gg": _sb(162, BF), "oht": _sb(NT, BF),
     "oh": _sb(NT, BF), "val": _sb(NT, BF), "valt": _sb(NT, BF), "csel": _sb(160, BF), "sel": _sb(160, BF),
-    "th": _sb(160, BF), "ta": _sb(20, F32), "tb": _sb(20, F32), "tv": _sb(20, F32), "rr": _sb(64, F32),
+    "th": _sb(160, BF), "kk": _sb(40, F32), "rr": _sb(128, F32),
     "xx": _sb(64, F32), "wo": _sb(32, U16), "win": _sb(800, BF), "ex": _sb(384, BF), "offs": _sb(96, U16),
     "hb": _sb(20, F32), "lh": _sb(32, U16), "ob": _sb(32, F32), "ob2": _sb(32, F32), "ob3": _sb(32, F32),
-    "xt": _sb(4 * 8 * C, BF), "xq": _sb(XEND, X4), "xs": _sb(XEND, U8),
-    "ht": _sb(8 * NE, BF), "hq": _sb(2 * NE, X4), "hs": _sb(2 * NE, U8), "zb": _sb(4 * NE, BF),
+    "xt": _sb(4 * 8 * C, BF), "xq": _sb(XEND, X4), "xs": _sb(XEND, U8), "wq": _sb(NO, X4), "wsl": _sb(NO, U8),
+    "ot": _sb(4 * (2 * C + NO), BF), "oq": _sb(C + NO, X4), "osl": _sb(C + NO, U8),
+    "ht": _sb(8 * 7 * C, BF), "hq": _sb(2 * 7 * C, X4), "hs": _sb(2 * 7 * C, U8), "zb": _sb(4 * 7 * C, BF),
     "zq": _sb(ZEND, X4), "zs": _sb(ZEND, U8), "dd": _sb(2 * DW, BF), "dx": _sb(2 * DX, BF),
     "yb": _sb(4 * NT, BF), "yq": _sb(NT, X4), "ys": _sb(NT, U8), "yo": _sb(NT, F32),
 }
@@ -41,14 +49,22 @@ SEMAPHORES = ["cv", "cs", "ct", "cg", "ldu", "ldxa", "ldxb", "lda", "ldc", "ldv"
               "sent", "sty", "sts"]
 
 
-def _pieces(T, topo, r, sign):
-    cores = T.cores
-    mine = [k for k in range(N) if topo.die(cores[k]) == topo.die(cores[r])]
+def _pieces(T, topo, r):
+    mine = [k for k in range(N) if topo.die(T.cores[k]) == topo.die(T.cores[r])]
     other = [k for k in range(N) if k not in mine]
-    i = mine.index(r)
-    near = lambda k: mine[(i + sign * k) % len(mine)]
-    far = lambda k: other[(i + sign * k) % len(other)]
-    return [far(0), far(1), near(2), near(3)], [near(1), far(2), far(3)]
+    h = mine.index(r) // 2 * 2
+    return (sorted([k for k in mine[h:h + 2] if k != r] + other[h:h + 2]),
+            sorted(mine[2 - h:4 - h] + other[2 - h:4 - h]))
+
+
+def _runs(numbers):
+    runs = []
+    for k, d in enumerate(numbers):
+        if runs and runs[-1][1] + runs[-1][2] == d:
+            runs[-1][2] += 1
+        else:
+            runs.append([k, d, 1])
+    return runs
 
 
 def rank_program(g, core, T, topo):
@@ -86,6 +102,10 @@ def rank_program(g, core, T, topo):
     u32 = lambda ap: ap.bitcast(dt.uint32)
     bank = lambda b, n, o=0: T.ps[:, 512 * b + o:512 * b + o + n]
 
+    def rev(buf, lo, hi, step=1):
+        last = lo + (hi - 1 - lo) // step * step
+        return buf[:, last::-step] if lo - step < 0 else buf[:, last:lo - step:-step]
+
     def ts(deps, out, in0, s1, op0, s2=None, op1=None):
         if op1 is None:
             return run("v", deps, lambda: V.tensor_scalar(out, in0, s1, None, op0))
@@ -115,288 +135,288 @@ def rank_program(g, core, T, topo):
     def mm(deps, out, wq, ws, xq, xs, start, stop):
         return run("t", deps, lambda: P.matmul_mx(out, wq, ws, xq, xs, start, stop))
 
-    def iota(out, pattern, base, cm, flag=True):
-        if flag:
-            return run("g", [], lambda: g.iota(out, pattern, base, cm, allow_small_or_imprecise_dtypes=True))
-        return run("g", [], lambda: g.iota(out, pattern, base, cm))
+    def iota(out, pattern, base, cm):
+        return run("g", [], lambda: g.iota(out, pattern, base, cm, allow_small_or_imprecise_dtypes=True))
 
-    H = NT // 2
-    ldu = dma("y", "ldu", T.ub[:], T.u[:])
-    ldxa = dma("s", "ldxa", T.xb[:, :4 * H], T.x[:, :4 * H])
-    ldxb = dma("y", "ldxb", T.xb[:, 4 * H:], T.x[:, 4 * H:])
-    dma("y", "lda", u8(T.aq[:]), T.ac[:], [ldu])
+    ra, rb = _pieces(T, topo, r)
+    order = ra + [r] + rb
+
+    ldu = dma(LOADQ[0], "ldu", T.ub[:], T.u[:])
+    ldxa = dma(LOADQ[1], "ldxa", T.xb[:, :4 * H], T.x[:, :4 * H])
+    ldxb = dma(LOADQ[2], "ldxb", T.xb[:, 4 * H:], T.x[:, 4 * H:])
+    dma("y", "lda", u8(T.aq[:]), T.ac[:], [ldxb])
     lda = dma("y", "lda", T.asc[:], T.ap[:])
     dma("y", "ldc", u8(T.cq[:]), T.cc[:])
     ldc = dma("y", "ldc", T.csc[:], T.cp[:])
     ldv = dma("y", "ldv", T.vb[:], T.v[:])
 
-    i_p = iota(T.pi[:], [[0, 1]], 0, 1, False)
+    i_k0 = iota(T.k0[:], [[0, 2], [1, 8], [0, 2]], 0, 0)
     i_c16 = iota(T.c16[:], [[16, 8]], 0, 0)
     i_thr = iota(T.thr[:], [[0, 20], [C, 8]], C - 193, 0)
+    i_k2 = [iota(T.k2[:, 0:32], [[0, 2], [512, 4], [0, 4]], 256, 0),
+            iota(T.k2[:, 32:64], [[0, 8], [1, 4]], 256, 0),
+            iota(T.k2[:, 64:96], [[1, 32]], 0, 0),
+            iota(T.k2[:, 96:112], [[4, 8], [64, 2]], 0, 0),
+            iota(T.k2[:, 112:128], [[4, 8], [-64, 2]], 66, 0)]
+    i_uniq = iota(T.uniq0[:], [[32, 10], [0, 2]], N * C - 193, 0)
     i_jv = iota(T.jv[:], [[1, NT]], -64, 0)
-    i_uniq = iota(T.uniq0[:], [[32, 10], [0, 2]], N * C, 0)
-    i_cx0 = iota(T.cx0[:], [[0, 96], [-512, 4]], 0, 0)
+    i_cx0 = iota(T.cx0[:], [[0, 48], [-512, 4]], 0, 0)
     i_ff = iota(T.ff[:], [[-1, 516]], 3, 4)
-    PAD = 4 * (NO - C)
-    pads = [iota(T.ht[:, 4 * C:4 * NO], [[0, PAD]], 0, 0), iota(T.ht[:, 4 * (NO + C):8 * NO], [[0, PAD]], 0, 0),
-            iota(T.zb[:, 4 * C:4 * NO], [[0, PAD]], 0, 0)]
     m_dd = iota(T.dd[:, N * C::DW], [[0, 2]], 0, 0)
     m_ob = iota(T.ob[:], [[0, 32]], 0, 0)
 
-    AND, SHR = A.bitwise_and, A.logical_shift_right
-    m_g = ms(T.gg[:], 0.5)
     m_oht = ms(T.oht[:], 0.0)
+    c_k1 = tr([i_k0], T.k1[:], T.k0[:])
     m_win = ms(T.win[:, 0:N * C], 255.0)
-    m_rr = ms(T.rr[:], 0.0)
-    bits = [ts([i_p], T.bits[:, 0:1], T.pi[:], 15, AND, 1, SHR),
-            ts([i_p], T.bits[:, 1:2], T.pi[:], 12, AND, 2, SHR),
-            ts([i_p], T.bits[:, 2:3], T.pi[:], 3, AND),
-            ts([i_p], T.bits[:, 3:4], T.pi[:], 16, AND, 4, SHR),
-            ts([i_p], T.bits[:, 4:5], T.pi[:], 1, AND),
-            ts([i_p], T.bits[:, 5:6], T.pi[:], 14, AND),
-            ts([i_p], T.bits[:, 6:7], T.pi[:], 31, AND)]
-    c_bf = cp(bits, T.bf[:, 0:7], T.bits[:, 0:7])
-    c_uoff = ts([c_bf, i_c16], T.uoff[:], T.c16[:], T.bf[:, 0:1], A.add)
-    c_x1 = ts([c_bf], T.col[:, 5:6], T.bf[:, 4:5], T.bf[:, 3:4], A.not_equal, 32.0, A.mult)
-    c_x2 = tt([c_x1], T.col[:, 6:7], T.col[:, 5:6], T.bf[:, 5:6], A.add)
-    c_offw = ts([c_x2], T.offw[:], T.c16[:, 0:2], T.col[:, 6:7], A.add, T.bf[:, 3:4], A.add)
+    c_uoff = ts([c_k1, i_c16], T.uoff[:], T.c16[:], T.k1[:, 0:1], A.add)
+    m_rr = ms(T.rr[:, 40:128], 0.0)
+    m_kk = ms(T.kk[:], 0.0)
+    m_g = ms(T.gg[:, 0:2], 0.0)
+    m_pad = ms(T.ot[:, 4 * 3 * C:], 0.0)
 
-    c_cr = act([i_thr], T.cr[:], T.thr[:], F.Identity, scale=1e26, bias=1.21e28)
-    c_base = act([c_bf], T.col[:, 0:1], T.bf[:, 0:1], F.Identity, scale=float(C), bias=-193.0)
-    c_top = act([c_bf], T.col[:, 1:2], T.bf[:, 0:1], F.Identity, scale=float(C), bias=C + 1 - 193.0)
-    c_cxc = act([c_bf], T.col[:, 2:3], T.bf[:, 1:2], F.Identity, scale=512.0, bias=256.0)
-    c_tc = act([c_bf], T.col[:, 3:4], T.bf[:, 2:3], F.Identity, scale=1.0, bias=256.0)
+    c_base = act([c_k1], T.col[:, 0:1], T.k1[:, 0:1], F.Identity, scale=float(C), bias=-193.0)
+    c_top = act([c_k1], T.col[:, 1:2], T.k1[:, 0:1], F.Identity, scale=float(C), bias=C + 1 - 193.0)
+    c_cr = act([i_thr], T.cr[:], T.thr[:, 0:80], F.Identity, scale=1e26, bias=1.21e28)
+    c_clip = act([c_top], T.clip[:], T.thr[:], F.Identity, scale=0.0, bias=T.col[:, 1:2])
 
     q_u = quant([ldu], T.uq[:], T.us[:], T.ub[:])
     p_uc = cp([q_u, c_uoff], u32(T.uq2[:]), u32(T.uq[:]).indirect(T.uoff[:]))
     p_us = act([q_u, c_uoff], T.us2[:], T.us[:].indirect(T.uoff[:]), F.Copy)
-    c_clip = act([i_jv, c_top], T.clip[:], T.jv[:], F.Identity, scale=0.0, bias=T.col[:, 1:2])
-    c_uniq = act([i_uniq, c_bf], T.uniq[:], T.uniq0[:], F.Identity, scale=1.0, bias=T.bf[:, 6:7])
-    c_cx = act([i_cx0, c_cxc], T.cx[:], T.cx0[:], F.Identity, scale=1.0, bias=T.col[:, 2:3])
     q_xa = quant([ldxa], T.sq[:, :H], T.ss[:, :H], T.xb[:, :4 * H])
-    q_xb = quant([ldxb], T.sq[:, H:], T.ss[:, H:], T.xb[:, 4 * H:])
     s_a = mm([p_uc, p_us, q_xa], bank(0, H), T.uq2[:], T.us2[:], T.sq[:, :H], T.ss[:, :H], True, True)
+    c_k3 = tr(i_k2, T.k3[:], T.k2[:])
+
+    W = H // 2
+    half = lambda buf, k, step=1: buf[:, H * k:H * k + H:step]
+    part = lambda buf, k, o=0, step=1: buf[:, W * k + o:W * k + W + o:step]
+    f_t1 = lambda k, e: tr([e], half(T.pt, k), bank(k, H))
+    f_rm = lambda k, e: scan([e, c_cr], part(T.rm, k), T.cr[:], half(T.pt, k, 2), 0.0, A.min, A.max)
+    f_sm = lambda k: scan([], rev(T.sm, W * k, W * k + W), T.cr[:], rev(T.pt, H * k, H * k + H, 2), 0.0, A.min, A.max)
+    f_ng = lambda k, e: tt([e, m_g], part(T.gg, k, 1), part(T.rm, k), part(T.sm, k), A.is_lt)
+    f_st = lambda k, e: scan([e, m_oht], rev(T.oht, H * k, H * k + H, 2), rev(T.gg, W * k, W * k + W),
+                             rev(T.gg, W * k + 1, W * k + W + 1), 0.0, A.max, A.subtract)
+    f_r0 = lambda k, e: tt([e], half(T.oht, k, 16), part(T.rm, k, 0, 8), part(T.sm, k, 0, 8), A.is_ge)
+    f_t2 = lambda k, e: tr([e], half(T.oh, k), half(T.oht, k))
+    f_t3 = lambda k, e: tr([e], half(T.valt, k), half(T.val, k))
+    t1a = f_t1(0, s_a)
+    q_xb = quant([ldxb], T.sq[:, H:], T.ss[:, H:], T.xb[:, 4 * H:])
     s_b = mm([q_xb], bank(1, H), T.uq2[:], T.us2[:], T.sq[:, H:], T.ss[:, H:], True, True)
-    t1a = tr([s_a], T.pt[:, :H], bank(0, H))
-    t1b = tr([s_b], T.pt[:, H:], bank(1, H))
-
-    e_r = scan([t1a, t1b, c_cr], T.rm[:], T.cr[:], T.pt[:, 0:NT:2], 0.0, A.min, A.max)
-    e_s = scan([], T.sm[:, 159::-1], T.cr[:], T.pt[:, NT - 2::-2], 0.0, A.min, A.max)
-    e_g = [tt([e_r, e_s, m_g], T.gg[:, 1 + o:161:st], T.rm[:, o::st], T.sm[:, o::st], A.is_ge)
-           for o, st in ((0, 2), (1, 4), (3, 8))]
-    e_oh = tt(e_g + [m_oht], T.oht[:, 0:NT:2], T.gg[:, 1:161], T.gg[:, 0:160], A.is_gt)
-    e_c = act(e_g, T.csel[:], T.gg[:, 160:0:-1], F.Identity, scale=-1024.0, bias=256.0)
+    x_pl = [act([ldxa, ldxb], T.dx[:, N * C:DX], T.xb[:, 0::4], F.Copy)]
+    f_rm(0, t1a)
+    sma = f_sm(0)
+    t1b = f_t1(1, s_b)
+    nga = f_ng(0, sma)
+    f_rm(1, t1b)
+    smb = f_sm(1)
+    sta = f_st(0, nga)
+    ngb = f_ng(1, smb)
+    e_c = act([ngb], T.csel[:], rev(T.gg, 1, 161), F.Identity, scale=1024.0, bias=-768.0)
+    c_uniq = act([i_uniq, c_k3], T.uniq[:], T.uniq0[:], F.Identity, scale=1.0, bias=T.k3[:, 64:65])
+    c_cx = [act([i_cx0], T.cx[:, o:o + 192], T.cx0[:], F.Identity, scale=1.0, bias=T.k3[:, 0:1]) for o in (0, 192)]
+    x_pl.append(act([], T.dx[:, DX + N * C:2 * DX], T.xb[:, 1::4], F.Copy))
     c_fa = act([i_ff], T.fa[:], T.ff[:], F.Abs)
-    e_t2 = tr([e_oh], T.oh[:], T.oht[:])
-    e_cnt = scan([e_t2, c_clip, c_base], T.val[:], T.oh[:], T.clip[:], T.col[:, 0:1], A.add, A.min)
-    e_th = scan([e_c, i_thr], T.th[:, 159::-1], T.csel[:], T.thr[:, 159::-1], 0.0, A.min, A.max)
-    e_t3 = tr([e_cnt], T.valt[:], T.val[:])
-    e_sel = scan([e_t3], T.sel[:, 159::-1], T.csel[:], T.valt[:, NT - 2::-2], 0.0, A.min, A.max)
-    e_a = tt([e_sel, e_th], T.ta[:], T.sel[:, 0::8], T.th[:, 0::8], A.is_gt)
-    e_v = act([e_sel], T.tv[:], T.sel[:, 0::8], F.Identity, scale=1.0, bias=192.0)
+    r0a = f_r0(0, sta)
+    stb = f_st(1, ngb)
+    t2a = f_t2(0, r0a)
+    r0b = f_r0(1, stb)
+    n_a = scan([t2a, c_base, c_clip], half(T.val, 0), half(T.oh, 0), T.clip[:], T.col[:, 0:1], A.add, A.min)
+    t2b = f_t2(1, r0b)
+    f_t3(0, n_a)
+    n_b = scan([t2b], half(T.val, 1), half(T.oh, 1), T.clip[:], T.val[:, H - 1:H], A.add, A.min)
+    e_th = scan([e_c, i_thr], rev(T.th, 0, 160), T.csel[:], rev(T.thr, 0, 160), 0.0, A.min, A.max)
+    t3b = f_t3(1, n_b)
+    e_k = tt([e_th, c_uniq, m_kk], T.kk[:, 0::2], T.uniq[:], T.th[:, 0::8], A.subtract)
+    e_sel = scan([t3b], rev(T.sel, 0, 160), T.csel[:], rev(T.valt, 0, NT, 2), 0.0, A.min, A.max)
+    c_offw = ts([c_k3], T.offw[:], T.c16[:, 0:3:2], T.k3[:, 96:97], A.add)
+    e_a = tt([e_sel], T.sel[:, 4::8], T.sel[:, 0::8], T.th[:, 0::8], A.is_gt)
+    e_w = scan([e_a, e_k], rev(T.rr, 0, 40), rev(T.kk, 0, 40), rev(T.sel, 0, 160, 4), 0.0, A.mult, A.add)
     c_fe = act([c_fa], T.fe[:], T.fa[:], F.Relu, scale=-1.0, bias=1.0)
-    e_b = tt([e_a, c_uniq], T.tb[:], T.ta[:], T.uniq[:], A.mult)
-    e_w = tt([e_b, e_v, m_rr], T.rr[:, 0:20], T.tv[:], T.tb[:], A.max)
-    h_b = act([e_w], T.hb[:], T.rr[:, 0:20], F.Relu, scale=1000.0, bias=500.0 - 1000.0 * N * C)
-    e_t4 = [tr([e_w], T.xx[:, 0:32], T.rr[:, 0:32]), tr([e_w], T.xx[:, 32:64], T.rr[:, 0:32])]
-    e_t5 = tr(e_t4, T.rr[:, 32:64], T.xx[:, 16:48])
-    e_wo = cp([e_t5, c_offw], T.wo[:], T.rr[:].indirect(T.offw[:]))
+    h_b = act([e_w], T.hb[:], T.rr[:, 1:40:2], F.Identity, scale=1000.0, bias=-192.0)
+    e_t4 = [tr([e_w, m_rr], T.xx[:, 0:32], T.rr[:, 0:64:2]), tr([e_w], T.xx[:, 32:64], T.rr[:, 0:64:2])]
+    e_t5 = tr(e_t4, T.rr[:, 64:128:2], T.xx[:, 16:48])
+    lists = T.rr[:].indirect(T.offw[:])
+    e_wo = ts([e_t5, c_offw], T.wo[:], lists, 192.0, A.add)
     e_sc = cp([e_wo, i_jv, m_win], T.win[:].indirect(T.wo[:, 0:20]), T.jv[:])
-    e_ex = scan([e_sc, c_cx], T.ex[:], T.cx[:], T.win[:, 0:N * C], 0.0, A.max, A.min)
-    e_of = ts([e_ex, c_tc], T.offs[:], T.ex[:, 3::4], 4.0, A.mult, T.col[:, 3:4], A.add)
-
-    out_a, out_b = _pieces(T, topo, r, 1)
-    in_a, in_b = _pieces(T, topo, r, -1)
-    order = sorted(out_a) + [r] + sorted(out_b)
+    e_ex = scan([e_sc] + c_cx, T.ex[:], T.cx[:], T.win[:, 0:N * C], 0.0, A.max, A.min)
+    e_of = [ts([e_ex], T.offs[:], T.ex[:, 3::4], 4.0, A.mult, T.k3[:, 32:33], A.add)]
 
     def gather(q, lo, hi):
-        runs = []
-        for k in range(lo, hi):
-            o = 12 * order[k // 2] + 6 * (k % 2)
-            if runs and runs[-1][1] + runs[-1][2] == o:
-                runs[-1][2] += 6
-            else:
-                runs.append([k, o, 6])
         evs = []
-        for k, o, n in runs:
-            out = T.xt[:, 96 * k:96 * k + 16 * n]
-            src = T.xb[:].indirect(T.offs[:, o:o + n])
-            evs.append(cp([e_of, ldxa, ldxb], out, src) if q == "v" else act([e_of, ldxa, ldxb], out, src, F.Copy))
+        for k, o, n in _runs([6 * order[k // 12] + k % 12 // 2 for k in range(lo, hi, 2)]):
+            out = T.xt[:, 16 * lo + 32 * k:16 * lo + 32 * (k + n)]
+            src = T.xb[:].indirect(T.offs[:, 2 * o:2 * (o + n)])
+            evs.append(cp(e_of, out, src) if q == "v" else act(e_of, out, src, F.Copy))
         return evs
 
-    ga = gather("v", 0, 4) + gather("s", 4, 8)
-    q_a = quant(ga, T.xq[:, 0:NA], T.xs[:, 0:NA], T.xt[:, 0:4 * NA])
-    gb = gather("v", 8, 11) + gather("s", 11, 16)
-    q_b = quant(gb, T.xq[:, NA:2 * NA], T.xs[:, NA:2 * NA], T.xt[:, 4 * NA:8 * NA])
+    q_a = quant(gather("v", 0, GA) + gather("s", GA, 36), T.xq[:, 0:NA], T.xs[:, 0:NA], T.xt[:, 0:4 * NA])
+    go = gather("s", 36, 48)
+    gb = gather("s", 48 + GB, 96)
+    q_o = quant(go, T.wq[:], T.wsl[:], T.xt[:, 4 * (NA + C - NO):4 * (NA + C)])
+    gb += gather("v", 48, 48 + GB)
+    q_b = quant(gb, T.xq[:, NA + C:N * C], T.xs[:, NA + C:N * C], T.xt[:, 4 * (NA + C):4 * N * C])
 
-    def send(deps, sem, q, s, moves, apart=False):
+    def send(deps, sem, q, s, moves, apart=0):
         wait("g", deps)
         eng = topo.engines(core, T.cores[moves[0][0]])
         far = [m for m in moves if topo.die(T.cores[m[0]]) != topo.die(core)]
         near = [m for m in moves if m not in far]
         total = 0
         for buf, flip in ((q, 0), (s, 1)):
-            if apart:
-                es = eng[flip::2]
-                lanes = ((far, es[flip::2]), (near, es[1 - flip::2]))
-            else:
-                lanes = ((far, eng[1 - flip::2]), (near, eng[flip::2]))
+            es = eng[flip::2] if apart else eng
             trs = []
-            for part, es in lanes:
-                w = len(es) // len(part)
-                for k, (d, here, there) in enumerate(part):
-                    mask = sum(1 << e for e in es[w * k:w * k + w])
+            for some, lanes in ((far, es[1 - flip::2]), (near, es[flip::2])):
+                w = len(lanes) // len(some)
+                for k, (d, here, there) in enumerate(some):
                     rid, pid, _ = topo.addr(T.cores[d])
                     src, dst = buf[:, here:here + C], buf[:, there:there + C]
                     if not flip:
                         src, dst = u8(src), u8(dst)
-                    trs.append(RemoteDMATransfer(dst_ids=[DstId(rid=rid, pnc=pid)], dma_engine_mask=mask,
-                                                 remote_sem=T.sem[sem], src=src, dst=dst))
-                    total += w
+                    trs.append(RemoteDMATransfer(dst_ids=[DstId(rid=rid, pnc=pid)], remote_sem=T.sem[sem], src=src, dst=dst,
+                                                 dma_engine_mask=sum(1 << e for e in lanes[w * k:w * k + w])))
+            total += len(es)
             g.remote_dma_fused(trs, local_sem=T.sem["sent"])
         count["sent"] = count.get("sent", 0) + total
         return (sem, total)
 
-    got_a = send([q_a], "fa", T.xq, T.xs, [(d, C * order.index(d), XINA + C * k) for k, d in enumerate(out_a)], True)
-    got_b = send([q_b], "fb", T.xq, T.xs, [(d, C * order.index(d), XINB + C * k) for k, d in enumerate(out_b)])
+    def there(d, piece, base):
+        return base + C * _pieces(T, topo, d)[piece].index(r)
+
+    got_a = send([q_a], "fa", T.xq, T.xs, [(d, C * order.index(d), there(d, 0, XINA)) for d in ra], APART)
+    got_b = send([q_b], "fb", T.xq, T.xs, [(d, C * order.index(d), there(d, 1, XINB)) for d in rb])
 
     free = {b: [] for b in range(8)}
     free[0], free[1] = [t1a], [t1b]
     q_e = []
 
-    def unpackers(bs):
-        for b in bs:
+    def unpackers(lo, hi):
+        for b in range(lo, hi):
             w = slice(128 * b, 128 * b + 128)
             q_e.append(quant([c_fe], T.eq[:, w], T.es[:, w], T.fe[:, 3 - b:515 - b]))
 
-    def layer_a(job, i, base, deps):
-        at, col0, n, m, zcol = job
+    def layer(wq, ws, i, base, q, s, col0, n, deps, start, stop):
         prod = []
         for b in range(4):
             w = slice(512 * i + 128 * b, 512 * i + 128 * b + 128)
-            prod.append(mm(deps + [lda] + free[base + b], bank(base + b, n), T.aq[:, w], T.asc[:, w],
-                           T.xq[:, col0:col0 + n], T.xs[:, col0:col0 + n], True, True))
+            prod.append(mm(deps + free[base + b], bank(base + b, n), wq[:, w], ws[:, w],
+                           q[:, col0:col0 + n], s[:, col0:col0 + n], start, stop))
         return prod
 
-    def tile_h(job, i, base, prod, on):
-        at, col0, n, m, zcol = job
-        c0 = 2 * at + n * i
-        evs = list(pads)
-        for b in range(4):
-            out = T.ht[:, 4 * c0 + b:4 * (c0 + m):4]
-            if on[b] == "v":
-                e = ts([prod[b]], out, bank(base + b, m), 0.0, A.max, 0.0625, A.mult)
-            else:
-                e = act([prod[b]], out, bank(base + b, m), F.Relu, scale=0.0625)
-            free[base + b] = [e]
-            evs.append(e)
-        return quant(evs, T.hq[:, c0:c0 + n], T.hs[:, c0:c0 + n], T.ht[:, 4 * c0:4 * (c0 + n)])
-
-    def layer_c(job, i, base, qh):
-        at, col0, n, m, zcol = job
-        c0 = 2 * at + n * i
-        prod = []
-        for b in range(4):
-            w = slice(512 * i + 128 * b, 512 * i + 128 * b + 128)
-            prod.append(mm([qh, ldc] + free[base + b], bank(base + b, n), T.cq[:, w], T.csc[:, w],
-                           T.hq[:, c0:c0 + n], T.hs[:, c0:c0 + n], i == 0, i == 1))
-        return prod
-
-    def tile_z(job, base, prod, on):
-        at, col0, n, m, zcol = job
+    def leave(tile, at, m, base, prod, on, relu, o=0):
         evs = []
         for b in range(4):
-            out = T.zb[:, 4 * at + b:4 * (at + m):4]
-            if on[b] == "v":
-                e = ts([prod[b]], out, bank(base + b, m), 0.0625, A.mult)
+            out = tile[:, 4 * at + b:4 * (at + m):4]
+            if on[b] == "s":
+                e = act([prod[b]], out, bank(base + b, m, o), F.Relu if relu else F.Copy, scale=0.0625)
+            elif relu:
+                e = ts([prod[b]], out, bank(base + b, m, o), 0.0, A.max, 0.0625, A.mult)
             else:
-                e = act([prod[b]], out, bank(base + b, m), F.Copy, scale=0.0625)
+                e = ts([prod[b]], out, bank(base + b, m, o), 0.0625, A.mult)
             free[base + b] = [e]
             evs.append(e)
+        return evs
+
+    p0 = layer(T.aq, T.asc, 0, 0, T.wq, T.wsl, 0, NO, [q_o, lda], True, True)
+    p1 = layer(T.aq, T.asc, 1, 4, T.wq, T.wsl, 0, NO, [q_o, lda], True, True)
+    evs = leave(T.ot, C, C, 0, p0, ON[6], True, NO - C) + leave(T.ot, 2 * C, C, 4, p1, ON[7], True, NO - C)
+    h = quant(evs + [m_pad], T.oq[:], T.osl[:], T.ot[:, 4 * C:])
+    unpackers(0, E1)
+    layer(T.cq, T.csc, 0, 0, T.oq, T.osl, 0, NO, [h, ldc], True, False)
+    pc = layer(T.cq, T.csc, 1, 0, T.oq, T.osl, C, NO, [h], False, True)
+    evs = leave(T.ot, 0, C, 0, pc, ON[8], False)
+    z_o = quant(evs, T.zq[:, ZOWN:ZOWN + NO], T.zs[:, ZOWN:ZOWN + NO], T.ot[:, 0:4 * NO])
+
+    ja, jb = (0, XINA, NA, ZA), (NA, XINB, NB, ZB)
+
+    def la(job, i, base, got):
+        return layer(T.aq, T.asc, i, base, T.xq, T.xs, job[1], job[2], [got], True, True)
+
+    def tile_h(job, i, base, prod, on):
+        c0, n = 2 * job[0] + job[2] * i, job[2]
+        evs = leave(T.ht, c0, n, base, prod, on, True)
+        return quant(evs, T.hq[:, c0:c0 + n], T.hs[:, c0:c0 + n], T.ht[:, 4 * c0:4 * (c0 + n)])
+
+    def lc(job, i, base, qh):
+        return layer(T.cq, T.csc, i, base, T.hq, T.hs, 2 * job[0] + job[2] * i, job[2], [qh], i == 0, i == 1)
+
+    def tile_z(job, base, prod, on):
+        at, col0, n, zcol = job
+        evs = leave(T.zb, at, n, base, prod, on, False)
         return quant(evs, T.zq[:, zcol:zcol + n], T.zs[:, zcol:zcol + n], T.zb[:, 4 * at:4 * (at + n)])
 
-    def home(s, piece, base):
-        return base + C * sorted(_pieces(T, topo, s, 1)[piece]).index(r)
+    p0, p1 = la(ja, 0, 4, got_a), la(ja, 1, 0, got_a)
+    ha0 = tile_h(ja, 0, 4, p0, ON[0])
+    p0 = la(jb, 0, 4, got_b)
+    ha1 = tile_h(ja, 1, 0, p1, ON[1])
+    p1 = la(jb, 1, 0, got_b)
+    hb0 = tile_h(jb, 0, 4, p0, ON[2])
+    lc(ja, 0, 4, ha0)
+    pa = lc(ja, 1, 4, ha1)
+    hb1 = tile_h(jb, 1, 0, p1, ON[3])
+    lc(jb, 0, 0, hb0)
+    pb = lc(jb, 1, 0, hb1)
+    z_a = tile_z(ja, 4, pa, ON[4])
+    back_a = send([z_a], "ra", T.zq, T.zs, [(s, ZA + C * k, there(s, 0, ZINA)) for k, s in enumerate(ra)])
+    z_b = tile_z(jb, 0, pb, ON[5])
+    back_b = send([z_b], "rb", T.zq, T.zs, [(s, ZB + C * k, there(s, 1, 0)) for k, s in enumerate(rb)])
 
-    own, ja, jb = (0, XOWN, NO, C, ZOWN), (NO, XINA, NA, NA, ZA), (NO + NA, XINB, NB, NB, ZB)
-    p0, p1 = layer_a(own, 0, 0, [q_b]), layer_a(own, 1, 4, [q_b])
-    h0 = tile_h(own, 0, 0, p0, "vsvs")
-    h1 = tile_h(own, 1, 4, p1, "svsv")
-    unpackers((0, 1))
-    layer_c(own, 0, 0, h0)
-    z_o = tile_z(own, 0, layer_c(own, 1, 0, h1), "svsv")
-    unpackers((2,))
-    p0, p1 = layer_a(ja, 0, 4, [got_a]), layer_a(ja, 1, 0, [got_a])
-    h0 = tile_h(ja, 0, 4, p0, "vsvs")
-    h1 = tile_h(ja, 1, 0, p1, "svss")
-    layer_c(ja, 0, 4, h0)
-    p0 = layer_a(jb, 0, 0, [got_b])
-    pc = layer_c(ja, 1, 4, h1)
-    h0 = tile_h(jb, 0, 0, p0, "sssv")
-    p1 = layer_a(jb, 1, 0, [got_b])
-    z_a = tile_z(ja, 4, pc, "vsvs")
-    back_a = send([z_a], "ra", T.zq, T.zs, [(s, ZA + C * k, home(s, 0, ZINA)) for k, s in enumerate(in_a)])
-    layer_c(jb, 0, 4, h0)
-    h1 = tile_h(jb, 1, 0, p1, "sssv")
-    z_b = tile_z(jb, 4, layer_c(jb, 1, 4, h1), "vsvs")
-    back_b = send([z_b], "rb", T.zq, T.zs, [(s, ZB + C * k, home(s, 1, 0)) for k, s in enumerate(in_b)])
-
-    unpackers((3,))
-    x_pl = [act([ldxa, ldxb], T.dx[:, DX * b + N * C:DX * (b + 1)], T.xb[:, b::4], F.Copy) for b in range(2)]
-    l_h = ts([e_t5], T.lh[:], T.rr[:].indirect(T.offw[:]), float(N * C), A.min)
-    o_a = [tt([h_b, m_ob], T.ob[:, 16 * p:16 * p + 10], T.rr[:, p:20:2], T.hb[:, p:20:2], A.subtract) for p in range(2)]
+    l_h = ts([e_t5], T.lh[:], lists, 192.0, A.add, float(N * C), A.min)
+    o_a = [tt([h_b, m_ob], T.ob[:, 16 * p:16 * p + 10], T.rr[:, 2 * p:40:4], T.hb[:, p:20:2], A.subtract) for p in range(2)]
     q_v = quant([ldv], T.vq[:], T.vs[:], T.vb[:])
     o_b = tr(o_a, T.ob2[:], T.ob[:])
+    unpackers(E1, 4)
     o_c = ts([o_b], T.ob3[:], T.ob2[:], -1.0, A.max)
     for k in range(8):
         dma("y", "sts", T.ol[k], T.ob3[16 * k:16 * k + 10, :], [o_c])
 
     def unpack(ranks, col0, deps, base):
         n = C * len(ranks)
-        runs = []
-        for k, d in enumerate(ranks):
-            if runs and runs[-1][1] + runs[-1][2] == d:
-                runs[-1][2] += 1
-            else:
-                runs.append([k, d, 1])
-        ms_ = {b: mm(deps + q_e + free[base + b], bank(base + b, n), T.eq[:, 128 * b:128 * b + 128],
-                     T.es[:, 128 * b:128 * b + 128], T.zq[:, col0:col0 + n], T.zs[:, col0:col0 + n], True, True)
-               for b in (0, 2, 1, 3)}
+        prod = {b: mm(deps + q_e + free[base + b], bank(base + b, n), T.eq[:, 128 * b:128 * b + 128],
+                      T.es[:, 128 * b:128 * b + 128], T.zq[:, col0:col0 + n], T.zs[:, col0:col0 + n], True, True)
+                for b in (0, 2, 1, 3)}
         done = []
         for b in range(4):
             evs = []
-            for k, d, m in runs:
+            for k, d, m in _runs(ranks):
                 src = bank(base + b, C * m, C * k)
                 if b < 2:
                     at = C * order.index(d)
-                    evs.append(tt([ms_[b]], T.dx[:, DX * b + C * d:DX * b + C * (d + m)], src,
+                    evs.append(tt([prod[b]], T.dx[:, DX * b + C * d:DX * b + C * (d + m)], src,
                                   T.xt[:, 4 * at + b:4 * (at + C * m):4], A.add))
                 else:
-                    evs.append(act([ms_[b]], T.dd[:, DW * (b - 2) + C * d:DW * (b - 2) + C * (d + m)], src, F.Copy))
+                    evs.append(act([prod[b]], T.dd[:, DW * (b - 2) + C * d:DW * (b - 2) + C * (d + m)], src, F.Copy))
+            free[base + b] = evs[-1:]
             done.append(evs)
         return done
 
-    d_a = unpack(order[:5], ZINA, [back_a, z_o], 4)
-    d_b = unpack(order[5:], 0, [back_b], 0)
+    d_a = unpack(ra + [r], ZINA, [back_a, z_o], 4)
+    d_b = unpack(rb, 0, [back_b], 0)
 
-    runs = ((0, 192), (192, NT))
-    q_y = []
-    for lo, hi in runs:
-        evs = [act(d_a[b] + d_b[b] + x_pl + [e_wo], T.yb[:, 4 * lo + b:4 * hi:4],
-                   T.dx[:, DX * b:DX * (b + 1)].indirect(T.wo[:, lo // 16:hi // 16]), F.Copy) for b in range(2)]
-        evs += [tt(d_a[b] + d_b[b] + [l_h, m_dd], T.yb[:, 4 * lo + b:4 * hi:4],
-                   T.dd[:, DW * (b - 2):DW * (b - 2) + N * C + 1].indirect(T.lh[:, lo // 16:hi // 16]),
-                   T.xb[:, 4 * lo + b:4 * hi:4], A.add) for b in range(2, 4)]
-        q_y.append(quant(evs, T.yq[:, lo:hi], T.ys[:, lo:hi], T.yb[:, 4 * lo:4 * hi]))
-    for h, (lo, hi) in enumerate(runs):
-        m = mm([q_y[h], q_v], bank(4 + h, hi - lo), T.vq[:], T.vs[:], T.yq[:, lo:hi], T.ys[:, lo:hi], True, True)
+    def pick_s(b, lo, hi):
+        return act(d_a[b] + d_b[b] + x_pl + [e_wo], T.yb[:, 4 * lo + b:4 * hi:4],
+                   T.dx[:, DX * b:DX * (b + 1)].indirect(T.wo[:, lo // 16:hi // 16]), F.Copy)
+
+    def pick_v(b, lo, hi):
+        return tt(d_a[b] + d_b[b] + [l_h, m_dd], T.yb[:, 4 * lo + b:4 * hi:4],
+                  T.dd[:, DW * (b - 2):DW * (b - 2) + N * C + 1].indirect(T.lh[:, lo // 16:hi // 16]),
+                  T.xb[:, 4 * lo + b:4 * hi:4], A.add)
+
+    def q_run(evs, lo, hi):
+        return quant(evs, T.yq[:, lo:hi], T.ys[:, lo:hi], T.yb[:, 4 * lo:4 * hi])
+
+    e0 = [pick_s(0, 0, CUT), pick_s(1, 0, CUT), pick_v(2, 0, CUT), pick_v(3, 0, CUT)]
+    e1 = [pick_s(0, CUT, NT), pick_s(1, CUT, NT), pick_v(2, CUT, NT)]
+    q_y = [q_run(e0, 0, CUT)]
+    e1.append(pick_v(3, CUT, NT))
+    q_y.append(q_run(e1, CUT, NT))
+    for h, (lo, hi) in enumerate(((0, CUT), (CUT, NT))):
+        m = mm([q_y[h], q_v] + free[4 + h], bank(4 + h, hi - lo), T.vq[:], T.vs[:], T.yq[:, lo:hi], T.ys[:, lo:hi], True, True)
+        dma("y", "sts", T.oc[:, 4 * lo:4 * hi], u8(T.yq[:, lo:hi]), [q_y[h]])
         if h == 0:
             c = act([m], T.yo[:, lo:hi], bank(4 + h, hi - lo), F.Copy)
         else:
             c = cp([m], T.yo[:, lo:hi], bank(4 + h, hi - lo))
-        dma("y", "sts", T.oc[:, 4 * lo:4 * hi], u8(T.yq[:, lo:hi]), [q_y[h]])
+            for k in range(4):
+                dma("sy"[k % 2], "sts", T.osc[4 * k:4 * k + 4, :], T.ys[32 * k:32 * k + 4, :], q_y)
         dma("s", "sty", T.y[:, lo:hi], T.yo[:, lo:hi], [c])
-    for k in range(4):
-        dma("y", "sts", T.osc[4 * k:4 * k + 4, :], T.ys[32 * k:32 * k + 4, :], q_y)
 
     wait("g", list(count.items()))

@@ -6,16 +6,12 @@ H = NT // 2
 NO = 128
 NA, NB = 3 * C, 4 * C
 XINB, XINA, XEND = N * C, N * C + NB, N * C + NB + NA
-ZINA, ZOWN = NB, NB + NA
-ZB, ZA, ZEND = ZOWN + NO, ZOWN + NO + NB, ZOWN + NO + NB + NA
-DW = 400
-DX = N * C + NT
-CUT = 160
-GA, GB = 18, 22
-ON = ["svss", "sssv", "vsvs", "svss", "svss", "vsvs", "ssss", "svsv", "svsv"]
-E1 = 3
-APART = 0
-LOADQ = "yyy"
+ZIN = (NA + NO, NA + NO + 2 * C)
+ZB = NA + NO + NB
+ZA, ZEND = ZB + 2 * NO, ZB + 2 * NO + NA
+FAR = 2 * N * C
+DX = FAR + NT
+GB = 20
 X4, U8, BF, F32, U16 = "float8_e4m3fn_x4", "uint8", "bfloat16", "float32", "uint16"
 
 
@@ -29,32 +25,32 @@ SCRATCH = {
     "aq": _sb(1024, X4), "asc": _sb(1024, U8), "cq": _sb(1024, X4), "csc": _sb(1024, U8),
     "uq": _sb(128, X4), "us": _sb(128, U8), "uq2": _sb(128, X4), "us2": _sb(128, U8),
     "vq": _sb(128, X4), "vs": _sb(128, U8), "sq": _sb(NT, X4), "ss": _sb(NT, U8),
-    "k0": _sb(32, F32), "k1": _sb(32, F32), "k2": _sb(128, F32), "k3": _sb(128, F32), "col": _sb(8, F32),
-    "c16": _sb(8, F32), "uoff": _sb(8, U16), "uniq0": _sb(20, F32), "uniq": _sb(20, F32), "jv": _sb(NT, BF),
-    "cx0": _sb(192, BF), "cx": _sb(384, BF), "thr": _sb(160, BF), "cr": _sb(80, F32), "clip": _sb(H, BF),
-    "offw": _sb(2, U16), "ff": _sb(516, BF), "fa": _sb(516, BF), "fe": _sb(516, BF),
-    "eq": _sb(512, X4), "es": _sb(512, U8),
+    "k0": _sb(32, F32), "k1": _sb(32, F32), "k2": _sb(192, F32), "k3": _sb(192, F32), "col": _sb(8, F32),
+    "c16": _sb(8, F32), "uoff": _sb(8, U16), "uniq0": _sb(20, F32), "uniq": _sb(20, F32), "j0": _sb(H, BF),
+    "jv": _sb(NT, BF), "cx0": _sb(192, BF), "cx": _sb(384, BF), "thr": _sb(160, BF), "cr": _sb(80, F32),
+    "clip": _sb(H, BF), "offw": _sb(2, U16), "offo": _sb(2, U16), "ff": _sb(516, BF), "fa": _sb(516, BF),
+    "fe": _sb(516, BF), "eq": _sb(512, X4), "es": _sb(512, U8),
     "pt": _sb(NT, F32), "rm": _sb(160, F32), "sm": _sb(160, F32), "gg": _sb(162, BF), "oht": _sb(NT, BF),
     "oh": _sb(NT, BF), "val": _sb(NT, BF), "valt": _sb(NT, BF), "csel": _sb(160, BF), "sel": _sb(160, BF),
-    "th": _sb(160, BF), "kk": _sb(40, F32), "rr": _sb(128, F32),
-    "xx": _sb(64, F32), "wo": _sb(32, U16), "win": _sb(800, BF), "ex": _sb(384, BF), "offs": _sb(96, U16),
-    "hb": _sb(20, F32), "lh": _sb(32, U16), "ob": _sb(32, F32), "ob2": _sb(32, F32), "ob3": _sb(32, F32),
+    "th": _sb(160, BF), "kk": _sb(40, F32), "rr": _sb(128, F32), "xx": _sb(64, F32), "wo": _sb(32, U16),
+    "w2": _sb(32, U16), "win": _sb(DX, BF), "ex": _sb(384, BF), "offs": _sb(96, U16),
+    "ob": _sb(32, F32), "ob2": _sb(32, F32), "ob3": _sb(32, F32), "ob4": _sb(32, F32),
     "xt": _sb(4 * 8 * C, BF), "xq": _sb(XEND, X4), "xs": _sb(XEND, U8), "wq": _sb(NO, X4), "wsl": _sb(NO, U8),
-    "ot": _sb(4 * (2 * C + NO), BF), "oq": _sb(C + NO, X4), "osl": _sb(C + NO, U8),
+    "ot": _sb(4 * (3 * C + NO), BF), "oq": _sb(C + NO, X4), "osl": _sb(C + NO, U8),
     "ht": _sb(8 * 7 * C, BF), "hq": _sb(2 * 7 * C, X4), "hs": _sb(2 * 7 * C, U8), "zb": _sb(4 * 7 * C, BF),
-    "zq": _sb(ZEND, X4), "zs": _sb(ZEND, U8), "dd": _sb(2 * DW, BF), "dx": _sb(2 * DX, BF),
+    "zq": _sb(ZEND, X4), "zs": _sb(ZEND, U8), "dd": _sb(2 * DX, BF), "dx": _sb(2 * DX, BF),
     "yb": _sb(4 * NT, BF), "yq": _sb(NT, X4), "ys": _sb(NT, U8), "yo": _sb(NT, F32),
 }
-SEMAPHORES = ["cv", "cs", "ct", "cg", "ldu", "ldxa", "ldxb", "lda", "ldc", "ldv", "fa", "fb", "ra", "rb",
+SEMAPHORES = ["cv", "cs", "ct", "cg", "ldu", "ldxa", "ldxb", "lda", "ldc", "ldv", "fa", "fb", "ra", "rb", "rc",
               "sent", "sty", "sts"]
 
 
-def _pieces(T, topo, r):
+def _order(T, topo, r):
     mine = [k for k in range(N) if topo.die(T.cores[k]) == topo.die(T.cores[r])]
     other = [k for k in range(N) if k not in mine]
     h = mine.index(r) // 2 * 2
-    return (sorted([k for k in mine[h:h + 2] if k != r] + other[h:h + 2]),
-            sorted(mine[2 - h:4 - h] + other[2 - h:4 - h]))
+    own, far = mine[h:h + 2], other[h:h + 2]
+    return (own + far if own[0] == r else far + own) + other[2 - h:4 - h] + mine[2 - h:4 - h]
 
 
 def _runs(numbers):
@@ -123,8 +119,8 @@ def rank_program(g, core, T, topo):
     def scan(deps, out, d0, d1, init, op0, op1):
         return run("v", deps, lambda: V.tensor_tensor_scan(out, d0, d1, init, op0, op1))
 
-    def quant(deps, q, s, a):
-        return run("v", deps, lambda: V.quantize_mx(q, s, a))
+    def quant(deps, q, s, col, n, tile, at):
+        return run("v", deps, lambda: V.quantize_mx(q[:, col:col + n], s[:, col:col + n], tile[:, 4 * at:4 * (at + n)]))
 
     def ms(ap, c):
         return run("v", [], lambda: V.memset(ap, c))
@@ -132,19 +128,22 @@ def rank_program(g, core, T, topo):
     def act(deps, out, a, func, **kw):
         return run("s", deps, lambda: S.activation(out, a, func, **kw))
 
-    def mm(deps, out, wq, ws, xq, xs, start, stop):
-        return run("t", deps, lambda: P.matmul_mx(out, wq, ws, xq, xs, start, stop))
+    def mm(deps, b, wq, ws, w, q, s, col, n, start=True, stop=True):
+        return run("t", deps, lambda: P.matmul_mx(bank(b, n), wq[:, w:w + 128], ws[:, w:w + 128],
+                                                  q[:, col:col + n], s[:, col:col + n], start, stop))
 
     def iota(out, pattern, base, cm):
         return run("g", [], lambda: g.iota(out, pattern, base, cm, allow_small_or_imprecise_dtypes=True))
 
-    ra, rb = _pieces(T, topo, r)
-    order = ra + [r] + rb
+    order = _order(T, topo, r)
+    lead = order[0] == r
+    ra, rb = [d for d in order[:4] if d != r], order[4:]
+    a0, o0 = (C, 0) if lead else (0, NA)
 
-    ldu = dma(LOADQ[0], "ldu", T.ub[:], T.u[:])
-    ldxa = dma(LOADQ[1], "ldxa", T.xb[:, :4 * H], T.x[:, :4 * H])
-    ldxb = dma(LOADQ[2], "ldxb", T.xb[:, 4 * H:], T.x[:, 4 * H:])
-    dma("y", "lda", u8(T.aq[:]), T.ac[:], [ldxb])
+    ldu = dma("y", "ldu", T.ub[:], T.u[:])
+    ldxa = dma("y", "ldxa", T.xb[:, :4 * H], T.x[:, :4 * H])
+    ldxb = dma("y", "ldxb", T.xb[:, 4 * H:], T.x[:, 4 * H:])
+    dma("y", "lda", u8(T.aq[:]), T.ac[:])
     lda = dma("y", "lda", T.asc[:], T.ap[:])
     dma("y", "ldc", u8(T.cq[:]), T.cc[:])
     ldc = dma("y", "ldc", T.csc[:], T.cp[:])
@@ -157,12 +156,13 @@ def rank_program(g, core, T, topo):
             iota(T.k2[:, 32:64], [[0, 8], [1, 4]], 256, 0),
             iota(T.k2[:, 64:96], [[1, 32]], 0, 0),
             iota(T.k2[:, 96:112], [[4, 8], [64, 2]], 0, 0),
-            iota(T.k2[:, 112:128], [[4, 8], [-64, 2]], 66, 0)]
-    i_uniq = iota(T.uniq0[:], [[32, 10], [0, 2]], N * C - 193, 0)
-    i_jv = iota(T.jv[:], [[1, NT]], -64, 0)
+            iota(T.k2[:, 112:128], [[4, 8], [-64, 2]], 66, 0),
+            iota(T.k2[:, 128:160], [[2, 2], [4, 16]], 0, 0),
+            iota(T.k2[:, 160:192], [[16, 2], [0, 16]], 0, 0)]
+    i_uniq = iota(T.uniq0[:], [[32, 10], [0, 2]], FAR - 193, 0)
+    i_jv = iota(T.j0[:], [[32, 10], [1, 16]], -64, 0)
     i_cx0 = iota(T.cx0[:], [[0, 48], [-512, 4]], 0, 0)
     i_ff = iota(T.ff[:], [[-1, 516]], 3, 4)
-    m_dd = iota(T.dd[:, N * C::DW], [[0, 2]], 0, 0)
     m_ob = iota(T.ob[:], [[0, 32]], 0, 0)
 
     m_oht = ms(T.oht[:], 0.0)
@@ -172,19 +172,18 @@ def rank_program(g, core, T, topo):
     m_rr = ms(T.rr[:, 40:128], 0.0)
     m_kk = ms(T.kk[:], 0.0)
     m_g = ms(T.gg[:, 0:2], 0.0)
-    m_pad = ms(T.ot[:, 4 * 3 * C:], 0.0)
+    m_pad = ms(T.ot[:, 4 * 3 * C:4 * (2 * C + NO)], 0.0)
 
     c_base = act([c_k1], T.col[:, 0:1], T.k1[:, 0:1], F.Identity, scale=float(C), bias=-193.0)
     c_top = act([c_k1], T.col[:, 1:2], T.k1[:, 0:1], F.Identity, scale=float(C), bias=C + 1 - 193.0)
-    c_cr = act([i_thr], T.cr[:], T.thr[:, 0:80], F.Identity, scale=1e26, bias=1.21e28)
-    c_clip = act([c_top], T.clip[:], T.thr[:], F.Identity, scale=0.0, bias=T.col[:, 1:2])
 
-    q_u = quant([ldu], T.uq[:], T.us[:], T.ub[:])
+    q_u = quant([ldu], T.uq, T.us, 0, 128, T.ub, 0)
     p_uc = cp([q_u, c_uoff], u32(T.uq2[:]), u32(T.uq[:]).indirect(T.uoff[:]))
     p_us = act([q_u, c_uoff], T.us2[:], T.us[:].indirect(T.uoff[:]), F.Copy)
-    q_xa = quant([ldxa], T.sq[:, :H], T.ss[:, :H], T.xb[:, :4 * H])
-    s_a = mm([p_uc, p_us, q_xa], bank(0, H), T.uq2[:], T.us2[:], T.sq[:, :H], T.ss[:, :H], True, True)
-    c_k3 = tr(i_k2, T.k3[:], T.k2[:])
+    c_cr = act([i_thr], T.cr[:], T.thr[:, 0:80], F.Identity, scale=1e26, bias=1.21e28)
+    c_clip = act([c_top], T.clip[:], T.thr[:], F.Identity, scale=0.0, bias=T.col[:, 1:2])
+    q_xa = quant([ldxa], T.sq, T.ss, 0, H, T.xb, 0)
+    s_a = mm([p_uc, p_us, q_xa], 0, T.uq2, T.us2, 0, T.sq, T.ss, 0, H)
 
     W = H // 2
     half = lambda buf, k, step=1: buf[:, H * k:H * k + H:step]
@@ -198,10 +197,11 @@ def rank_program(g, core, T, topo):
     f_r0 = lambda k, e: tt([e], half(T.oht, k, 16), part(T.rm, k, 0, 8), part(T.sm, k, 0, 8), A.is_ge)
     f_t2 = lambda k, e: tr([e], half(T.oh, k), half(T.oht, k))
     f_t3 = lambda k, e: tr([e], half(T.valt, k), half(T.val, k))
+    q_xb = quant([ldxb], T.sq, T.ss, H, H, T.xb, H)
     t1a = f_t1(0, s_a)
-    q_xb = quant([ldxb], T.sq[:, H:], T.ss[:, H:], T.xb[:, 4 * H:])
-    s_b = mm([q_xb], bank(1, H), T.uq2[:], T.us2[:], T.sq[:, H:], T.ss[:, H:], True, True)
-    x_pl = [act([ldxa, ldxb], T.dx[:, N * C:DX], T.xb[:, 0::4], F.Copy)]
+    c_k3 = tr(i_k2, T.k3[:], T.k2[:])
+    s_b = mm([q_xb], 1, T.uq2, T.us2, 0, T.sq, T.ss, H, H)
+    x_pl = [act([ldxa, ldxb], T.dx[:, FAR:DX], T.xb[:, 0::4], F.Copy)]
     f_rm(0, t1a)
     sma = f_sm(0)
     t1b = f_t1(1, s_b)
@@ -213,7 +213,10 @@ def rank_program(g, core, T, topo):
     e_c = act([ngb], T.csel[:], rev(T.gg, 1, 161), F.Identity, scale=1024.0, bias=-768.0)
     c_uniq = act([i_uniq, c_k3], T.uniq[:], T.uniq0[:], F.Identity, scale=1.0, bias=T.k3[:, 64:65])
     c_cx = [act([i_cx0], T.cx[:, o:o + 192], T.cx0[:], F.Identity, scale=1.0, bias=T.k3[:, 0:1]) for o in (0, 192)]
-    x_pl.append(act([], T.dx[:, DX + N * C:2 * DX], T.xb[:, 1::4], F.Copy))
+    x_pl.append(act([], T.dx[:, DX + FAR:2 * DX], T.xb[:, 1::4], F.Copy))
+    c_h = act([], T.col[:, 2:3], T.k3[:, 160:161], F.Identity, scale=-1.0, bias=16.0)
+    c_jv = [act([i_jv], T.jv[:, :H], T.j0[:], F.Identity, bias=T.k3[:, 160:161]),
+            act([c_h], T.jv[:, H:], T.j0[:], F.Identity, bias=T.col[:, 2:3])]
     c_fa = act([i_ff], T.fa[:], T.ff[:], F.Abs)
     r0a = f_r0(0, sta)
     stb = f_st(1, ngb)
@@ -227,16 +230,23 @@ def rank_program(g, core, T, topo):
     t3b = f_t3(1, n_b)
     e_k = tt([e_th, c_uniq, m_kk], T.kk[:, 0::2], T.uniq[:], T.th[:, 0::8], A.subtract)
     e_sel = scan([t3b], rev(T.sel, 0, 160), T.csel[:], rev(T.valt, 0, NT, 2), 0.0, A.min, A.max)
-    c_offw = ts([c_k3], T.offw[:], T.c16[:, 0:3:2], T.k3[:, 96:97], A.add)
+    c_offo = cp([c_k3], T.offo[:], T.k3[:, 128:130])
     e_a = tt([e_sel], T.sel[:, 4::8], T.sel[:, 0::8], T.th[:, 0::8], A.is_gt)
     e_w = scan([e_a, e_k], rev(T.rr, 0, 40), rev(T.kk, 0, 40), rev(T.sel, 0, 160, 4), 0.0, A.mult, A.add)
     c_fe = act([c_fa], T.fe[:], T.fa[:], F.Relu, scale=-1.0, bias=1.0)
-    h_b = act([e_w], T.hb[:], T.rr[:, 1:40:2], F.Identity, scale=1000.0, bias=-192.0)
+    o_a = [act([e_w, m_ob], T.ob[:, 10 * p:10 * p + 10], T.rr[:, 2 * p:40:4], F.Abs, bias=192.5 - N * C) for p in range(2)]
+    x_no = [act([], T.dd[:, FAR:DX], T.xb[:, 0:NT], F.Identity, scale=0.0)]
+    o_r = act(o_a, T.ob2[:], T.ob[:], F.Relu, scale=-1.0, bias=N * C + 0.5)
+    x_no.append(act([], T.dd[:, DX + FAR:2 * DX], T.xb[:, 0:NT], F.Identity, scale=0.0))
+    o_s = act([o_r], T.ob3[:], T.ob2[:], F.Identity, bias=-1.0)
     e_t4 = [tr([e_w, m_rr], T.xx[:, 0:32], T.rr[:, 0:64:2]), tr([e_w], T.xx[:, 32:64], T.rr[:, 0:64:2])]
+    w_a = ts([c_offo], T.w2[:, 0:16], T.rr[:, 0:64].indirect(T.offo[:, 0:1]), 192.0, A.add)
     e_t5 = tr(e_t4, T.rr[:, 64:128:2], T.xx[:, 16:48])
-    lists = T.rr[:].indirect(T.offw[:])
-    e_wo = ts([e_t5, c_offw], T.wo[:], lists, 192.0, A.add)
-    e_sc = cp([e_wo, i_jv, m_win], T.win[:].indirect(T.wo[:, 0:20]), T.jv[:])
+    cp([w_a, m_win] + c_jv, T.win[:].indirect(T.w2[:, 0:10]), T.jv[:, :H])
+    w_b = ts([e_t5], T.w2[:, 16:32], T.rr[:, 64:128].indirect(T.offo[:, 0:1]), 192.0, A.add)
+    c_offw = ts([c_k3], T.offw[:], T.c16[:, 0:3:2], T.k3[:, 96:97], A.add)
+    e_sc = cp([w_b], T.win[:].indirect(T.w2[:, 16:26]), T.jv[:, H:])
+    e_wo = ts([c_offw], T.wo[:], T.rr[:].indirect(T.offw[:]), 192.0, A.add)
     e_ex = scan([e_sc] + c_cx, T.ex[:], T.cx[:], T.win[:, 0:N * C], 0.0, A.max, A.min)
     e_of = [ts([e_ex], T.offs[:], T.ex[:, 3::4], 4.0, A.mult, T.k3[:, 32:33], A.add)]
 
@@ -248,23 +258,24 @@ def rank_program(g, core, T, topo):
             evs.append(cp(e_of, out, src) if q == "v" else act(e_of, out, src, F.Copy))
         return evs
 
-    q_a = quant(gather("v", 0, GA) + gather("s", GA, 36), T.xq[:, 0:NA], T.xs[:, 0:NA], T.xt[:, 0:4 * NA])
-    go = gather("s", 36, 48)
+    ga = a0 // 4
+    gv = ga + (18 if lead else 20)
+    q_a = quant(gather("v", ga, gv) + gather("s", gv, ga + 36), T.xq, T.xs, a0, NA, T.xt, a0)
+    go = gather("s", o0 // 4, o0 // 4 + 12)
     gb = gather("s", 48 + GB, 96)
-    q_o = quant(go, T.wq[:], T.wsl[:], T.xt[:, 4 * (NA + C - NO):4 * (NA + C)])
+    keep = 0 if lead else NO - C
+    q_o = quant(go + [q_a], T.wq, T.wsl, 0, NO, T.xt, o0 - keep)
     gb += gather("v", 48, 48 + GB)
-    q_b = quant(gb, T.xq[:, NA + C:N * C], T.xs[:, NA + C:N * C], T.xt[:, 4 * (NA + C):4 * N * C])
+    q_b = quant(gb, T.xq, T.xs, 4 * C, NB, T.xt, 4 * C)
 
-    def send(deps, sem, q, s, moves, apart=0):
+    def send(deps, sem, q, s, moves):
         wait("g", deps)
         eng = topo.engines(core, T.cores[moves[0][0]])
         far = [m for m in moves if topo.die(T.cores[m[0]]) != topo.die(core)]
         near = [m for m in moves if m not in far]
-        total = 0
         for buf, flip in ((q, 0), (s, 1)):
-            es = eng[flip::2] if apart else eng
             trs = []
-            for some, lanes in ((far, es[1 - flip::2]), (near, es[flip::2])):
+            for some, lanes in ((far, eng[1 - flip::2]), (near, eng[flip::2])) if far and near else ((moves, eng),):
                 w = len(lanes) // len(some)
                 for k, (d, here, there) in enumerate(some):
                     rid, pid, _ = topo.addr(T.cores[d])
@@ -273,33 +284,23 @@ def rank_program(g, core, T, topo):
                         src, dst = u8(src), u8(dst)
                     trs.append(RemoteDMATransfer(dst_ids=[DstId(rid=rid, pnc=pid)], remote_sem=T.sem[sem], src=src, dst=dst,
                                                  dma_engine_mask=sum(1 << e for e in lanes[w * k:w * k + w])))
-            total += len(es)
             g.remote_dma_fused(trs, local_sem=T.sem["sent"])
-        count["sent"] = count.get("sent", 0) + total
-        return (sem, total)
+        count["sent"] = count.get("sent", 0) + 2 * len(eng)
+        return (sem, 2 * len(eng))
 
-    def there(d, piece, base):
-        return base + C * _pieces(T, topo, d)[piece].index(r)
+    def spot(d):
+        o = _order(T, topo, d)
+        return o.index(r), (NO - C if o[0] == d else 0)
 
-    got_a = send([q_a], "fa", T.xq, T.xs, [(d, C * order.index(d), there(d, 0, XINA)) for d in ra], APART)
-    got_b = send([q_b], "fb", T.xq, T.xs, [(d, C * order.index(d), there(d, 1, XINB)) for d in rb])
+    inx = lambda d: spot(d)[0] - (spot(d)[1] > 0)
+    got_a = send([q_a], "fa", T.xq, T.xs, [(d, C * order.index(d), XINA + C * inx(d)) for d in ra])
+    got_b = send([q_b], "fb", T.xq, T.xs, [(d, C * order.index(d), XINB + C * (spot(d)[0] - 4)) for d in rb])
 
     free = {b: [] for b in range(8)}
     free[0], free[1] = [t1a], [t1b]
-    q_e = []
 
-    def unpackers(lo, hi):
-        for b in range(lo, hi):
-            w = slice(128 * b, 128 * b + 128)
-            q_e.append(quant([c_fe], T.eq[:, w], T.es[:, w], T.fe[:, 3 - b:515 - b]))
-
-    def layer(wq, ws, i, base, q, s, col0, n, deps, start, stop):
-        prod = []
-        for b in range(4):
-            w = slice(512 * i + 128 * b, 512 * i + 128 * b + 128)
-            prod.append(mm(deps + free[base + b], bank(base + b, n), wq[:, w], ws[:, w],
-                           q[:, col0:col0 + n], s[:, col0:col0 + n], start, stop))
-        return prod
+    def layer(wq, ws, i, base, q, s, col, n, deps, start=True, stop=True):
+        return [mm(deps + free[base + b], base + b, wq, ws, 512 * i + 128 * b, q, s, col, n, start, stop) for b in range(4)]
 
     def leave(tile, at, m, base, prod, on, relu, o=0):
         evs = []
@@ -315,106 +316,95 @@ def rank_program(g, core, T, topo):
             evs.append(e)
         return evs
 
-    p0 = layer(T.aq, T.asc, 0, 0, T.wq, T.wsl, 0, NO, [q_o, lda], True, True)
-    p1 = layer(T.aq, T.asc, 1, 4, T.wq, T.wsl, 0, NO, [q_o, lda], True, True)
-    evs = leave(T.ot, C, C, 0, p0, ON[6], True, NO - C) + leave(T.ot, 2 * C, C, 4, p1, ON[7], True, NO - C)
-    h = quant(evs + [m_pad], T.oq[:], T.osl[:], T.ot[:, 4 * C:])
-    unpackers(0, E1)
-    layer(T.cq, T.csc, 0, 0, T.oq, T.osl, 0, NO, [h, ldc], True, False)
-    pc = layer(T.cq, T.csc, 1, 0, T.oq, T.osl, C, NO, [h], False, True)
-    evs = leave(T.ot, 0, C, 0, pc, ON[8], False)
-    z_o = quant(evs, T.zq[:, ZOWN:ZOWN + NO], T.zs[:, ZOWN:ZOWN + NO], T.ot[:, 0:4 * NO])
+    def unpacker(b):
+        return run("v", [c_fe], lambda: V.quantize_mx(T.eq[:, 128 * b:128 * b + 128], T.es[:, 128 * b:128 * b + 128],
+                                                      T.fe[:, 3 - b:515 - b]))
 
-    ja, jb = (0, XINA, NA, ZA), (NA, XINB, NB, ZB)
+    p0 = layer(T.aq, T.asc, 0, 0, T.wq, T.wsl, 0, NO, [q_o, lda])
+    p1 = layer(T.aq, T.asc, 1, 4, T.wq, T.wsl, 0, NO, [q_o, lda])
+    evs = leave(T.ot, C, C, 0, p0, "ssss", True, keep) + leave(T.ot, 2 * C, C, 4, p1, "svsv", True, keep)
+    h_o = quant(evs + [m_pad], T.oq, T.osl, 0, C + NO, T.ot, C)
+    q_e = [unpacker(b) for b in range(3)]
 
-    def la(job, i, base, got):
-        return layer(T.aq, T.asc, i, base, T.xq, T.xs, job[1], job[2], [got], True, True)
+    HA0, HA1, HB0, HB1 = 0, NA, 2 * NA, 2 * NA + NB
+    la = lambda i, base, col, n, got: layer(T.aq, T.asc, i, base, T.xq, T.xs, col, n, [got])
+    lc = lambda i, base, col, n, qh: layer(T.cq, T.csc, i, base, T.hq, T.hs, col, n, [qh, ldc], i == 0, i == 1)
+    q_h = lambda evs, col, n: quant(evs, T.hq, T.hs, col, n, T.ht, col)
+    pa0, pa1 = la(0, 4, XINA, NA, got_a), la(1, 0, XINA, NA, got_a)
+    ea0 = leave(T.ht, HA0, NA, 4, pa0, "svvs", True)
+    pb0 = la(0, 4, XINB, NB, got_b)
+    ea1 = leave(T.ht, HA1, NA, 0, pa1, "sssv", True)
+    ha0 = q_h(ea0, HA0, NA)
+    pb1 = la(1, 0, XINB, NB, got_b)
+    eb0 = leave(T.ht, HB0, NB, 4, pb0, "svsv", True)
+    ha1 = q_h(ea1, HA1, NA)
+    lc(0, 4, HA0, NA, ha0)
+    pa = lc(1, 4, HA1, NA, ha1)
+    eb1 = leave(T.ht, HB1, NB, 0, pb1, "svss", True)
+    hb0 = q_h(eb0, HB0, NB)
+    hb1 = q_h(eb1, HB1, NB)
+    lc(0, 0, HB0, NB, hb0)
+    pb = lc(1, 0, HB1, NB, hb1)
+    z_a = quant(leave(T.zb, 0, NA, 4, pa, "svss", False), T.zq, T.zs, ZA, NA, T.zb, 0)
+    back_a = send([z_a], "ra", T.zq, T.zs, [(s, ZA + C * k, spot(s)[1] + C * spot(s)[0]) for k, s in enumerate(ra)])
+    layer(T.cq, T.csc, 0, 4, T.oq, T.osl, 0, NO, [h_o], True, False)
+    pc = layer(T.cq, T.csc, 1, 4, T.oq, T.osl, C, NO, [h_o], False, True)
+    evs = leave(T.zb, NA, NB, 0, pb, "vsvs", False)
+    back = []
+    for n in range(2):
+        w0 = n * (NB - NO)
+        z = quant(evs, T.zq, T.zs, ZB + NO * n, NO, T.zb, NA + w0)
+        back.append(send([z], ("rb", "rc")[n], T.zq, T.zs,
+                         [(rb[k], ZB + NO * n + C * k - w0, ZIN[n] + C * (spot(rb[k])[0] % 2)) for k in (2 * n, 2 * n + 1)]))
 
-    def tile_h(job, i, base, prod, on):
-        c0, n = 2 * job[0] + job[2] * i, job[2]
-        evs = leave(T.ht, c0, n, base, prod, on, True)
-        return quant(evs, T.hq[:, c0:c0 + n], T.hs[:, c0:c0 + n], T.ht[:, 4 * c0:4 * (c0 + n)])
+    evs = leave(T.ot, 2 * C + NO if lead else 0, C, 4, pc, "ssss", False)
+    q_e.append(unpacker(3))
+    o_c = tr([o_s], T.ob4[:], T.ob3[:])
+    z_o = quant(evs, T.zq, T.zs, 0 if lead else NA, NO, T.ot, 3 * C if lead else 0)
+    for k in range(4):
+        dma("y", "sts", T.ol[2 * k:2 * k + 2, :], T.ob4[32 * k:32 * k + 20, :], [o_c, back[1]])
 
-    def lc(job, i, base, qh):
-        return layer(T.cq, T.csc, i, base, T.hq, T.hs, 2 * job[0] + job[2] * i, job[2], [qh], i == 0, i == 1)
-
-    def tile_z(job, base, prod, on):
-        at, col0, n, zcol = job
-        evs = leave(T.zb, at, n, base, prod, on, False)
-        return quant(evs, T.zq[:, zcol:zcol + n], T.zs[:, zcol:zcol + n], T.zb[:, 4 * at:4 * (at + n)])
-
-    p0, p1 = la(ja, 0, 4, got_a), la(ja, 1, 0, got_a)
-    ha0 = tile_h(ja, 0, 4, p0, ON[0])
-    p0 = la(jb, 0, 4, got_b)
-    ha1 = tile_h(ja, 1, 0, p1, ON[1])
-    p1 = la(jb, 1, 0, got_b)
-    hb0 = tile_h(jb, 0, 4, p0, ON[2])
-    lc(ja, 0, 4, ha0)
-    pa = lc(ja, 1, 4, ha1)
-    hb1 = tile_h(jb, 1, 0, p1, ON[3])
-    lc(jb, 0, 0, hb0)
-    pb = lc(jb, 1, 0, hb1)
-    z_a = tile_z(ja, 4, pa, ON[4])
-    back_a = send([z_a], "ra", T.zq, T.zs, [(s, ZA + C * k, there(s, 0, ZINA)) for k, s in enumerate(ra)])
-    z_b = tile_z(jb, 0, pb, ON[5])
-    back_b = send([z_b], "rb", T.zq, T.zs, [(s, ZB + C * k, there(s, 1, 0)) for k, s in enumerate(rb)])
-
-    l_h = ts([e_t5], T.lh[:], lists, 192.0, A.add, float(N * C), A.min)
-    o_a = [tt([h_b, m_ob], T.ob[:, 16 * p:16 * p + 10], T.rr[:, 2 * p:40:4], T.hb[:, p:20:2], A.subtract) for p in range(2)]
-    q_v = quant([ldv], T.vq[:], T.vs[:], T.vb[:])
-    o_b = tr(o_a, T.ob2[:], T.ob[:])
-    unpackers(E1, 4)
-    o_c = ts([o_b], T.ob3[:], T.ob2[:], -1.0, A.max)
-    for k in range(8):
-        dma("y", "sts", T.ol[k], T.ob3[16 * k:16 * k + 10, :], [o_c])
-
-    def unpack(ranks, col0, deps, base):
-        n = C * len(ranks)
-        prod = {b: mm(deps + q_e + free[base + b], bank(base + b, n), T.eq[:, 128 * b:128 * b + 128],
-                      T.es[:, 128 * b:128 * b + 128], T.zq[:, col0:col0 + n], T.zs[:, col0:col0 + n], True, True)
-                for b in (0, 2, 1, 3)}
+    def unpack(ranks, col, deps, base):
+        o = max(0, NO - C * len(ranks))
+        prod = {b: mm(deps + q_e + free[base + b], base + b, T.eq, T.es, 128 * b, T.zq, T.zs, col - o, C * len(ranks) + o)
+                for b in (2, 0, 1, 3)}
         done = []
         for b in range(4):
             evs = []
             for k, d, m in _runs(ranks):
-                src = bank(base + b, C * m, C * k)
+                src = bank(base + b, C * m, C * k + o)
                 if b < 2:
                     at = C * order.index(d)
                     evs.append(tt([prod[b]], T.dx[:, DX * b + C * d:DX * b + C * (d + m)], src,
                                   T.xt[:, 4 * at + b:4 * (at + C * m):4], A.add))
                 else:
-                    evs.append(act([prod[b]], T.dd[:, DW * (b - 2) + C * d:DW * (b - 2) + C * (d + m)], src, F.Copy))
+                    evs.append(act([prod[b]], T.dd[:, DX * (b - 2) + C * d:DX * (b - 2) + C * (d + m)], src, F.Copy))
             free[base + b] = evs[-1:]
             done.append(evs)
         return done
 
-    d_a = unpack(ra + [r], ZINA, [back_a, z_o], 4)
-    d_b = unpack(rb, 0, [back_b], 0)
+    d_a = unpack(order[:4], NO - C if lead else 0, [back_a, z_o], 4)
+    q_v = quant([ldv], T.vq, T.vs, 0, 128, T.vb, 0)
+    d_1 = unpack(rb[:2], ZIN[0], back[:1], 0)
+    d_2 = unpack(rb[2:], ZIN[1], back, 4)
+    got = [d_a[b] + d_1[b] + d_2[b] for b in range(4)]
 
-    def pick_s(b, lo, hi):
-        return act(d_a[b] + d_b[b] + x_pl + [e_wo], T.yb[:, 4 * lo + b:4 * hi:4],
-                   T.dx[:, DX * b:DX * (b + 1)].indirect(T.wo[:, lo // 16:hi // 16]), F.Copy)
+    def pick(b, lo, hi):
+        out, at = T.yb[:, 4 * lo + b:4 * hi:4], T.wo[:, lo // 16:hi // 16]
+        if b < 2:
+            return act(got[b] + x_pl + [e_wo], out, T.dx[:, DX * b:DX * (b + 1)].indirect(at), F.Copy)
+        return tt(got[b] + x_no, out, T.dd[:, DX * (b - 2):DX * (b - 1)].indirect(at), T.xb[:, 4 * lo + b:4 * hi:4], A.add)
 
-    def pick_v(b, lo, hi):
-        return tt(d_a[b] + d_b[b] + [l_h, m_dd], T.yb[:, 4 * lo + b:4 * hi:4],
-                  T.dd[:, DW * (b - 2):DW * (b - 2) + N * C + 1].indirect(T.lh[:, lo // 16:hi // 16]),
-                  T.xb[:, 4 * lo + b:4 * hi:4], A.add)
-
-    def q_run(evs, lo, hi):
-        return quant(evs, T.yq[:, lo:hi], T.ys[:, lo:hi], T.yb[:, 4 * lo:4 * hi])
-
-    e0 = [pick_s(0, 0, CUT), pick_s(1, 0, CUT), pick_v(2, 0, CUT), pick_v(3, 0, CUT)]
-    e1 = [pick_s(0, CUT, NT), pick_s(1, CUT, NT), pick_v(2, CUT, NT)]
-    q_y = [q_run(e0, 0, CUT)]
-    e1.append(pick_v(3, CUT, NT))
-    q_y.append(q_run(e1, CUT, NT))
-    for h, (lo, hi) in enumerate(((0, CUT), (CUT, NT))):
-        m = mm([q_y[h], q_v] + free[4 + h], bank(4 + h, hi - lo), T.vq[:], T.vs[:], T.yq[:, lo:hi], T.ys[:, lo:hi], True, True)
+    runs = ((0, H), (H, NT))
+    picks = [[pick(b, lo, hi) for b in range(4)] for lo, hi in runs]
+    q_y = [quant(picks[h], T.yq, T.ys, lo, hi - lo, T.yb, lo) for h, (lo, hi) in enumerate(runs)]
+    for h, (lo, hi) in enumerate(runs):
+        m = mm([q_y[h], q_v] + free[h], h, T.vq, T.vs, 0, T.yq, T.ys, lo, hi - lo)
         dma("y", "sts", T.oc[:, 4 * lo:4 * hi], u8(T.yq[:, lo:hi]), [q_y[h]])
         if h == 0:
-            c = act([m], T.yo[:, lo:hi], bank(4 + h, hi - lo), F.Copy)
+            c = act([m], T.yo[:, lo:hi], bank(h, hi - lo), F.Copy)
         else:
-            c = cp([m], T.yo[:, lo:hi], bank(4 + h, hi - lo))
+            c = cp([m], T.yo[:, lo:hi], bank(h, hi - lo))
             for k in range(4):
                 dma("sy"[k % 2], "sts", T.osc[4 * k:4 * k + 4, :], T.ys[32 * k:32 * k + 4, :], q_y)
         dma("s", "sty", T.y[:, lo:hi], T.yo[:, lo:hi], [c])

@@ -6,13 +6,19 @@ H = NT // 2
 NO = 128
 NA, NB = 3 * C, 4 * C
 XINB, XINA, XEND = N * C, N * C + NB, N * C + NB + NA
-ZIN = (NA + NO, NA + NO + 2 * C)
-ZB = NA + NO + NB
-ZA, ZEND = ZB + 2 * NO, ZB + 2 * NO + NA
+ZIN = (2 * NA, 2 * NA + 2 * C)
+ZE = 2 * NA + NB
+ZA, ZEND = ZE + NO, ZE + NO + NA
+SP = 16 * C
+MID = -3 * SP // 2
+LOW = NT - MID
 FAR = 2 * N * C
 DX = FAR + NT
-GB = 20
-X4, U8, BF, F32, U16 = "float8_e4m3fn_x4", "uint8", "bfloat16", "float32", "uint16"
+BIG = 2.0 ** 20
+CFG = dict(gv=20, gb=18, own0="svsv", own="sssv", cut=192, mid=1, oq="sysys", unp=(2, 0, 1, 3),
+           plan="qo gv x0 qb k5 x1 u hw u ht u hu u wo aA0 xA0svsv aA1 aB0 xA1vvsv hA0 aB1 xB0svsv hA1 xB1vsss cA0 cA1 "
+                "hB0 hB1 cD0 xA2vsss cD1 qv cE0 zA xD2svsv zD cE1 xE2svsv zE ot og uA u1 ol")
+X4, U8, BF, F16, F32, U16 = "float8_e4m3fn_x4", "uint8", "bfloat16", "float16", "float32", "uint16"
 
 
 def _sb(n, d):
@@ -25,23 +31,22 @@ SCRATCH = {
     "aq": _sb(1024, X4), "asc": _sb(1024, U8), "cq": _sb(1024, X4), "csc": _sb(1024, U8),
     "uq": _sb(128, X4), "us": _sb(128, U8), "uq2": _sb(128, X4), "us2": _sb(128, U8),
     "vq": _sb(128, X4), "vs": _sb(128, U8), "sq": _sb(NT, X4), "ss": _sb(NT, U8),
-    "k0": _sb(32, F32), "k1": _sb(32, F32), "k2": _sb(192, F32), "k3": _sb(192, F32), "col": _sb(8, F32),
-    "c16": _sb(8, F32), "uoff": _sb(8, U16), "uniq0": _sb(20, F32), "uniq": _sb(20, F32), "j0": _sb(H, BF),
-    "jv": _sb(NT, BF), "cx0": _sb(192, BF), "cx": _sb(384, BF), "thr": _sb(160, BF), "cr": _sb(80, F32),
-    "clip": _sb(H, BF), "offw": _sb(2, U16), "offo": _sb(2, U16), "ff": _sb(516, BF), "fa": _sb(516, BF),
-    "fe": _sb(516, BF), "eq": _sb(512, X4), "es": _sb(512, U8),
+    "zz": _sb(H, BF), "k0": _sb(32, F32), "k1": _sb(32, F32), "k2": _sb(256, F32), "k3": _sb(256, F32),
+    "col": _sb(8, F32), "c16": _sb(8, F32), "uoff": _sb(8, U16), "uniq0": _sb(20, F32), "j0": _sb(H, BF),
+    "jv": _sb(NT, BF), "cx0": _sb(96, BF), "cx1": _sb(96, BF), "cx2": _sb(96, BF), "cx": _sb(96, BF), "t1": _sb(160, BF),
+    "cr": _sb(80, F32), "dm": _sb(H, BF), "offw": _sb(2, U16), "offo": _sb(2, U16),
+    "ff": _sb(516, BF), "fe": _sb(516, BF), "eq": _sb(512, X4), "es": _sb(512, U8), "tab": _sb(DX, F32),
     "pt": _sb(NT, F32), "rm": _sb(160, F32), "sm": _sb(160, F32), "gg": _sb(162, BF), "oht": _sb(NT, BF),
-    "oh": _sb(NT, BF), "val": _sb(NT, BF), "valt": _sb(NT, BF), "csel": _sb(160, BF), "sel": _sb(160, BF),
-    "th": _sb(160, BF), "kk": _sb(40, F32), "rr": _sb(128, F32), "xx": _sb(64, F32), "wo": _sb(32, U16),
-    "w2": _sb(32, U16), "win": _sb(DX, BF), "ex": _sb(384, BF), "offs": _sb(96, U16),
-    "ob": _sb(32, F32), "ob2": _sb(32, F32), "ob3": _sb(32, F32), "ob4": _sb(32, F32),
+    "oh": _sb(NT, BF), "val": _sb(NT, F16), "valt": _sb(NT, F16), "csel": _sb(160, BF), "sel": _sb(512, F32),
+    "xx": _sb(32, F32), "w2": _sb(32, U16), "win": _sb(4 * SP, BF), "ex": _sb(N * C, BF), "offs": _sb(96, U16),
+    "h1": _sb(160, BF), "hs1": _sb(20, F32), "hc": _sb(20, F32), "ha": _sb(20, F32), "hz": _sb(40, F32), "kk": _sb(40, F32),
+    "rr": _sb(128, F32), "x2": _sb(64, F32), "wo": _sb(32, U16), "olb": _sb(NT, F32),
     "xt": _sb(4 * 8 * C, BF), "xq": _sb(XEND, X4), "xs": _sb(XEND, U8), "wq": _sb(NO, X4), "wsl": _sb(NO, U8),
-    "ot": _sb(4 * (3 * C + NO), BF), "oq": _sb(C + NO, X4), "osl": _sb(C + NO, U8),
-    "ht": _sb(8 * 7 * C, BF), "hq": _sb(2 * 7 * C, X4), "hs": _sb(2 * 7 * C, U8), "zb": _sb(4 * 7 * C, BF),
+    "ht": _sb(8 * N * C, BF), "hq": _sb(2 * N * C, X4), "hs": _sb(2 * N * C, U8), "zb": _sb(4 * N * C, BF),
     "zq": _sb(ZEND, X4), "zs": _sb(ZEND, U8), "dd": _sb(2 * DX, BF), "dx": _sb(2 * DX, BF),
     "yb": _sb(4 * NT, BF), "yq": _sb(NT, X4), "ys": _sb(NT, U8), "yo": _sb(NT, F32),
 }
-SEMAPHORES = ["cv", "cs", "ct", "cg", "ldu", "ldxa", "ldxb", "lda", "ldc", "ldv", "fa", "fb", "ra", "rb", "rc",
+SEMAPHORES = ["cv", "cs", "ct", "cg", "ldu", "ldxa", "ldxb", "lda", "ldc", "ldv", "fa", "fb", "ra", "rd", "rf",
               "sent", "sty", "sts"]
 
 
@@ -51,16 +56,6 @@ def _order(T, topo, r):
     h = mine.index(r) // 2 * 2
     own, far = mine[h:h + 2], other[h:h + 2]
     return (own + far if own[0] == r else far + own) + other[2 - h:4 - h] + mine[2 - h:4 - h]
-
-
-def _runs(numbers):
-    runs = []
-    for k, d in enumerate(numbers):
-        if runs and runs[-1][1] + runs[-1][2] == d:
-            runs[-1][2] += 1
-        else:
-            runs.append([k, d, 1])
-    return runs
 
 
 def rank_program(g, core, T, topo):
@@ -122,8 +117,8 @@ def rank_program(g, core, T, topo):
     def quant(deps, q, s, col, n, tile, at):
         return run("v", deps, lambda: V.quantize_mx(q[:, col:col + n], s[:, col:col + n], tile[:, 4 * at:4 * (at + n)]))
 
-    def ms(ap, c):
-        return run("v", [], lambda: V.memset(ap, c))
+    def ms(ap, c, deps=()):
+        return run("v", deps, lambda: V.memset(ap, c))
 
     def act(deps, out, a, func, **kw):
         return run("s", deps, lambda: S.activation(out, a, func, **kw))
@@ -132,13 +127,17 @@ def rank_program(g, core, T, topo):
         return run("t", deps, lambda: P.matmul_mx(bank(b, n), wq[:, w:w + 128], ws[:, w:w + 128],
                                                   q[:, col:col + n], s[:, col:col + n], start, stop))
 
-    def iota(out, pattern, base, cm):
+    def iota(out, pattern, base, cm=0):
         return run("g", [], lambda: g.iota(out, pattern, base, cm, allow_small_or_imprecise_dtypes=True))
+
+    def select(deps, out, in_, pattern, op, fill, base, cm):
+        return run("g", deps, lambda: g.affine_select(out, in_, pattern, op, fill, base, cm))
 
     order = _order(T, topo, r)
     lead = order[0] == r
     ra, rb = [d for d in order[:4] if d != r], order[4:]
     a0, o0 = (C, 0) if lead else (0, NA)
+    pairs = [d // 2 for d in order[::2]]
 
     ldu = dma("y", "ldu", T.ub[:], T.u[:])
     ldxa = dma("y", "ldxa", T.xb[:, :4 * H], T.x[:, :4 * H])
@@ -147,126 +146,134 @@ def rank_program(g, core, T, topo):
     lda = dma("y", "lda", T.asc[:], T.ap[:])
     dma("y", "ldc", u8(T.cq[:]), T.cc[:])
     ldc = dma("y", "ldc", T.csc[:], T.cp[:])
-    ldv = dma("y", "ldv", T.vb[:], T.v[:])
 
-    i_k0 = iota(T.k0[:], [[0, 2], [1, 8], [0, 2]], 0, 0)
-    i_c16 = iota(T.c16[:], [[16, 8]], 0, 0)
-    i_thr = iota(T.thr[:], [[0, 20], [C, 8]], C - 193, 0)
-    i_k2 = [iota(T.k2[:, 0:32], [[0, 2], [512, 4], [0, 4]], 256, 0),
-            iota(T.k2[:, 32:64], [[0, 8], [1, 4]], 256, 0),
-            iota(T.k2[:, 64:96], [[1, 32]], 0, 0),
-            iota(T.k2[:, 96:112], [[4, 8], [64, 2]], 0, 0),
-            iota(T.k2[:, 112:128], [[4, 8], [-64, 2]], 66, 0),
-            iota(T.k2[:, 128:160], [[2, 2], [4, 16]], 0, 0),
-            iota(T.k2[:, 160:192], [[16, 2], [0, 16]], 0, 0)]
-    i_uniq = iota(T.uniq0[:], [[32, 10], [0, 2]], FAR - 193, 0)
-    i_jv = iota(T.j0[:], [[32, 10], [1, 16]], -64, 0)
-    i_cx0 = iota(T.cx0[:], [[0, 48], [-512, 4]], 0, 0)
-    i_ff = iota(T.ff[:], [[-1, 516]], 3, 4)
-    m_ob = iota(T.ob[:], [[0, 32]], 0, 0)
+    i_k0 = iota(T.k0[:], [[0, 2], [1, 8], [0, 2]], 0)
+    i_c16 = iota(T.c16[:], [[16, 8]], 0)
+    i_k2 = [iota(T.k2[:, 0:32], [[0, 2], [2 * SP, 4], [-1, 4]], 2 * MID + 2),
+            iota(T.k2[:, 32:64], [[8, 2], [16, 16]], 0),
+            iota(T.k2[:, 64:96], [[16, 2], [0, 16]], 0),
+            iota(T.k2[:, 96:128], [[0, 2], [-1, 4], [0, 4]], 0),
+            iota(T.k2[:, 128:160], [[0, 8], [1, 4]], 256)]
+    i_jv = iota(T.j0[:], [[32, 10], [1, 16]], -64)
+    i_cx0 = iota(T.cx0[:], [[0, 24], [1, 4]], 0)
+    i_t1 = iota(T.t1[:], [[0, 20], [SP, 4], [0, 2]], MID)
+    i_k4 = iota(T.k2[:, 160:192], [[0, 32]], 4)
+    i_k5 = [iota(T.k2[:, 192:224], [[1, 32]], 0),
+            iota(T.k2[:, 224:240], [[4, 8], [64, 2]], 0),
+            iota(T.k2[:, 240:256], [[4, 8], [-64, 2]], 66)]
+    for s in (3, 2, 1):
+        i_k4 = select([i_k4], T.k2[:, 160:192], T.k2[:, 160:192], [[0, 2], [1, 4], [0, 4]], A.is_ge, 4.0 / BIG ** (4 - s), -s, 0)
+    i_uniq = iota(T.uniq0[:], [[32, 10], [0, 2]], FAR - C + 1)
 
-    m_oht = ms(T.oht[:], 0.0)
+    m_z = ms(T.zz[:], 0.0)
+    m_cr = ms(T.cr[:], 1e27)
     c_k1 = tr([i_k0], T.k1[:], T.k0[:])
-    m_win = ms(T.win[:, 0:N * C], 255.0)
-    c_uoff = ts([c_k1, i_c16], T.uoff[:], T.c16[:], T.k1[:, 0:1], A.add)
-    m_rr = ms(T.rr[:, 40:128], 0.0)
-    m_kk = ms(T.kk[:], 0.0)
     m_g = ms(T.gg[:, 0:2], 0.0)
-    m_pad = ms(T.ot[:, 4 * 3 * C:4 * (2 * C + NO)], 0.0)
+    c_uoff = ts([c_k1, i_c16], T.uoff[:], T.c16[:], T.k1[:, 0:1], A.add)
+    m_sel = ms(T.sel[:, 160:256:8], 0.0)
+    c_cr = ms(T.cr[:, 0::8], -1e27, [m_cr])
+    m_oht = ms(T.oht[:, 1::2], 0.0)
 
-    c_base = act([c_k1], T.col[:, 0:1], T.k1[:, 0:1], F.Identity, scale=float(C), bias=-193.0)
-    c_top = act([c_k1], T.col[:, 1:2], T.k1[:, 0:1], F.Identity, scale=float(C), bias=C + 1 - 193.0)
+    kept = lambda e: T.win[:, SP * e + NT - C + 1:SP * e + NT + C + 1]
+    c_one = act([c_k1], T.col[:, 0:1], T.k1[:, 0:1], F.Relu, scale=-1.0, bias=1.0)
+    m_win = [act([m_z], kept(0), T.zz[:, 0:2 * C], F.Copy)]
+    c_neg = act([c_one], T.col[:, 1:2], T.col[:, 0:1], F.Identity, scale=-1.0)
+    m_win.append(act([], kept(1), T.zz[:, 0:2 * C], F.Copy))
+    c_dm = act([c_neg], T.dm[:], T.zz[:], F.Identity, bias=T.col[:, 1:2])
 
     q_u = quant([ldu], T.uq, T.us, 0, 128, T.ub, 0)
     p_uc = cp([q_u, c_uoff], u32(T.uq2[:]), u32(T.uq[:]).indirect(T.uoff[:]))
     p_us = act([q_u, c_uoff], T.us2[:], T.us[:].indirect(T.uoff[:]), F.Copy)
-    c_cr = act([i_thr], T.cr[:], T.thr[:, 0:80], F.Identity, scale=1e26, bias=1.21e28)
-    c_clip = act([c_top], T.clip[:], T.thr[:], F.Identity, scale=0.0, bias=T.col[:, 1:2])
     q_xa = quant([ldxa], T.sq, T.ss, 0, H, T.xb, 0)
     s_a = mm([p_uc, p_us, q_xa], 0, T.uq2, T.us2, 0, T.sq, T.ss, 0, H)
+    c_k3 = tr(i_k2, T.k3[:, 0:160], T.k2[:, 0:160])
+    m_win += [act([], kept(e), T.zz[:, 0:2 * C], F.Copy) for e in (2, 3)]
+    c_base = act([c_k3], T.col[:, 4:5], T.k3[:, 0:1], F.Identity, scale=0.5)
+    c_h = act([], T.col[:, 2:3], T.k3[:, 64:65], F.Identity, scale=-1.0, bias=16.0)
+    c_t = act([], T.col[:, 3:4], T.k3[:, 128:129], F.Identity, bias=0.25)
+    c_x1 = act([i_cx0], T.cx1[:], T.cx0[:], F.Relu, bias=T.k3[:, 96:97])
+    c_jv = [act([i_jv], T.jv[:, :H], T.j0[:], F.Identity, bias=T.k3[:, 64:65])]
+    c_x2 = act([c_x1], T.cx2[:], T.cx1[:], F.Sign)
+    c_jv.append(act([c_h], rev(T.jv, H, NT), T.j0[:], F.Identity, bias=T.col[:, 2:3]))
 
     W = H // 2
-    half = lambda buf, k, step=1: buf[:, H * k:H * k + H:step]
+    half = lambda buf, k, o=0, step=1: buf[:, H * k + o:H * k + H:step]
     part = lambda buf, k, o=0, step=1: buf[:, W * k + o:W * k + W + o:step]
     f_t1 = lambda k, e: tr([e], half(T.pt, k), bank(k, H))
-    f_rm = lambda k, e: scan([e, c_cr], part(T.rm, k), T.cr[:], half(T.pt, k, 2), 0.0, A.min, A.max)
+    f_rm = lambda k, e: scan([e, c_cr], part(T.rm, k), T.cr[:], half(T.pt, k, 0, 2), 0.0, A.min, A.max)
     f_sm = lambda k: scan([], rev(T.sm, W * k, W * k + W), T.cr[:], rev(T.pt, H * k, H * k + H, 2), 0.0, A.min, A.max)
     f_ng = lambda k, e: tt([e, m_g], part(T.gg, k, 1), part(T.rm, k), part(T.sm, k), A.is_lt)
-    f_st = lambda k, e: scan([e, m_oht], rev(T.oht, H * k, H * k + H, 2), rev(T.gg, W * k, W * k + W),
-                             rev(T.gg, W * k + 1, W * k + W + 1), 0.0, A.max, A.subtract)
-    f_r0 = lambda k, e: tt([e], half(T.oht, k, 16), part(T.rm, k, 0, 8), part(T.sm, k, 0, 8), A.is_ge)
-    f_t2 = lambda k, e: tr([e], half(T.oh, k), half(T.oht, k))
+    f_dn = lambda k, e: tt([e], half(T.oht, k, 0, 4), part(T.gg, k, 1, 2), part(T.gg, k, 0, 2), A.subtract)
+    f_up = lambda k: tt([], half(T.oht, k, 2, 4), part(T.gg, k, 1, 2), part(T.gg, k, 2, 2), A.subtract)
+    f_cs = lambda k, e: act([e], part(T.csel, k), part(T.gg, k, 1), F.Identity, scale=4096.0, bias=-2048.0)
+    f_t2 = lambda k, e: tr([e, m_oht], half(T.oh, k), half(T.oht, k))
     f_t3 = lambda k, e: tr([e], half(T.valt, k), half(T.val, k))
+    f_sel = lambda k, es: scan(es, rev(T.sel, W * k, W * k + W), rev(T.csel, W * k, W * k + W),
+                               rev(T.valt, H * k, H * k + H, 2), 0.0, A.min, A.max)
     q_xb = quant([ldxb], T.sq, T.ss, H, H, T.xb, H)
     t1a = f_t1(0, s_a)
-    c_k3 = tr(i_k2, T.k3[:], T.k2[:])
     s_b = mm([q_xb], 1, T.uq2, T.us2, 0, T.sq, T.ss, H, H)
-    x_pl = [act([ldxa, ldxb], T.dx[:, FAR:DX], T.xb[:, 0::4], F.Copy)]
+    c_offo = cp([c_k3], T.offo[:], T.k3[:, 32:34])
     f_rm(0, t1a)
     sma = f_sm(0)
     t1b = f_t1(1, s_b)
     nga = f_ng(0, sma)
     f_rm(1, t1b)
     smb = f_sm(1)
-    sta = f_st(0, nga)
+    f_dn(0, nga)
+    upa = f_up(0)
     ngb = f_ng(1, smb)
-    e_c = act([ngb], T.csel[:], rev(T.gg, 1, 161), F.Identity, scale=1024.0, bias=-768.0)
-    c_uniq = act([i_uniq, c_k3], T.uniq[:], T.uniq0[:], F.Identity, scale=1.0, bias=T.k3[:, 64:65])
-    c_cx = [act([i_cx0], T.cx[:, o:o + 192], T.cx0[:], F.Identity, scale=1.0, bias=T.k3[:, 0:1]) for o in (0, 192)]
-    x_pl.append(act([], T.dx[:, DX + FAR:2 * DX], T.xb[:, 1::4], F.Copy))
-    c_h = act([], T.col[:, 2:3], T.k3[:, 160:161], F.Identity, scale=-1.0, bias=16.0)
-    c_jv = [act([i_jv], T.jv[:, :H], T.j0[:], F.Identity, bias=T.k3[:, 160:161]),
-            act([c_h], T.jv[:, H:], T.j0[:], F.Identity, bias=T.col[:, 2:3])]
-    c_fa = act([i_ff], T.fa[:], T.ff[:], F.Abs)
-    r0a = f_r0(0, sta)
-    stb = f_st(1, ngb)
-    t2a = f_t2(0, r0a)
-    r0b = f_r0(1, stb)
-    n_a = scan([t2a, c_base, c_clip], half(T.val, 0), half(T.oh, 0), T.clip[:], T.col[:, 0:1], A.add, A.min)
-    t2b = f_t2(1, r0b)
-    f_t3(0, n_a)
-    n_b = scan([t2b], half(T.val, 1), half(T.oh, 1), T.clip[:], T.val[:, H - 1:H], A.add, A.min)
-    e_th = scan([e_c, i_thr], rev(T.th, 0, 160), T.csel[:], rev(T.thr, 0, 160), 0.0, A.min, A.max)
+    csa = f_cs(0, nga)
+    c_cx = act([c_x2], T.cx[:], T.cx2[:], F.Identity, scale=BIG)
+    csb = f_cs(1, ngb)
+    c_ff = act([ldxa, ldxb], T.ff[:], T.xb[:, 0:516], F.Identity, scale=0.0, bias=1.0)
+    c_fe = select([c_ff], T.fe[:], T.ff[:], [[-1, 516]], A.is_equal, 0.0, 3, 4)
+    x_pl = [act([], T.dx[:, DX * b + FAR:DX * (b + 1)], T.xb[:, b::4], F.Copy) for b in range(2)]
+    m_rr = act([], T.rr[:, 40:64], T.zz[:, 0:24], F.Copy)
+    m_kk = act([], T.kk[:, 1::2], T.zz[:, 0:20], F.Identity, bias=-1e6)
+    t2a = f_t2(0, upa)
+    f_dn(1, ngb)
+    upb = f_up(1)
+    n_a = scan([t2a, c_base, c_dm], half(T.val, 0), half(T.oh, 0), T.dm[:], T.col[:, 4:5], A.add, A.add)
+    t2b = f_t2(1, upb)
+    t3a = f_t3(0, n_a)
+    n_b = scan([t2b], half(T.val, 1), half(T.oh, 1), T.dm[:], T.val[:, H - 1:H], A.add, A.add)
+    f_sel(0, [t3a, csa])
     t3b = f_t3(1, n_b)
-    e_k = tt([e_th, c_uniq, m_kk], T.kk[:, 0::2], T.uniq[:], T.th[:, 0::8], A.subtract)
-    e_sel = scan([t3b], rev(T.sel, 0, 160), T.csel[:], rev(T.valt, 0, NT, 2), 0.0, A.min, A.max)
-    c_offo = cp([c_k3], T.offo[:], T.k3[:, 128:130])
-    e_a = tt([e_sel], T.sel[:, 4::8], T.sel[:, 0::8], T.th[:, 0::8], A.is_gt)
-    e_w = scan([e_a, e_k], rev(T.rr, 0, 40), rev(T.kk, 0, 40), rev(T.sel, 0, 160, 4), 0.0, A.mult, A.add)
-    c_fe = act([c_fa], T.fe[:], T.fa[:], F.Relu, scale=-1.0, bias=1.0)
-    o_a = [act([e_w, m_ob], T.ob[:, 10 * p:10 * p + 10], T.rr[:, 2 * p:40:4], F.Abs, bias=192.5 - N * C) for p in range(2)]
-    x_no = [act([], T.dd[:, FAR:DX], T.xb[:, 0:NT], F.Identity, scale=0.0)]
-    o_r = act(o_a, T.ob2[:], T.ob[:], F.Relu, scale=-1.0, bias=N * C + 0.5)
-    x_no.append(act([], T.dd[:, DX + FAR:2 * DX], T.xb[:, 0:NT], F.Identity, scale=0.0))
-    o_s = act([o_r], T.ob3[:], T.ob2[:], F.Identity, bias=-1.0)
-    e_t4 = [tr([e_w, m_rr], T.xx[:, 0:32], T.rr[:, 0:64:2]), tr([e_w], T.xx[:, 32:64], T.rr[:, 0:64:2])]
-    w_a = ts([c_offo], T.w2[:, 0:16], T.rr[:, 0:64].indirect(T.offo[:, 0:1]), 192.0, A.add)
-    e_t5 = tr(e_t4, T.rr[:, 64:128:2], T.xx[:, 16:48])
-    cp([w_a, m_win] + c_jv, T.win[:].indirect(T.w2[:, 0:10]), T.jv[:, :H])
-    w_b = ts([e_t5], T.w2[:, 16:32], T.rr[:, 64:128].indirect(T.offo[:, 0:1]), 192.0, A.add)
-    c_offw = ts([c_k3], T.offw[:], T.c16[:, 0:3:2], T.k3[:, 96:97], A.add)
-    e_sc = cp([w_b], T.win[:].indirect(T.w2[:, 16:26]), T.jv[:, H:])
-    e_wo = ts([c_offw], T.wo[:], T.rr[:].indirect(T.offw[:]), 192.0, A.add)
-    e_ex = scan([e_sc] + c_cx, T.ex[:], T.cx[:], T.win[:, 0:N * C], 0.0, A.max, A.min)
-    e_of = [ts([e_ex], T.offs[:], T.ex[:, 3::4], 4.0, A.mult, T.k3[:, 32:33], A.add)]
+    h_1 = scan([i_t1, csb], rev(T.h1, 0, H), rev(T.csel, 0, H), rev(T.t1, 0, H), 0.0, A.min, A.max)
+    e_sel = f_sel(1, [t3b])
+    e_t4 = tr([e_sel, m_sel], T.xx[:], T.sel[:, 0:256:8])
+    w_a = ts([c_offo], T.w2[:, 0:16], T.sel[:, 0:256].indirect(T.offo[:, 0:1]), float(LOW), A.add)
+    e_t5 = tr([e_t4], T.sel[:, 256:512:8], rev(T.xx, 0, 32))
+    cp([w_a] + m_win + c_jv, T.win[:].indirect(T.w2[:, 0:10]), T.jv[:, :H])
+    w_b = ts([e_t5], rev(T.w2, 16, 32), T.sel[:, 256:512].indirect(T.offo[:, 0:1]), float(LOW), A.add)
+    c_k4 = tr([i_k4], T.k3[:, 160:192], T.k2[:, 160:192])
+    h_c = tt([h_1], T.hc[:], T.sel[:, 0:H:8], T.h1[:, 0::8], A.subtract)
+    h_s = act([h_1], T.hs1[:], T.h1[:, 0::8], F.Identity, scale=2.0 * C / SP, bias=-2.0 * C * MID / SP)
+    h_a = act([h_c], T.ha[:], T.hc[:], F.Abs, bias=-0.5)
+    h_z = act([h_a], T.hz[:, 1::2], T.ha[:], F.Identity, scale=4096.0, bias=-4096.0 * C)
+    e_sc = cp([w_b], T.win[:].indirect(T.w2[:, 22:32]), T.jv[:, H:])
+    h_0 = tt([h_c, h_s], T.hz[:, 0::2], T.hc[:], T.hs1[:], A.add)
 
-    def gather(q, lo, hi):
-        evs = []
-        for k, o, n in _runs([6 * order[k // 12] + k % 12 // 2 for k in range(lo, hi, 2)]):
-            out = T.xt[:, 16 * lo + 32 * k:16 * lo + 32 * (k + n)]
-            src = T.xb[:].indirect(T.offs[:, 2 * o:2 * (o + n)])
-            evs.append(cp(e_of, out, src) if q == "v" else act(e_of, out, src, F.Copy))
-        return evs
+    f_ex = lambda n: scan([e_sc, c_cx], T.ex[:, 2 * C * n:2 * C * (n + 1)], T.cx[:], kept(pairs[n]), 0.0, A.mult, A.add)
+    f_of = lambda k, evs: ts(evs + [c_t, c_k4], T.offs[:, 24 * k:24 * k + 48], T.ex[:, 2 * C * k + 3:2 * C * (k + 2):4],
+                             T.k3[:, 160:161], A.mult, T.col[:, 3:4], A.add)
 
+    def gather(q, lo, hi, dep):
+        out, src = T.xt[:, 16 * lo:16 * hi], T.xb[:].indirect(T.offs[:, lo:hi])
+        return cp([dep], out, src) if q == "v" else act([dep], out, src, F.Copy)
+
+    ex = [f_ex(n) for n in range(3)]
+    of_a = f_of(0, ex[:2])
+    ex.append(f_ex(3))
     ga = a0 // 4
-    gv = ga + (18 if lead else 20)
-    q_a = quant(gather("v", ga, gv) + gather("s", gv, ga + 36), T.xq, T.xs, a0, NA, T.xt, a0)
-    go = gather("s", o0 // 4, o0 // 4 + 12)
-    gb = gather("s", 48 + GB, 96)
     keep = 0 if lead else NO - C
-    q_o = quant(go + [q_a], T.wq, T.wsl, 0, NO, T.xt, o0 - keep)
-    gb += gather("v", 48, 48 + GB)
-    q_b = quant(gb, T.xq, T.xs, 4 * C, NB, T.xt, 4 * C)
+    gv = ga + CFG["gv"]
+    evs = [gather("v", ga, gv, of_a), gather("s", gv, ga + 36, of_a)]
+    of_b = f_of(2, ex[2:])
+    q_a = quant(evs, T.xq, T.xs, a0, NA, T.xt, a0)
+    go = gather("s", o0 // 4, o0 // 4 + 12, of_a)
+    gb = [gather("s", 48 + CFG["gb"], 96, of_b)]
 
     def send(deps, sem, q, s, moves):
         wait("g", deps)
@@ -290,11 +297,9 @@ def rank_program(g, core, T, topo):
 
     def spot(d):
         o = _order(T, topo, d)
-        return o.index(r), (NO - C if o[0] == d else 0)
+        return o.index(r), int(o[0] == d)
 
-    inx = lambda d: spot(d)[0] - (spot(d)[1] > 0)
-    got_a = send([q_a], "fa", T.xq, T.xs, [(d, C * order.index(d), XINA + C * inx(d)) for d in ra])
-    got_b = send([q_b], "fb", T.xq, T.xs, [(d, C * order.index(d), XINB + C * (spot(d)[0] - 4)) for d in rb])
+    got_a = send([q_a], "fa", T.xq, T.xs, [(d, C * order.index(d), XINA + C * (spot(d)[0] - spot(d)[1])) for d in ra])
 
     free = {b: [] for b in range(8)}
     free[0], free[1] = [t1a], [t1b]
@@ -316,97 +321,134 @@ def rank_program(g, core, T, topo):
             evs.append(e)
         return evs
 
-    def unpacker(b):
-        return run("v", [c_fe], lambda: V.quantize_mx(T.eq[:, 128 * b:128 * b + 128], T.es[:, 128 * b:128 * b + 128],
-                                                      T.fe[:, 3 - b:515 - b]))
+    q_e = []
 
-    p0 = layer(T.aq, T.asc, 0, 0, T.wq, T.wsl, 0, NO, [q_o, lda])
-    p1 = layer(T.aq, T.asc, 1, 4, T.wq, T.wsl, 0, NO, [q_o, lda])
-    evs = leave(T.ot, C, C, 0, p0, "ssss", True, keep) + leave(T.ot, 2 * C, C, 4, p1, "svsv", True, keep)
-    h_o = quant(evs + [m_pad], T.oq, T.osl, 0, C + NO, T.ot, C)
-    q_e = [unpacker(b) for b in range(3)]
-
-    HA0, HA1, HB0, HB1 = 0, NA, 2 * NA, 2 * NA + NB
-    la = lambda i, base, col, n, got: layer(T.aq, T.asc, i, base, T.xq, T.xs, col, n, [got])
-    lc = lambda i, base, col, n, qh: layer(T.cq, T.csc, i, base, T.hq, T.hs, col, n, [qh, ldc], i == 0, i == 1)
-    q_h = lambda evs, col, n: quant(evs, T.hq, T.hs, col, n, T.ht, col)
-    pa0, pa1 = la(0, 4, XINA, NA, got_a), la(1, 0, XINA, NA, got_a)
-    ea0 = leave(T.ht, HA0, NA, 4, pa0, "svvs", True)
-    pb0 = la(0, 4, XINB, NB, got_b)
-    ea1 = leave(T.ht, HA1, NA, 0, pa1, "sssv", True)
-    ha0 = q_h(ea0, HA0, NA)
-    pb1 = la(1, 0, XINB, NB, got_b)
-    eb0 = leave(T.ht, HB0, NB, 4, pb0, "svsv", True)
-    ha1 = q_h(ea1, HA1, NA)
-    lc(0, 4, HA0, NA, ha0)
-    pa = lc(1, 4, HA1, NA, ha1)
-    eb1 = leave(T.ht, HB1, NB, 0, pb1, "svss", True)
-    hb0 = q_h(eb0, HB0, NB)
-    hb1 = q_h(eb1, HB1, NB)
-    lc(0, 0, HB0, NB, hb0)
-    pb = lc(1, 0, HB1, NB, hb1)
-    z_a = quant(leave(T.zb, 0, NA, 4, pa, "svss", False), T.zq, T.zs, ZA, NA, T.zb, 0)
-    back_a = send([z_a], "ra", T.zq, T.zs, [(s, ZA + C * k, spot(s)[1] + C * spot(s)[0]) for k, s in enumerate(ra)])
-    layer(T.cq, T.csc, 0, 4, T.oq, T.osl, 0, NO, [h_o], True, False)
-    pc = layer(T.cq, T.csc, 1, 4, T.oq, T.osl, C, NO, [h_o], False, True)
-    evs = leave(T.zb, NA, NB, 0, pb, "vsvs", False)
-    back = []
-    for n in range(2):
-        w0 = n * (NB - NO)
-        z = quant(evs, T.zq, T.zs, ZB + NO * n, NO, T.zb, NA + w0)
-        back.append(send([z], ("rb", "rc")[n], T.zq, T.zs,
-                         [(rb[k], ZB + NO * n + C * k - w0, ZIN[n] + C * (spot(rb[k])[0] % 2)) for k in (2 * n, 2 * n + 1)]))
-
-    evs = leave(T.ot, 2 * C + NO if lead else 0, C, 4, pc, "ssss", False)
-    q_e.append(unpacker(3))
-    o_c = tr([o_s], T.ob4[:], T.ob3[:])
-    z_o = quant(evs, T.zq, T.zs, 0 if lead else NA, NO, T.ot, 3 * C if lead else 0)
-    for k in range(4):
-        dma("y", "sts", T.ol[2 * k:2 * k + 2, :], T.ob4[32 * k:32 * k + 20, :], [o_c, back[1]])
-
-    def unpack(ranks, col, deps, base):
-        o = max(0, NO - C * len(ranks))
-        prod = {b: mm(deps + q_e + free[base + b], base + b, T.eq, T.es, 128 * b, T.zq, T.zs, col - o, C * len(ranks) + o)
-                for b in (2, 0, 1, 3)}
-        done = []
-        for b in range(4):
-            evs = []
-            for k, d, m in _runs(ranks):
-                src = bank(base + b, C * m, C * k + o)
+    def unpack(k0, k1, col, deps, base):
+        m = 2 * C * (k1 - k0)
+        o = max(0, NO - m)
+        prod = {b: mm(deps + q_e + free[base + b], base + b, T.eq, T.es, 128 * b, T.zq, T.zs, col - o, m + o) for b in CFG["unp"]}
+        done = {}
+        for b in CFG["unp"]:
+            for k in range(k0, k1):
+                src, at, to = bank(base + b, 2 * C, 2 * C * (k - k0) + o), 2 * C * k, 2 * C * pairs[k]
                 if b < 2:
-                    at = C * order.index(d)
-                    evs.append(tt([prod[b]], T.dx[:, DX * b + C * d:DX * b + C * (d + m)], src,
-                                  T.xt[:, 4 * at + b:4 * (at + C * m):4], A.add))
+                    e = tt([prod[b]], T.dx[:, DX * b + to:DX * b + to + 2 * C], src, T.xt[:, 4 * at + b:4 * (at + 2 * C):4], A.add)
                 else:
-                    evs.append(act([prod[b]], T.dd[:, DX * (b - 2) + C * d:DX * (b - 2) + C * (d + m)], src, F.Copy))
-            free[base + b] = evs[-1:]
-            done.append(evs)
+                    e = act([prod[b]], T.dd[:, DX * (b - 2) + to:DX * (b - 2) + to + 2 * C], src, F.Copy)
+            free[base + b] = [e]
+            done[b] = e
         return done
 
-    d_a = unpack(order[:4], NO - C if lead else 0, [back_a, z_o], 4)
-    q_v = quant([ldv], T.vq, T.vs, 0, 128, T.vb, 0)
-    d_1 = unpack(rb[:2], ZIN[0], back[:1], 0)
-    d_2 = unpack(rb[2:], ZIN[1], back, 4)
-    got = [d_a[b] + d_1[b] + d_2[b] for b in range(4)]
+    NW = NB + C
+    hb = (2 * NA, 2 * NA + NW)
+    cb, co = (0, NB) if lead else (C, 0)
+    cd, ce, oe = (2 * C, 0, 0) if lead else (0, NW - NO, NO - 2 * C)
+    zd = 0 if lead else NA
+    home = lambda k: ZIN[k // 2] + C * (spot(rb[k])[0] % 2)
+    prod, left, hq, back, base, turn = {}, {}, {}, {}, {}, 4
+    for step in CFG["plan"].split():
+        kind, p = step[0], step[1:2]
+        i = int(step[2]) if len(step) > 2 else 0
+        if step == "qo":
+            q_o = quant([go, q_a], T.wq, T.wsl, 0, NO, T.xt, o0 - keep)
+            po = [layer(T.aq, T.asc, k, 4 * k, T.wq, T.wsl, 0, NO, [q_o, lda]) for k in range(2)]
+        elif step == "gv":
+            gb.append(gather("v", 48, 48 + CFG["gb"], of_b))
+        elif step == "qb":
+            q_b = quant(gb, T.xq, T.xs, 4 * C, NB, T.xt, 4 * C)
+            got_b = send([q_b], "fb", T.xq, T.xs,
+                         [(d, C * order.index(d), XINB + C * ((spot(d)[0] + 2 * spot(d)[1]) % 4)) for d in rb])
+            i_tab = [iota(T.tab[:, 0:N * C], [[1, N * C]], 0), iota(T.tab[:, FAR:DX], [[0, NT]], -1)]
+            x_no = [iota(T.dd[:, DX * b + FAR:DX * (b + 1)], [[0, NT]], 0) for b in range(2)]
+            ldv = dma("y", "ldv", T.vb[:], T.v[:], [got_b])
+        elif step in ("x0", "x1"):
+            k = int(p)
+            left["o", k] = leave(T.ht, hb[k] + co, C, 4 * k, po[k], CFG["own" if k else "own0"], True, keep)
+        elif step == "k5":
+            c_k5 = tr(i_k5, T.k3[:, 192:256], T.k2[:, 192:256])
+            c_uniq = act([i_uniq, c_k5], T.kk[:, 0::2], T.uniq0[:], F.Identity, bias=T.k3[:, 192:193])
+        elif step == "hw":
+            c_offw = ts([c_k5], T.offw[:], T.c16[:, 0:3:2], T.k3[:, 224:225], A.add)
+            h_w = scan([h_0, h_z, m_kk, c_uniq], rev(T.rr, 0, 40), rev(T.kk, 0, 40), rev(T.hz, 0, 40), 0.0, A.min, A.max)
+        elif step == "ht":
+            h_t = [tr([h_w, m_rr], T.x2[:, o:o + 32], T.rr[:, 0:64:2]) for o in (0, 32)]
+        elif step == "hu":
+            h_u = tr(h_t, T.rr[:, 64:128:2], T.x2[:, 16:48])
+        elif step == "wo":
+            e_wo = ts([h_u, c_offw], T.wo[:], T.rr[:].indirect(T.offw[:]), C - 1.0, A.add)
+        elif step == "u":
+            b = len(q_e)
+            q_e.append(run("v", [c_fe], lambda: V.quantize_mx(T.eq[:, 128 * b:128 * b + 128], T.es[:, 128 * b:128 * b + 128],
+                                                              T.fe[:, 3 - b:515 - b])))
+        elif step == "ot":
+            c_tab = [act(i_tab[:1], T.tab[:, C * d:C * d + C], T.tab[:, C * d:C * d + C], F.Abs, bias=1.0 - C * (2 * d + 1))
+                     for d in range(0, N, 2)]
+        elif step == "og":
+            o_g = act([e_wo] + c_tab + i_tab, T.olb[:], T.tab[:].indirect(T.wo[:, 0:20]), F.Copy)
+        elif step == "ol":
+            dma("y", "sts", T.ol[:], T.olb[0:128:16, :], [o_g, back["E"]])
+        elif step == "qv":
+            q_v = quant([ldv], T.vq, T.vs, 0, 128, T.vb, 0)
+        elif step == "uA":
+            d_a = unpack(0, 2, 2 * C if lead else 0, [back["A"], z_d], turn)
+        elif step == "u1":
+            d_1 = unpack(2, 3, ZIN[0], [back["D"]], 4 - turn)
+        elif kind == "a":
+            base[p, i] = turn
+            turn = 4 - turn
+            col, n, got = (XINA, NA, got_a) if p == "A" else (XINB, NB, got_b)
+            prod[p, i] = layer(T.aq, T.asc, i, base[p, i], T.xq, T.xs, col, n, [got])
+        elif kind == "x" and i < 2:
+            at, n = (NA * i, NA) if p == "A" else (hb[i] + cb, NB)
+            left[p, i] = leave(T.ht, at, n, base[p, i], prod[p, i], step[3:], True)
+        elif kind == "x":
+            at, n, o = {"A": (0, NA, 0), "D": (NA + cd, NA, 0), "E": (NA + ce + oe, 2 * C, oe)}[p]
+            left[p, i] = leave(T.zb, at, n, base[p, i], prod[p, i], step[3:], False, o)
+        elif kind == "h":
+            at, n, more = (NA * i, NA, []) if p == "A" else (hb[i], NW, left["o", i])
+            hq[p, i] = quant(left[p, i] + more, T.hq, T.hs, at, n, T.ht, at)
+        elif kind == "c":
+            if i == 0:
+                base[p, 2] = turn
+                turn = 4 - turn
+            col, n = {"A": (NA * i, NA), "D": (hb[i] + cd, NA), "E": (hb[i] + ce, NO)}[p]
+            prod[p, 2] = layer(T.cq, T.csc, i, base[p, 2], T.hq, T.hs, col, n, [hq["A" if p == "A" else "B", i], ldc], i == 0, i == 1)
+        elif p == "A":
+            back[p] = send([quant(left[p, 2], T.zq, T.zs, ZA, NA, T.zb, 0)], "ra", T.zq, T.zs,
+                           [(s, ZA + C * k, C * (spot(s)[0] + 2 * spot(s)[1])) for k, s in enumerate(ra)])
+        elif p == "D":
+            z_d = quant(left[p, 2], T.zq, T.zs, zd, NA, T.zb, NA + cd)
+            back[p] = send([z_d], "rd", T.zq, T.zs, [(rb[k], zd + cb + C * k, home(k)) for k in (0, 1)])
+        else:
+            z = quant(left[p, 2] + left["D", 2], T.zq, T.zs, ZE, NO, T.zb, NA + ce)
+            back[p] = send([z], "rf", T.zq, T.zs, [(rb[k], ZE + oe + C * (k - 2), home(k)) for k in (2, 3)])
+
+    d_2 = unpack(3, 4, ZIN[1], [back["D"], back["E"]], turn)
+    yb = 4 - turn
 
     def pick(b, lo, hi):
         out, at = T.yb[:, 4 * lo + b:4 * hi:4], T.wo[:, lo // 16:hi // 16]
+        deps = [d_a[b], d_1[b], d_2[b], e_wo]
         if b < 2:
-            return act(got[b] + x_pl + [e_wo], out, T.dx[:, DX * b:DX * (b + 1)].indirect(at), F.Copy)
-        return tt(got[b] + x_no, out, T.dd[:, DX * (b - 2):DX * (b - 1)].indirect(at), T.xb[:, 4 * lo + b:4 * hi:4], A.add)
+            return act(deps + x_pl, out, T.dx[:, DX * b:DX * (b + 1)].indirect(at), F.Copy)
+        return tt(deps + x_no, out, T.dd[:, DX * (b - 2):DX * (b - 1)].indirect(at), T.xb[:, 4 * lo + b:4 * hi:4], A.add)
 
-    runs = ((0, H), (H, NT))
-    picks = [[pick(b, lo, hi) for b in range(4)] for lo, hi in runs]
-    q_y = [quant(picks[h], T.yq, T.ys, lo, hi - lo, T.yb, lo) for h, (lo, hi) in enumerate(runs)]
-    for h, (lo, hi) in enumerate(runs):
-        m = mm([q_y[h], q_v] + free[h], h, T.vq, T.vs, 0, T.yq, T.ys, lo, hi - lo)
-        dma("y", "sts", T.oc[:, 4 * lo:4 * hi], u8(T.yq[:, lo:hi]), [q_y[h]])
-        if h == 0:
-            c = act([m], T.yo[:, lo:hi], bank(h, hi - lo), F.Copy)
-        else:
-            c = cp([m], T.yo[:, lo:hi], bank(h, hi - lo))
-            for k in range(4):
-                dma("sy"[k % 2], "sts", T.osc[4 * k:4 * k + 4, :], T.ys[32 * k:32 * k + 4, :], q_y)
-        dma("s", "sty", T.y[:, lo:hi], T.yo[:, lo:hi], [c])
+    cut = CFG["cut"]
+    runs = ((0, cut), (cut, NT))
+    picks = [[pick(b, 0, cut) for b in range(4)]]
+    q_0 = lambda: quant(picks[0], T.yq, T.ys, 0, cut, T.yb, 0)
+    picks.append([pick(b, cut, NT) for b in (0, 2)])
+    q_y = [q_0()] if CFG["mid"] else []
+    picks[1] += [pick(b, cut, NT) for b in (1, 3)]
+    q_y = q_y or [q_0()]
+    q_y.append(quant(picks[1], T.yq, T.ys, cut, NT - cut, T.yb, cut))
+    m = [mm([q_y[h], q_v] + free[yb + h], yb + h, T.vq, T.vs, 0, T.yq, T.ys, lo, hi - lo) for h, (lo, hi) in enumerate(runs)]
+    c = [act([m[0]], T.yo[:, :cut], bank(yb, cut), F.Copy), cp([m[1]], T.yo[:, cut:], bank(yb + 1, NT - cut))]
+    dma("y", "sts", T.oc[:, :4 * cut], u8(T.yq[:, :cut]), [q_y[0]])
+    dma("s", "sty", T.y[:, :cut], T.yo[:, :cut], [c[0]])
+    dma("y", "sts", T.oc[:, 4 * cut:], u8(T.yq[:, cut:NT]), [q_y[1]])
+    for k in range(4):
+        dma(CFG["oq"][k], "sts", T.osc[4 * k:4 * k + 4, :], T.ys[32 * k:32 * k + 4, :], q_y)
+    dma(CFG["oq"][4], "sty", T.y[:, cut:], T.yo[:, cut:], [c[1]])
 
     wait("g", list(count.items()))

from concourse.bass import DstId, RemoteDMATransfer
from concourse.mybir import dt, AluOpType as A, ActivationFunctionType as F

NT, C, N = 320, 48, 8
H = NT // 2
NO = 128
NA, NB = 3 * C, 4 * C
XINB, XINA, XEND = N * C, N * C + NB, N * C + NB + NA
ZIN = (2 * NA, 2 * NA + 2 * C)
ZE = 2 * NA + NB
ZA, ZEND = ZE + NO, ZE + NO + NA
SP = 16 * C
MID = -3 * SP // 2
LOW = NT - MID
FAR = 2 * N * C
DX = FAR + NT
BIG = 2.0 ** 20
CFG = dict(gv=20, gb=18, own0="svsv", own="sssv", cut=192, mid=1, oq="sysys", unp=(2, 0, 1, 3),
           plan="qo gv x0 qb k5 x1 u hw u ht u hu u wo aA0 xA0svsv aA1 aB0 xA1vvsv hA0 aB1 xB0svsv hA1 xB1vsss cA0 cA1 "
                "hB0 hB1 cD0 xA2vsss cD1 qv cE0 zA xD2svsv zD cE1 xE2svsv zE ot og uA u1 ol")
X4, U8, BF, F16, F32, U16 = "float8_e4m3fn_x4", "uint8", "bfloat16", "float16", "float32", "uint16"


def _sb(n, d):
    return ("sbuf", [128, n], d)


SCRATCH = {
    "ps": ("psum", [128, 4096], F32),
    "xb": _sb(4 * NT, BF), "ub": _sb(512, BF), "vb": _sb(512, BF),
    "aq": _sb(1024, X4), "asc": _sb(1024, U8), "cq": _sb(1024, X4), "csc": _sb(1024, U8),
    "uq": _sb(128, X4), "us": _sb(128, U8), "uq2": _sb(128, X4), "us2": _sb(128, U8),
    "vq": _sb(128, X4), "vs": _sb(128, U8), "sq": _sb(NT, X4), "ss": _sb(NT, U8),
    "zz": _sb(H, BF), "k0": _sb(32, F32), "k1": _sb(32, F32), "k2": _sb(256, F32), "k3": _sb(256, F32),
    "col": _sb(8, F32), "c16": _sb(8, F32), "uoff": _sb(8, U16), "uniq0": _sb(20, F32), "j0": _sb(H, BF),
    "jv": _sb(NT, BF), "cx0": _sb(96, BF), "cx1": _sb(96, BF), "cx2": _sb(96, BF), "cx": _sb(96, BF), "t1": _sb(160, BF),
    "cr": _sb(80, F32), "dm": _sb(H, BF), "offw": _sb(2, U16), "offo": _sb(2, U16),
    "ff": _sb(516, BF), "fe": _sb(516, BF), "eq": _sb(512, X4), "es": _sb(512, U8), "tab": _sb(DX, F32),
    "pt": _sb(NT, F32), "rm": _sb(160, F32), "sm": _sb(160, F32), "gg": _sb(162, BF), "oht": _sb(NT, BF),
    "oh": _sb(NT, BF), "val": _sb(NT, F16), "valt": _sb(NT, F16), "csel": _sb(160, BF), "sel": _sb(512, F32),
    "xx": _sb(32, F32), "w2": _sb(32, U16), "win": _sb(4 * SP, BF), "ex": _sb(N * C, BF), "offs": _sb(96, U16),
    "h1": _sb(160, BF), "hs1": _sb(20, F32), "hc": _sb(20, F32), "ha": _sb(20, F32), "hz": _sb(40, F32), "kk": _sb(40, F32),
    "rr": _sb(128, F32), "x2": _sb(64, F32), "wo": _sb(32, U16), "olb": _sb(NT, F32),
    "xt": _sb(4 * 8 * C, BF), "xq": _sb(XEND, X4), "xs": _sb(XEND, U8), "wq": _sb(NO, X4), "wsl": _sb(NO, U8),
    "ht": _sb(8 * N * C, BF), "hq": _sb(2 * N * C, X4), "hs": _sb(2 * N * C, U8), "zb": _sb(4 * N * C, BF),
    "zq": _sb(ZEND, X4), "zs": _sb(ZEND, U8), "dd": _sb(2 * DX, BF), "dx": _sb(2 * DX, BF),
    "yb": _sb(4 * NT, BF), "yq": _sb(NT, X4), "ys": _sb(NT, U8), "yo": _sb(NT, F32),
}
SEMAPHORES = ["cv", "cs", "ct", "cg", "ldu", "ldxa", "ldxb", "lda", "ldc", "ldv", "fa", "fb", "ra", "rd", "rf",
              "sent", "sty", "sts"]


def _order(T, topo, r):
    mine = [k for k in range(N) if topo.die(T.cores[k]) == topo.die(T.cores[r])]
    other = [k for k in range(N) if k not in mine]
    h = mine.index(r) // 2 * 2
    own, far = mine[h:h + 2], other[h:h + 2]
    return (own + far if own[0] == r else far + own) + other[2 - h:4 - h] + mine[2 - h:4 - h]


def rank_program(g, core, T, topo):
    r = T.rank_of(core)
    if r is None:
        return
    Q = {"v": g.vector, "s": g.scalar, "t": g.tensor, "g": g, "y": g.sync}
    count = {}
    seen = {q: {} for q in Q}

    def wait(q, deps):
        need = {}
        for s, n in deps:
            need[s] = max(need.get(s, 0), n)
        for s, n in need.items():
            if seen[q].get(s, 0) < n:
                Q[q].wait_ge(T.sem[s], n)
                seen[q][s] = n

    def run(q, deps, fn):
        wait(q, deps)
        s = "c" + q
        count[s] = count.get(s, 0) + 1
        fn().then_inc(T.sem[s], 1)
        return (s, count[s])

    def dma(q, s, out, in_, deps=()):
        wait(q, deps)
        count[s] = count.get(s, 0) + 16
        Q[q].dma_start(out, in_).then_inc(T.sem[s], 16)
        return (s, count[s])

    V, S, P = g.vector, g.scalar, g.tensor
    u8 = lambda ap: ap.bitcast(dt.uint8)
    u32 = lambda ap: ap.bitcast(dt.uint32)
    bank = lambda b, n, o=0: T.ps[:, 512 * b + o:512 * b + o + n]

    def rev(buf, lo, hi, step=1):
        last = lo + (hi - 1 - lo) // step * step
        return buf[:, last::-step] if lo - step < 0 else buf[:, last:lo - step:-step]

    def ts(deps, out, in0, s1, op0, s2=None, op1=None):
        if op1 is None:
            return run("v", deps, lambda: V.tensor_scalar(out, in0, s1, None, op0))
        return run("v", deps, lambda: V.tensor_scalar(out, in0, s1, s2, op0, op1))

    def tt(deps, out, a, b, op):
        return run("v", deps, lambda: V.tensor_tensor(out, a, b, op))

    def cp(deps, out, a):
        return run("v", deps, lambda: V.tensor_copy(out, a))

    def tr(deps, out, a):
        return run("v", deps, lambda: V.transpose(out, a))

    def scan(deps, out, d0, d1, init, op0, op1):
        return run("v", deps, lambda: V.tensor_tensor_scan(out, d0, d1, init, op0, op1))

    def quant(deps, q, s, col, n, tile, at):
        return run("v", deps, lambda: V.quantize_mx(q[:, col:col + n], s[:, col:col + n], tile[:, 4 * at:4 * (at + n)]))

    def ms(ap, c, deps=()):
        return run("v", deps, lambda: V.memset(ap, c))

    def act(deps, out, a, func, **kw):
        return run("s", deps, lambda: S.activation(out, a, func, **kw))

    def mm(deps, b, wq, ws, w, q, s, col, n, start=True, stop=True):
        return run("t", deps, lambda: P.matmul_mx(bank(b, n), wq[:, w:w + 128], ws[:, w:w + 128],
                                                  q[:, col:col + n], s[:, col:col + n], start, stop))

    def iota(out, pattern, base, cm=0):
        return run("g", [], lambda: g.iota(out, pattern, base, cm, allow_small_or_imprecise_dtypes=True))

    def select(deps, out, in_, pattern, op, fill, base, cm):
        return run("g", deps, lambda: g.affine_select(out, in_, pattern, op, fill, base, cm))

    order = _order(T, topo, r)
    lead = order[0] == r
    ra, rb = [d for d in order[:4] if d != r], order[4:]
    a0, o0 = (C, 0) if lead else (0, NA)
    pairs = [d // 2 for d in order[::2]]

    ldu = dma("y", "ldu", T.ub[:], T.u[:])
    ldxa = dma("y", "ldxa", T.xb[:, :4 * H], T.x[:, :4 * H])
    ldxb = dma("y", "ldxb", T.xb[:, 4 * H:], T.x[:, 4 * H:])
    dma("y", "lda", u8(T.aq[:]), T.ac[:])
    lda = dma("y", "lda", T.asc[:], T.ap[:])
    dma("y", "ldc", u8(T.cq[:]), T.cc[:])
    ldc = dma("y", "ldc", T.csc[:], T.cp[:])

    i_k0 = iota(T.k0[:], [[0, 2], [1, 8], [0, 2]], 0)
    i_c16 = iota(T.c16[:], [[16, 8]], 0)
    i_k2 = [iota(T.k2[:, 0:32], [[0, 2], [2 * SP, 4], [-1, 4]], 2 * MID + 2),
            iota(T.k2[:, 32:64], [[8, 2], [16, 16]], 0),
            iota(T.k2[:, 64:96], [[16, 2], [0, 16]], 0),
            iota(T.k2[:, 96:128], [[0, 2], [-1, 4], [0, 4]], 0),
            iota(T.k2[:, 128:160], [[0, 8], [1, 4]], 256)]
    i_jv = iota(T.j0[:], [[32, 10], [1, 16]], -64)
    i_cx0 = iota(T.cx0[:], [[0, 24], [1, 4]], 0)
    i_t1 = iota(T.t1[:], [[0, 20], [SP, 4], [0, 2]], MID)
    i_k4 = iota(T.k2[:, 160:192], [[0, 32]], 4)
    i_k5 = [iota(T.k2[:, 192:224], [[1, 32]], 0),
            iota(T.k2[:, 224:240], [[4, 8], [64, 2]], 0),
            iota(T.k2[:, 240:256], [[4, 8], [-64, 2]], 66)]
    for s in (3, 2, 1):
        i_k4 = select([i_k4], T.k2[:, 160:192], T.k2[:, 160:192], [[0, 2], [1, 4], [0, 4]], A.is_ge, 4.0 / BIG ** (4 - s), -s, 0)
    i_uniq = iota(T.uniq0[:], [[32, 10], [0, 2]], FAR - C + 1)

    m_z = ms(T.zz[:], 0.0)
    m_cr = ms(T.cr[:], 1e27)
    c_k1 = tr([i_k0], T.k1[:], T.k0[:])
    m_g = ms(T.gg[:, 0:2], 0.0)
    c_uoff = ts([c_k1, i_c16], T.uoff[:], T.c16[:], T.k1[:, 0:1], A.add)
    m_sel = ms(T.sel[:, 160:256:8], 0.0)
    c_cr = ms(T.cr[:, 0::8], -1e27, [m_cr])
    m_oht = ms(T.oht[:, 1::2], 0.0)

    kept = lambda e: T.win[:, SP * e + NT - C + 1:SP * e + NT + C + 1]
    c_one = act([c_k1], T.col[:, 0:1], T.k1[:, 0:1], F.Relu, scale=-1.0, bias=1.0)
    m_win = [act([m_z], kept(0), T.zz[:, 0:2 * C], F.Copy)]
    c_neg = act([c_one], T.col[:, 1:2], T.col[:, 0:1], F.Identity, scale=-1.0)
    m_win.append(act([], kept(1), T.zz[:, 0:2 * C], F.Copy))
    c_dm = act([c_neg], T.dm[:], T.zz[:], F.Identity, bias=T.col[:, 1:2])

    q_u = quant([ldu], T.uq, T.us, 0, 128, T.ub, 0)
    p_uc = cp([q_u, c_uoff], u32(T.uq2[:]), u32(T.uq[:]).indirect(T.uoff[:]))
    p_us = act([q_u, c_uoff], T.us2[:], T.us[:].indirect(T.uoff[:]), F.Copy)
    q_xa = quant([ldxa], T.sq, T.ss, 0, H, T.xb, 0)
    s_a = mm([p_uc, p_us, q_xa], 0, T.uq2, T.us2, 0, T.sq, T.ss, 0, H)
    c_k3 = tr(i_k2, T.k3[:, 0:160], T.k2[:, 0:160])
    m_win += [act([], kept(e), T.zz[:, 0:2 * C], F.Copy) for e in (2, 3)]
    c_base = act([c_k3], T.col[:, 4:5], T.k3[:, 0:1], F.Identity, scale=0.5)
    c_h = act([], T.col[:, 2:3], T.k3[:, 64:65], F.Identity, scale=-1.0, bias=16.0)
    c_t = act([], T.col[:, 3:4], T.k3[:, 128:129], F.Identity, bias=0.25)
    c_x1 = act([i_cx0], T.cx1[:], T.cx0[:], F.Relu, bias=T.k3[:, 96:97])
    c_jv = [act([i_jv], T.jv[:, :H], T.j0[:], F.Identity, bias=T.k3[:, 64:65])]
    c_x2 = act([c_x1], T.cx2[:], T.cx1[:], F.Sign)
    c_jv.append(act([c_h], rev(T.jv, H, NT), T.j0[:], F.Identity, bias=T.col[:, 2:3]))

    W = H // 2
    half = lambda buf, k, o=0, step=1: buf[:, H * k + o:H * k + H:step]
    part = lambda buf, k, o=0, step=1: buf[:, W * k + o:W * k + W + o:step]
    f_t1 = lambda k, e: tr([e], half(T.pt, k), bank(k, H))
    f_rm = lambda k, e: scan([e, c_cr], part(T.rm, k), T.cr[:], half(T.pt, k, 0, 2), 0.0, A.min, A.max)
    f_sm = lambda k: scan([], rev(T.sm, W * k, W * k + W), T.cr[:], rev(T.pt, H * k, H * k + H, 2), 0.0, A.min, A.max)
    f_ng = lambda k, e: tt([e, m_g], part(T.gg, k, 1), part(T.rm, k), part(T.sm, k), A.is_lt)
    f_dn = lambda k, e: tt([e], half(T.oht, k, 0, 4), part(T.gg, k, 1, 2), part(T.gg, k, 0, 2), A.subtract)
    f_up = lambda k: tt([], half(T.oht, k, 2, 4), part(T.gg, k, 1, 2), part(T.gg, k, 2, 2), A.subtract)
    f_cs = lambda k, e: act([e], part(T.csel, k), part(T.gg, k, 1), F.Identity, scale=4096.0, bias=-2048.0)
    f_t2 = lambda k, e: tr([e, m_oht], half(T.oh, k), half(T.oht, k))
    f_t3 = lambda k, e: tr([e], half(T.valt, k), half(T.val, k))
    f_sel = lambda k, es: scan(es, rev(T.sel, W * k, W * k + W), rev(T.csel, W * k, W * k + W),
                               rev(T.valt, H * k, H * k + H, 2), 0.0, A.min, A.max)
    q_xb = quant([ldxb], T.sq, T.ss, H, H, T.xb, H)
    t1a = f_t1(0, s_a)
    s_b = mm([q_xb], 1, T.uq2, T.us2, 0, T.sq, T.ss, H, H)
    c_offo = cp([c_k3], T.offo[:], T.k3[:, 32:34])
    f_rm(0, t1a)
    sma = f_sm(0)
    t1b = f_t1(1, s_b)
    nga = f_ng(0, sma)
    f_rm(1, t1b)
    smb = f_sm(1)
    f_dn(0, nga)
    upa = f_up(0)
    ngb = f_ng(1, smb)
    csa = f_cs(0, nga)
    c_cx = act([c_x2], T.cx[:], T.cx2[:], F.Identity, scale=BIG)
    csb = f_cs(1, ngb)
    c_ff = act([ldxa, ldxb], T.ff[:], T.xb[:, 0:516], F.Identity, scale=0.0, bias=1.0)
    c_fe = select([c_ff], T.fe[:], T.ff[:], [[-1, 516]], A.is_equal, 0.0, 3, 4)
    x_pl = [act([], T.dx[:, DX * b + FAR:DX * (b + 1)], T.xb[:, b::4], F.Copy) for b in range(2)]
    m_rr = act([], T.rr[:, 40:64], T.zz[:, 0:24], F.Copy)
    m_kk = act([], T.kk[:, 1::2], T.zz[:, 0:20], F.Identity, bias=-1e6)
    t2a = f_t2(0, upa)
    f_dn(1, ngb)
    upb = f_up(1)
    n_a = scan([t2a, c_base, c_dm], half(T.val, 0), half(T.oh, 0), T.dm[:], T.col[:, 4:5], A.add, A.add)
    t2b = f_t2(1, upb)
    t3a = f_t3(0, n_a)
    n_b = scan([t2b], half(T.val, 1), half(T.oh, 1), T.dm[:], T.val[:, H - 1:H], A.add, A.add)
    f_sel(0, [t3a, csa])
    t3b = f_t3(1, n_b)
    h_1 = scan([i_t1, csb], rev(T.h1, 0, H), rev(T.csel, 0, H), rev(T.t1, 0, H), 0.0, A.min, A.max)
    e_sel = f_sel(1, [t3b])
    e_t4 = tr([e_sel, m_sel], T.xx[:], T.sel[:, 0:256:8])
    w_a = ts([c_offo], T.w2[:, 0:16], T.sel[:, 0:256].indirect(T.offo[:, 0:1]), float(LOW), A.add)
    e_t5 = tr([e_t4], T.sel[:, 256:512:8], rev(T.xx, 0, 32))
    cp([w_a] + m_win + c_jv, T.win[:].indirect(T.w2[:, 0:10]), T.jv[:, :H])
    w_b = ts([e_t5], rev(T.w2, 16, 32), T.sel[:, 256:512].indirect(T.offo[:, 0:1]), float(LOW), A.add)
    c_k4 = tr([i_k4], T.k3[:, 160:192], T.k2[:, 160:192])
    h_c = tt([h_1], T.hc[:], T.sel[:, 0:H:8], T.h1[:, 0::8], A.subtract)
    h_s = act([h_1], T.hs1[:], T.h1[:, 0::8], F.Identity, scale=2.0 * C / SP, bias=-2.0 * C * MID / SP)
    h_a = act([h_c], T.ha[:], T.hc[:], F.Abs, bias=-0.5)
    h_z = act([h_a], T.hz[:, 1::2], T.ha[:], F.Identity, scale=4096.0, bias=-4096.0 * C)
    e_sc = cp([w_b], T.win[:].indirect(T.w2[:, 22:32]), T.jv[:, H:])
    h_0 = tt([h_c, h_s], T.hz[:, 0::2], T.hc[:], T.hs1[:], A.add)

    f_ex = lambda n: scan([e_sc, c_cx], T.ex[:, 2 * C * n:2 * C * (n + 1)], T.cx[:], kept(pairs[n]), 0.0, A.mult, A.add)
    f_of = lambda k, evs: ts(evs + [c_t, c_k4], T.offs[:, 24 * k:24 * k + 48], T.ex[:, 2 * C * k + 3:2 * C * (k + 2):4],
                             T.k3[:, 160:161], A.mult, T.col[:, 3:4], A.add)

    def gather(q, lo, hi, dep):
        out, src = T.xt[:, 16 * lo:16 * hi], T.xb[:].indirect(T.offs[:, lo:hi])
        return cp([dep], out, src) if q == "v" else act([dep], out, src, F.Copy)

    ex = [f_ex(n) for n in range(3)]
    of_a = f_of(0, ex[:2])
    ex.append(f_ex(3))
    ga = a0 // 4
    keep = 0 if lead else NO - C
    gv = ga + CFG["gv"]
    evs = [gather("v", ga, gv, of_a), gather("s", gv, ga + 36, of_a)]
    of_b = f_of(2, ex[2:])
    q_a = quant(evs, T.xq, T.xs, a0, NA, T.xt, a0)
    go = gather("s", o0 // 4, o0 // 4 + 12, of_a)
    gb = [gather("s", 48 + CFG["gb"], 96, of_b)]

    def send(deps, sem, q, s, moves):
        wait("g", deps)
        eng = topo.engines(core, T.cores[moves[0][0]])
        far = [m for m in moves if topo.die(T.cores[m[0]]) != topo.die(core)]
        near = [m for m in moves if m not in far]
        for buf, flip in ((q, 0), (s, 1)):
            trs = []
            for some, lanes in ((far, eng[1 - flip::2]), (near, eng[flip::2])) if far and near else ((moves, eng),):
                w = len(lanes) // len(some)
                for k, (d, here, there) in enumerate(some):
                    rid, pid, _ = topo.addr(T.cores[d])
                    src, dst = buf[:, here:here + C], buf[:, there:there + C]
                    if not flip:
                        src, dst = u8(src), u8(dst)
                    trs.append(RemoteDMATransfer(dst_ids=[DstId(rid=rid, pnc=pid)], remote_sem=T.sem[sem], src=src, dst=dst,
                                                 dma_engine_mask=sum(1 << e for e in lanes[w * k:w * k + w])))
            g.remote_dma_fused(trs, local_sem=T.sem["sent"])
        count["sent"] = count.get("sent", 0) + 2 * len(eng)
        return (sem, 2 * len(eng))

    def spot(d):
        o = _order(T, topo, d)
        return o.index(r), int(o[0] == d)

    got_a = send([q_a], "fa", T.xq, T.xs, [(d, C * order.index(d), XINA + C * (spot(d)[0] - spot(d)[1])) for d in ra])

    free = {b: [] for b in range(8)}
    free[0], free[1] = [t1a], [t1b]

    def layer(wq, ws, i, base, q, s, col, n, deps, start=True, stop=True):
        return [mm(deps + free[base + b], base + b, wq, ws, 512 * i + 128 * b, q, s, col, n, start, stop) for b in range(4)]

    def leave(tile, at, m, base, prod, on, relu, o=0):
        evs = []
        for b in range(4):
            out = tile[:, 4 * at + b:4 * (at + m):4]
            if on[b] == "s":
                e = act([prod[b]], out, bank(base + b, m, o), F.Relu if relu else F.Copy, scale=0.0625)
            elif relu:
                e = ts([prod[b]], out, bank(base + b, m, o), 0.0, A.max, 0.0625, A.mult)
            else:
                e = ts([prod[b]], out, bank(base + b, m, o), 0.0625, A.mult)
            free[base + b] = [e]
            evs.append(e)
        return evs

    q_e = []

    def unpack(k0, k1, col, deps, base):
        m = 2 * C * (k1 - k0)
        o = max(0, NO - m)
        prod = {b: mm(deps + q_e + free[base + b], base + b, T.eq, T.es, 128 * b, T.zq, T.zs, col - o, m + o) for b in CFG["unp"]}
        done = {}
        for b in CFG["unp"]:
            for k in range(k0, k1):
                src, at, to = bank(base + b, 2 * C, 2 * C * (k - k0) + o), 2 * C * k, 2 * C * pairs[k]
                if b < 2:
                    e = tt([prod[b]], T.dx[:, DX * b + to:DX * b + to + 2 * C], src, T.xt[:, 4 * at + b:4 * (at + 2 * C):4], A.add)
                else:
                    e = act([prod[b]], T.dd[:, DX * (b - 2) + to:DX * (b - 2) + to + 2 * C], src, F.Copy)
            free[base + b] = [e]
            done[b] = e
        return done

    NW = NB + C
    hb = (2 * NA, 2 * NA + NW)
    cb, co = (0, NB) if lead else (C, 0)
    cd, ce, oe = (2 * C, 0, 0) if lead else (0, NW - NO, NO - 2 * C)
    zd = 0 if lead else NA
    home = lambda k: ZIN[k // 2] + C * (spot(rb[k])[0] % 2)
    prod, left, hq, back, base, turn = {}, {}, {}, {}, {}, 4
    for step in CFG["plan"].split():
        kind, p = step[0], step[1:2]
        i = int(step[2]) if len(step) > 2 else 0
        if step == "qo":
            q_o = quant([go, q_a], T.wq, T.wsl, 0, NO, T.xt, o0 - keep)
            po = [layer(T.aq, T.asc, k, 4 * k, T.wq, T.wsl, 0, NO, [q_o, lda]) for k in range(2)]
        elif step == "gv":
            gb.append(gather("v", 48, 48 + CFG["gb"], of_b))
        elif step == "qb":
            q_b = quant(gb, T.xq, T.xs, 4 * C, NB, T.xt, 4 * C)
            got_b = send([q_b], "fb", T.xq, T.xs,
                         [(d, C * order.index(d), XINB + C * ((spot(d)[0] + 2 * spot(d)[1]) % 4)) for d in rb])
            i_tab = [iota(T.tab[:, 0:N * C], [[1, N * C]], 0), iota(T.tab[:, FAR:DX], [[0, NT]], -1)]
            x_no = [iota(T.dd[:, DX * b + FAR:DX * (b + 1)], [[0, NT]], 0) for b in range(2)]
            ldv = dma("y", "ldv", T.vb[:], T.v[:], [got_b])
        elif step in ("x0", "x1"):
            k = int(p)
            left["o", k] = leave(T.ht, hb[k] + co, C, 4 * k, po[k], CFG["own" if k else "own0"], True, keep)
        elif step == "k5":
            c_k5 = tr(i_k5, T.k3[:, 192:256], T.k2[:, 192:256])
            c_uniq = act([i_uniq, c_k5], T.kk[:, 0::2], T.uniq0[:], F.Identity, bias=T.k3[:, 192:193])
        elif step == "hw":
            c_offw = ts([c_k5], T.offw[:], T.c16[:, 0:3:2], T.k3[:, 224:225], A.add)
            h_w = scan([h_0, h_z, m_kk, c_uniq], rev(T.rr, 0, 40), rev(T.kk, 0, 40), rev(T.hz, 0, 40), 0.0, A.min, A.max)
        elif step == "ht":
            h_t = [tr([h_w, m_rr], T.x2[:, o:o + 32], T.rr[:, 0:64:2]) for o in (0, 32)]
        elif step == "hu":
            h_u = tr(h_t, T.rr[:, 64:128:2], T.x2[:, 16:48])
        elif step == "wo":
            e_wo = ts([h_u, c_offw], T.wo[:], T.rr[:].indirect(T.offw[:]), C - 1.0, A.add)
        elif step == "u":
            b = len(q_e)
            q_e.append(run("v", [c_fe], lambda: V.quantize_mx(T.eq[:, 128 * b:128 * b + 128], T.es[:, 128 * b:128 * b + 128],
                                                              T.fe[:, 3 - b:515 - b])))
        elif step == "ot":
            c_tab = [act(i_tab[:1], T.tab[:, C * d:C * d + C], T.tab[:, C * d:C * d + C], F.Abs, bias=1.0 - C * (2 * d + 1))
                     for d in range(0, N, 2)]
        elif step == "og":
            o_g = act([e_wo] + c_tab + i_tab, T.olb[:], T.tab[:].indirect(T.wo[:, 0:20]), F.Copy)
        elif step == "ol":
            dma("y", "sts", T.ol[:], T.olb[0:128:16, :], [o_g, back["E"]])
        elif step == "qv":
            q_v = quant([ldv], T.vq, T.vs, 0, 128, T.vb, 0)
        elif step == "uA":
            d_a = unpack(0, 2, 2 * C if lead else 0, [back["A"], z_d], turn)
        elif step == "u1":
            d_1 = unpack(2, 3, ZIN[0], [back["D"]], 4 - turn)
        elif kind == "a":
            base[p, i] = turn
            turn = 4 - turn
            col, n, got = (XINA, NA, got_a) if p == "A" else (XINB, NB, got_b)
            prod[p, i] = layer(T.aq, T.asc, i, base[p, i], T.xq, T.xs, col, n, [got])
        elif kind == "x" and i < 2:
            at, n = (NA * i, NA) if p == "A" else (hb[i] + cb, NB)
            left[p, i] = leave(T.ht, at, n, base[p, i], prod[p, i], step[3:], True)
        elif kind == "x":
            at, n, o = {"A": (0, NA, 0), "D": (NA + cd, NA, 0), "E": (NA + ce + oe, 2 * C, oe)}[p]
            left[p, i] = leave(T.zb, at, n, base[p, i], prod[p, i], step[3:], False, o)
        elif kind == "h":
            at, n, more = (NA * i, NA, []) if p == "A" else (hb[i], NW, left["o", i])
            hq[p, i] = quant(left[p, i] + more, T.hq, T.hs, at, n, T.ht, at)
        elif kind == "c":
            if i == 0:
                base[p, 2] = turn
                turn = 4 - turn
            col, n = {"A": (NA * i, NA), "D": (hb[i] + cd, NA), "E": (hb[i] + ce, NO)}[p]
            prod[p, 2] = layer(T.cq, T.csc, i, base[p, 2], T.hq, T.hs, col, n, [hq["A" if p == "A" else "B", i], ldc], i == 0, i == 1)
        elif p == "A":
            back[p] = send([quant(left[p, 2], T.zq, T.zs, ZA, NA, T.zb, 0)], "ra", T.zq, T.zs,
                           [(s, ZA + C * k, C * (spot(s)[0] + 2 * spot(s)[1])) for k, s in enumerate(ra)])
        elif p == "D":
            z_d = quant(left[p, 2], T.zq, T.zs, zd, NA, T.zb, NA + cd)
            back[p] = send([z_d], "rd", T.zq, T.zs, [(rb[k], zd + cb + C * k, home(k)) for k in (0, 1)])
        else:
            z = quant(left[p, 2] + left["D", 2], T.zq, T.zs, ZE, NO, T.zb, NA + ce)
            back[p] = send([z], "rf", T.zq, T.zs, [(rb[k], ZE + oe + C * (k - 2), home(k)) for k in (2, 3)])

    d_2 = unpack(3, 4, ZIN[1], [back["D"], back["E"]], turn)
    yb = 4 - turn

    def pick(b, lo, hi):
        out, at = T.yb[:, 4 * lo + b:4 * hi:4], T.wo[:, lo // 16:hi // 16]
        deps = [d_a[b], d_1[b], d_2[b], e_wo]
        if b < 2:
            return act(deps + x_pl, out, T.dx[:, DX * b:DX * (b + 1)].indirect(at), F.Copy)
        return tt(deps + x_no, out, T.dd[:, DX * (b - 2):DX * (b - 1)].indirect(at), T.xb[:, 4 * lo + b:4 * hi:4], A.add)

    cut = CFG["cut"]
    runs = ((0, cut), (cut, NT))
    picks = [[pick(b, 0, cut) for b in range(4)]]
    q_0 = lambda: quant(picks[0], T.yq, T.ys, 0, cut, T.yb, 0)
    picks.append([pick(b, cut, NT) for b in (0, 2)])
    q_y = [q_0()] if CFG["mid"] else []
    picks[1] += [pick(b, cut, NT) for b in (1, 3)]
    q_y = q_y or [q_0()]
    q_y.append(quant(picks[1], T.yq, T.ys, cut, NT - cut, T.yb, cut))
    m = [mm([q_y[h], q_v] + free[yb + h], yb + h, T.vq, T.vs, 0, T.yq, T.ys, lo, hi - lo) for h, (lo, hi) in enumerate(runs)]
    c = [act([m[0]], T.yo[:, :cut], bank(yb, cut), F.Copy), cp([m[1]], T.yo[:, cut:], bank(yb + 1, NT - cut))]
    dma("y", "sts", T.oc[:, :4 * cut], u8(T.yq[:, :cut]), [q_y[0]])
    dma("s", "sty", T.y[:, :cut], T.yo[:, :cut], [c[0]])
    dma("y", "sts", T.oc[:, 4 * cut:], u8(T.yq[:, cut:NT]), [q_y[1]])
    for k in range(4):
        dma(CFG["oq"][k], "sts", T.osc[4 * k:4 * k + 4, :], T.ys[32 * k:32 * k + 4, :], q_y)
    dma(CFG["oq"][4], "sty", T.y[:, cut:], T.yo[:, cut:], [c[1]])

    wait("g", list(count.items()))
